import numpy as np
import ml_dtypes


def mxq(x, axis, fmt="e4m3"):
    dtype, down = {"e4m3": (ml_dtypes.float8_e4m3fn, 7), "e5m2": (ml_dtypes.float8_e5m2, 14)}[fmt]
    v = np.moveaxis(np.asarray(x, np.float32).astype(ml_dtypes.bfloat16).astype(np.float64), axis, -1)
    blocks = v.reshape(v.shape[:-1] + (-1, 32))
    amax = np.abs(blocks).max(-1, keepdims=True)
    byte = np.maximum(np.where(amax > 0, np.frexp(amax)[1] - 1 + 127, 0) - down, 1)
    scale = np.exp2(byte - 127.0)
    codes = (blocks / scale).astype(np.float32).astype(dtype).astype(np.float64)
    return np.moveaxis((codes * scale).reshape(v.shape), -1, axis)


WIDE = False


def mx_kscale(k):
    if not WIDE:
        return np.ones(k)
    levels = np.array([30, -30])
    if k % 512:
        return np.exp2(np.random.permutation(np.resize(levels, k // 32))).repeat(32)
    a = np.empty((k // 512, 16))
    for p in range(k // 512):
        a[p, :8] = np.random.permutation(np.resize(levels, 8))
        for g in range(8):
            far = levels[np.abs(levels - a[p, g]) >= 10]
            a[p, g + 8] = far[np.random.randint(len(far))]
    return np.exp2(a.ravel()).repeat(32)


def f64(x):
    return np.asarray(x).astype(np.float64)


def striped(idx):
    return np.tile(idx.reshape(-1, 16).T, (8, 1)).astype(np.uint16)


def unstriped(offs):
    return offs[:16].T.reshape(-1).astype(np.int64)


E2M1 = np.array([0.0, 0.5, 1.0, 1.5, 2.0, 3.0, 4.0, 6.0, -0.0, -0.5, -1.0, -1.5, -2.0, -3.0, -4.0, -6.0])


def pack_weight(w, fmt):
    k, n = w.shape
    w = f64(np.asarray(w, np.float32).astype(ml_dtypes.bfloat16)).reshape(k // 32, 32, n)
    amax = np.abs(w).max(1)
    if fmt == "e4m3":
        byte = np.frexp(amax)[1] - 1 + 127 - 7
    else:
        mant, ex = np.frexp(amax / 6.0)
        byte = np.where(mant > 0.5, ex, ex - 1) + 127
    byte = np.clip(np.where(amax > 0, byte, 1), 1, 254)
    scaled = (w * np.exp2(127.0 - byte)[:, None, :]).reshape(k, n).astype(np.float32)
    by_word = np.ascontiguousarray(scaled.reshape(k // 512, 128, 4, n).transpose(0, 1, 3, 2))
    if fmt == "e4m3":
        words = by_word.astype(ml_dtypes.float8_e4m3fn).view(np.uint8)
    else:
        c = by_word.astype(ml_dtypes.float4_e2m1fn).view(np.uint8) & 0xF
        words = (c[..., 0::2] | (c[..., 1::2] << 4)).reshape(k // 512, 128, 2 * n)
    return np.ascontiguousarray(words), np.ascontiguousarray(byte.astype(np.uint8).reshape(k // 512, 16, n))


def unpack_weight(words, scales, fmt):
    g, _, n = scales.shape
    words = np.ascontiguousarray(words).reshape(g, 128, n, -1)
    if fmt == "e4m3":
        vals = words.view(ml_dtypes.float8_e4m3fn).astype(np.float64)
    else:
        nib = np.empty((g, 128, n, 4), np.uint8)
        nib[..., 0::2] = words & 0xF
        nib[..., 1::2] = words >> 4
        vals = E2M1[nib]
    vals = vals * np.repeat(np.exp2(scales.astype(np.float64) - 127.0), 8, axis=1)[..., None]
    return vals.transpose(0, 1, 3, 2).reshape(g * 512, n)


def planes(y):
    n, m = y.shape
    v = y.astype(np.float32).astype(ml_dtypes.bfloat16).astype(np.float64).reshape(n // 32, 32, m)
    top = np.abs(v).max(1)
    byte = np.clip(np.where(top > 0, np.frexp(top)[1] - 1 + 127 - 7, 1), 1, 254)
    codes = (v * np.exp2(127.0 - byte)[:, None, :]).reshape(n, m).astype(np.float32).astype(ml_dtypes.float8_e4m3fn).view(np.uint8)
    words = codes.reshape(n // 512, 128, 4, m).transpose(0, 1, 3, 2)
    return np.ascontiguousarray(words), np.ascontiguousarray(byte.astype(np.uint8).reshape(n // 512, 16, m))


K, N, T, J = 1024, 512, 2048, 1024


def setup_inputs():
    n = np.random.standard_normal
    s = mx_kscale(K)[:, None]
    m = np.exp(0.5 * n((1, J)))
    w = n((K, N)) / np.sqrt(K) / s
    p_w8 = pack_weight(w[:512], "e4m3")
    p_w4 = pack_weight(w[512:], "e2m1")
    return {
        "dy": (m * n((K, J)) * s).astype(np.float32),
        "w8_words": p_w8[0],
        "w8_scales": p_w8[1],
        "w4_words": p_w4[0],
        "w4_scales": p_w4[1],
        "res": (n((N, J))).astype(np.float32),
        "wgo": np.tile(np.random.uniform(0.5, 2.0, J), (128, 1)).astype(np.float32),
        "offs": striped(np.random.permutation(T)[:J]),
    }


def reference(dy, w8_words, w8_scales, w4_words, w4_scales, res, wgo, offs):
    idx = unstriped(offs)
    dy_ = mxq(f64(dy), 0, "e5m2")
    w8_ = unpack_weight(w8_words, w8_scales, "e4m3")
    w4_ = unpack_weight(w4_words, w4_scales, "e2m1")
    dx = w8_.T @ dy_[:512] + w4_.T @ dy_[512:]
    out = np.zeros((N, T))
    out[:, idx] = f64(wgo)[0] * (dx + f64(res))
    return (out,) + planes(out)

@@ -1,0 +1,286 @@
+from contextlib import ExitStack
+
+import concourse.mybir as mybir
+from concourse.masks import make_identity
+
+K, N, T, J = 1024, 512, 2048, 1024
+FLOPS = 2 * K * N * J
+
+F32 = mybir.dt.float32
+BF16 = mybir.dt.bfloat16
+I32 = mybir.dt.int32
+U32 = mybir.dt.uint32
+U16 = mybir.dt.uint16
+U8 = mybir.dt.uint8
+E4M3 = mybir.dt.float8_e4m3fn_x4
+E5M2 = mybir.dt.float8_e5m2_x4
+E2M1 = mybir.dt.float4_e2m1fn_x4
+ADD = mybir.AluOpType.add
+MULT = mybir.AluOpType.mult
+
+P = 128
+HALF = 512
+PIECE = 256
+VEC_COLS = 160
+
+
+def tile_list_embg_mix_resP_kernel(
+    tc, dy, w8_words, w8_scales, w4_words, w4_scales, res, wgo, offs, out_0, out_1, out_2
+):
+    nc = tc.nc
+    with ExitStack() as ctx:
+        keep = ctx.enter_context(tc.tile_pool(name="keep", bufs=1))
+        ring = ctx.enter_context(tc.tile_pool(name="ring", bufs=2))
+        wins = ctx.enter_context(tc.tile_pool(name="wins", bufs=1))
+        psum = ctx.enter_context(tc.psum_pool(name="psum", bufs=1))
+        banks = [psum.tile([P, HALF], F32, name=f"bank{i}") for i in range(8)]
+
+        offsets = keep.tile([P, J // 16], U16, name="offsets")
+        w8 = keep.tile([P, N], U32, name="w8", align_bytes=64)
+        w4 = keep.tile([P, 2 * N], U8, name="w4", align_bytes=64)
+        wsc = keep.tile([P, 2 * N], U8, name="wsc", align_bytes=64)
+        gain = keep.tile([P, J], F32, name="gain", align_bytes=64)
+        ident = keep.tile([P, P], F32, name="ident", align_bytes=64)
+        out_scales = keep.tile([P, HALF], U8, name="out_scales", align_bytes=64)
+        windows = [wins.tile([P, T], F32, name=f"win{w}", align_bytes=64) for w in range(3)]
+
+        raw = {}
+        resid = {}
+
+        def load_dy(c, a, h):
+            raw[c, a, h] = keep.tile([P, 4, PIECE], F32, name=f"raw{c}{a}{h}", align_bytes=64)
+            j0 = c * HALF + h * PIECE
+            nc.sync.dma_start(
+                out=raw[c, a, h][:],
+                in_=dy[512 * a : 512 * (a + 1), j0 : j0 + PIECE].rearrange("(p i) j -> p i j", i=4),
+            )
+
+        def load_res(b, c):
+            resid[b, c] = keep.tile([P, HALF], F32, name=f"res{b}{c}", align_bytes=64)
+            nc.sync.dma_start(out=resid[b, c][:], in_=res[P * b : P * (b + 1), c * HALF : (c + 1) * HALF])
+
+        def load_gain(c):
+            nc.sync.dma_start(out=gain[:, c * HALF : (c + 1) * HALF], in_=wgo[:, c * HALF : (c + 1) * HALF])
+
+        nc.gpsimd.memset(wsc[:].bitcast(U32), 0)
+        def load_scales(s):
+            a, q = divmod(s, 4)
+            nc.sync.dma_start(
+                out=wsc[32 * q : 32 * q + 4, a * N : (a + 1) * N].bitcast(I32),
+                in_=(w8_scales, w4_scales)[a][0][4 * q : 4 * q + 4, :].bitcast(I32),
+            )
+
+        warm = keep.tile([P, 8], F32, name="warm")
+        warm2 = keep.tile([P, 8], BF16, name="warm2")
+        nc.vector.memset(warm[:], 0.0)
+        nc.scalar.copy(out=warm2[:], in_=warm[:])
+        load_dy(0, 0, 0)
+        load_dy(0, 0, 1)
+        load_dy(0, 1, 0)
+        for s in range(5):
+            load_scales(s)
+        load_dy(0, 1, 1)
+        nc.sync.dma_start(out=w8[:].bitcast(I32), in_=w8_words[0].rearrange("p n i -> p (n i)").bitcast(I32))
+        nc.sync.dma_start(out=w4[:].bitcast(I32), in_=w4_words[0].bitcast(I32))
+        for s in range(5, 8):
+            load_scales(s)
+        load_res(0, 0)
+        load_gain(0)
+        nc.sync.dma_start(offsets[:], offs)
+        load_res(1, 0)
+        for a in range(2):
+            for h in range(2):
+                load_dy(1, a, h)
+            if a == 0:
+                load_res(2, 0)
+        load_res(0, 1)
+        load_gain(1)
+        load_res(1, 1)
+        load_res(2, 1)
+        load_res(3, 0)
+        load_res(3, 1)
+
+        for w in range(3):
+            nc.vector.memset(windows[w][:].bitcast(U32), 0)
+        make_identity(nc, ident[:])
+
+        codes = {}
+        scales = {}
+        grouped = {}
+
+        def cast(engine_copy, c, a, h, lo, hi):
+            dst = grouped[c, a, h][:, lo:hi, :].rearrange("p (g e) i -> p g i e", e=4)
+            src = raw[c, a, h][:, :, lo:hi].rearrange("p i (g e) -> p g i e", e=4)
+            engine_copy(out=dst, in_=src)
+
+        def round_dy(c, a, h, vec_cols):
+            grouped[c, a, h] = keep.tile([P, PIECE, 4], BF16, name=f"grp{c}{a}{h}", align_bytes=64)
+            if vec_cols < PIECE:
+                cast(nc.scalar.copy, c, a, h, vec_cols, PIECE)
+            if vec_cols > 0:
+                cast(nc.vector.tensor_copy, c, a, h, 0, vec_cols)
+
+        def quant_dy(c, a, h):
+            if h == 0:
+                codes[c, a] = keep.tile([P, HALF], U32, name=f"dyc{c}{a}", align_bytes=64)
+                scales[c, a] = keep.tile([P, HALF], U8, name=f"dys{c}{a}", align_bytes=64)
+            cols = slice(h * PIECE, (h + 1) * PIECE)
+            nc.vector.quantize_mx(
+                out=codes[c, a][:, cols].bitcast(E5M2),
+                scales=scales[c, a][:, cols],
+                in_=grouped[c, a, h][:].rearrange("p j i -> p (j i)"),
+            )
+
+        def product(b, c, acc):
+            nc.tensor.matmul_mx(
+                out=acc[:],
+                lhsT=w8[:, P * b : P * (b + 1)].bitcast(E4M3),
+                lhsT_scale=wsc[:, P * b : P * (b + 1)],
+                rhs=codes[c, 0][:].bitcast(E5M2),
+                rhs_scale=scales[c, 0][:],
+                start=True,
+                stop=False,
+            )
+            nc.tensor.matmul_mx(
+                out=acc[:],
+                lhsT=w4[:, 2 * P * b : 2 * P * (b + 1)].bitcast(E2M1),
+                lhsT_scale=wsc[:, N + P * b : N + P * (b + 1)],
+                rhs=codes[c, 1][:].bitcast(E5M2),
+                rhs_scale=scales[c, 1][:],
+                start=False,
+                stop=True,
+            )
+            return acc
+
+        order = [(0, 0), (1, 0), (2, 0), (0, 1), (1, 1), (2, 1), (3, 0), (3, 1)]
+        sums = [keep.tile([P, HALF], F32, name=f"sum{i}", align_bytes=64) for i in range(2)]
+        pair_tiles = [keep.tile([P, HALF], F32, name=f"pairs{i}", align_bytes=64) for i in range(4)]
+
+        def sum_tile(k):
+            if k == 2:
+                return grouped[1, 1, 1][:].rearrange("p j i -> p (j i)").bitcast(F32)
+            return (pair_tiles[3] if k == 7 else sums[k % 2])[:]
+
+        def add_res(k):
+            b, c = order[k]
+            acc = product(b, c, banks[k % 3])
+            nc.vector.tensor_tensor(sum_tile(k), acc[:], resid[b, c][:], ADD)
+
+        def scatter(k):
+            b, c = order[k]
+            cols = slice(c * HALF, (c + 1) * HALF)
+            where = offsets[:, c * (HALF // 16) : (c + 1) * (HALF // 16)]
+            nc.vector.tensor_tensor(windows[b % 3][:].indirect(where), sum_tile(k), gain[:, cols], MULT)
+
+        words_out = out_1[0].rearrange("p t i -> p (t i)").bitcast(I32)
+        scales_out = out_2[0].bitcast(I32)
+
+        def store_rows(b):
+            nc.sync.dma_start(out=out_0[P * b : P * (b + 1), :], in_=windows[b % 3][:])
+
+        def turn(b, c, bank, copy, stage):
+            turned = bank[:].rearrange("t (q n) -> t q n", q=4)
+            for tq in range(4):
+                t0 = HALF * tq + P * c
+                nc.tensor.transpose(turned[:, tq, :], windows[b % 3][:, t0 : t0 + P], ident[:])
+            pairs = stage[:, 0 : 2 * P].bitcast(BF16).rearrange("t (u m e) -> t u m e", u=2, e=2)
+            copy(out=pairs, in_=turned.rearrange("t q (p u e) -> t u (q p) e", u=2, e=2))
+
+        def turn_back(stage, back):
+            for u in range(2):
+                nc.tensor.transpose(back[:, P * u : P * (u + 1)], stage[:, P * u : P * (u + 1)], ident[:])
+
+        def planes(b):
+            rounded = ring.tile([P, 4, P, 2], F32, name="rounded", align_bytes=64)
+            for h in range(2):
+                back = banks[(7, 3)[h]]
+                for g in range(2):
+                    c = 2 * h + g
+                    turn(b, c, banks[3 + c], nc.scalar.copy, pair_tiles[c])
+                    turn_back(pair_tiles[c], back[:, 2 * P * g : 2 * P * (g + 1)])
+                nc.scalar.copy(
+                    out=rounded[:, 2 * h : 2 * h + 2, :, :],
+                    in_=back[:].rearrange("m (g u t) -> m g t u", g=2, u=2),
+                )
+            return rounded
+
+        def planes_last(b):
+            rounded = ring.tile([P, 4, P, 2], F32, name="rounded", align_bytes=64)
+            copies = (nc.vector.tensor_copy, nc.scalar.copy)
+            stages = [keep.tile([P, 2 * P], F32, name=f"last{c}", align_bytes=64) for c in range(4)]
+            for c in range(4):
+                turn(b, c, banks[(3, 4, 5, 6)[c]], copies[c % 2], stages[c])
+            for c in range(4):
+                back = banks[(7, 0, 1, 2)[c]]
+                turn_back(stages[c], back[:, 0 : 2 * P])
+                copies[c % 2](out=rounded[:, c, :, :], in_=back[:, 0 : 2 * P].rearrange("m (u t) -> m t u", u=2))
+            return rounded
+
+        def quant_out(b, rounded, parts):
+            y_codes = ring.tile([P, HALF], U32, name="y_codes", align_bytes=64)
+            flat = rounded[:].rearrange("m c t u -> m (c t u)").bitcast(BF16)
+            w = HALF // parts
+            for s in range(parts):
+                nc.vector.quantize_mx(
+                    out=y_codes[:, s * w : (s + 1) * w].bitcast(E4M3),
+                    scales=out_scales[4 * b : P, s * w : (s + 1) * w],
+                    in_=flat[:, 4 * s * w : 4 * (s + 1) * w],
+                )
+            for tq in range(4):
+                nc.sync.dma_start(
+                    out=words_out[32 * b : 32 * (b + 1), HALF * tq : HALF * (tq + 1)],
+                    in_=y_codes[32 * tq : 32 * (tq + 1), :].bitcast(I32),
+                )
+
+        round_dy(0, 0, 0, 0)
+        round_dy(0, 0, 1, 0)
+        quant_dy(0, 0, 0)
+        round_dy(0, 1, 0, VEC_COLS)
+        quant_dy(0, 0, 1)
+        round_dy(0, 1, 1, VEC_COLS)
+        quant_dy(0, 1, 0)
+        quant_dy(0, 1, 1)
+        add_res(0)
+        add_res(1)
+        for a in range(2):
+            for h in range(2):
+                round_dy(1, a, h, 0)
+        probe0 = keep.tile([P, 8], I32, name="probe0")
+        nc.gpsimd.tensor_copy(out=probe0[:, 0:1], in_=wsc[:, N : N + 4].bitcast(I32))
+        scatter(0)
+        quant_dy(1, 0, 0)
+        quant_dy(1, 0, 1)
+        scatter(1)
+        quant_dy(1, 1, 0)
+        quant_dy(1, 1, 1)
+        add_res(2)
+        scatter(2)
+        add_res(3)
+        add_res(4)
+        scatter(3)
+        store_rows(0)
+        made0 = planes(0)
+        add_res(5)
+        scatter(4)
+        store_rows(1)
+        made1 = planes(1)
+        add_res(6)
+        scatter(5)
+        store_rows(2)
+        quant_out(0, made0, 1)
+        made2 = planes(2)
+        scatter(6)
+        add_res(7)
+        quant_out(1, made1, 1)
+        scatter(7)
+        store_rows(3)
+        probe = keep.tile([P, 8], F32, name="probe")
+        nc.gpsimd.tensor_copy(out=probe[:, 0:1], in_=windows[0][:, 0:1])
+        quant_out(2, made2, 1)
+        made3 = planes_last(3)
+        quant_out(3, made3, 2)
+        for tq in range(4):
+            nc.scalar.dma_start(
+                out=scales_out[:, P * tq : P * (tq + 1)],
+                in_=out_scales[32 * tq : 32 * tq + 16, :].bitcast(I32),
+            )

@@ -30,7 +30,7 @@ def tile_list_embg_mix_resP_kernel(
     nc = tc.nc
     with ExitStack() as ctx:
         keep = ctx.enter_context(tc.tile_pool(name="keep", bufs=1))
-        ring = ctx.enter_context(tc.tile_pool(name="ring", bufs=2))
+        ring = ctx.enter_context(tc.tile_pool(name="ring", bufs=4))
         wins = ctx.enter_context(tc.tile_pool(name="wins", bufs=1))
         psum = ctx.enter_context(tc.psum_pool(name="psum", bufs=1))
         banks = [psum.tile([P, HALF], F32, name=f"bank{i}") for i in range(8)]
@@ -39,10 +39,10 @@ def tile_list_embg_mix_resP_kernel(
         w8 = keep.tile([P, N], U32, name="w8", align_bytes=64)
         w4 = keep.tile([P, 2 * N], U8, name="w4", align_bytes=64)
         wsc = keep.tile([P, 2 * N], U8, name="wsc", align_bytes=64)
-        gain = keep.tile([P, J], F32, name="gain", align_bytes=64)
+        gain = [keep.tile([P, HALF], F32, name=f"gain{c}", align_bytes=64) for c in range(2)]
         ident = keep.tile([P, P], F32, name="ident", align_bytes=64)
         out_scales = keep.tile([P, HALF], U8, name="out_scales", align_bytes=64)
-        windows = [wins.tile([P, T], F32, name=f"win{w}", align_bytes=64) for w in range(3)]
+        windows = [wins.tile([P, T], F32, name=f"win{w}", align_bytes=64, offset=4 * T * w) for w in range(4)]
 
         raw = {}
         resid = {}
@@ -60,7 +60,7 @@ def tile_list_embg_mix_resP_kernel(
             nc.sync.dma_start(out=resid[b, c][:], in_=res[P * b : P * (b + 1), c * HALF : (c + 1) * HALF])
 
         def load_gain(c):
-            nc.sync.dma_start(out=gain[:, c * HALF : (c + 1) * HALF], in_=wgo[:, c * HALF : (c + 1) * HALF])
+            nc.sync.dma_start(out=gain[c][:], in_=wgo[:, c * HALF : (c + 1) * HALF])
 
         nc.gpsimd.memset(wsc[:].bitcast(U32), 0)
         def load_scales(s):
@@ -76,14 +76,14 @@ def tile_list_embg_mix_resP_kernel(
         nc.scalar.copy(out=warm2[:], in_=warm[:])
         load_dy(0, 0, 0)
         load_dy(0, 0, 1)
+        for s in range(4):
+            load_scales(s)
         load_dy(0, 1, 0)
-        for s in range(5):
-            load_scales(s)
-        load_dy(0, 1, 1)
         nc.sync.dma_start(out=w8[:].bitcast(I32), in_=w8_words[0].rearrange("p n i -> p (n i)").bitcast(I32))
-        nc.sync.dma_start(out=w4[:].bitcast(I32), in_=w4_words[0].bitcast(I32))
-        for s in range(5, 8):
+        load_dy(0, 1, 1)
+        for s in range(4, 8):
             load_scales(s)
+        nc.sync.dma_start(out=w4[:].bitcast(I32), in_=w4_words[0].bitcast(I32))
         load_res(0, 0)
         load_gain(0)
         nc.sync.dma_start(offsets[:], offs)
@@ -100,8 +100,7 @@ def tile_list_embg_mix_resP_kernel(
         load_res(3, 0)
         load_res(3, 1)
 
-        for w in range(3):
-            nc.vector.memset(windows[w][:].bitcast(U32), 0)
+        nc.vector.memset(windows[0][:].bitcast(U32), 0)
         make_identity(nc, ident[:])
 
         codes = {}
@@ -114,7 +113,12 @@ def tile_list_embg_mix_resP_kernel(
             engine_copy(out=dst, in_=src)
 
         def round_dy(c, a, h, vec_cols):
-            grouped[c, a, h] = keep.tile([P, PIECE, 4], BF16, name=f"grp{c}{a}{h}", align_bytes=64)
+            if (c, a, h) == (0, 1, 1):
+                grouped[c, a, h] = wins.tile([P, PIECE, 4], BF16, name="grp011", align_bytes=64, offset=8 * T - 1024)
+            elif (c, a, h) == (1, 1, 0):
+                grouped[c, a, h] = wins.tile([P, PIECE, 4], BF16, name="grp110", align_bytes=64, offset=12 * T)
+            else:
+                grouped[c, a, h] = keep.tile([P, PIECE, 4], BF16, name=f"grp{c}{a}{h}", align_bytes=64)
             if vec_cols < PIECE:
                 cast(nc.scalar.copy, c, a, h, vec_cols, PIECE)
             if vec_cols > 0:
@@ -153,36 +157,40 @@ def tile_list_embg_mix_resP_kernel(
             return acc
 
         order = [(0, 0), (1, 0), (2, 0), (0, 1), (1, 1), (2, 1), (3, 0), (3, 1)]
-        sums = [keep.tile([P, HALF], F32, name=f"sum{i}", align_bytes=64) for i in range(2)]
+        sums = [keep.tile([P, HALF], F32, name=f"sum{i}", align_bytes=64) for i in range(3)]
         pair_tiles = [keep.tile([P, HALF], F32, name=f"pairs{i}", align_bytes=64) for i in range(4)]
 
-        def sum_tile(k):
+        def sum_tile(k, lo, hi):
             if k == 2:
-                return grouped[1, 1, 1][:].rearrange("p j i -> p (j i)").bitcast(F32)
-            return (pair_tiles[3] if k == 7 else sums[k % 2])[:]
+                return grouped[1, 1, 1][:].rearrange("p j i -> p (j i)").bitcast(F32)[:, lo:hi]
+            if k == 7 and lo > 0:
+                return pair_tiles[3][:, 0 : hi - lo]
+            return sums[k % 3][:, lo:hi]
 
-        def add_res(k):
-            b, c = order[k]
-            acc = product(b, c, banks[k % 3])
-            nc.vector.tensor_tensor(sum_tile(k), acc[:], resid[b, c][:], ADD)
+        accs = {}
 
-        def scatter(k):
+        def add_res(k, lo=0, hi=HALF):
             b, c = order[k]
-            cols = slice(c * HALF, (c + 1) * HALF)
-            where = offsets[:, c * (HALF // 16) : (c + 1) * (HALF // 16)]
-            nc.vector.tensor_tensor(windows[b % 3][:].indirect(where), sum_tile(k), gain[:, cols], MULT)
+            if k not in accs:
+                accs[k] = product(b, c, banks[k % 2])
+            nc.vector.tensor_tensor(sum_tile(k, lo, hi), accs[k][:, lo:hi], resid[b, c][:, lo:hi], ADD)
+
+        def scatter(k, lo=0, hi=HALF):
+            b, c = order[k]
+            where = offsets[:, (c * HALF + lo) // 16 : (c * HALF + hi) // 16]
+            nc.vector.tensor_tensor(windows[b][:].indirect(where), sum_tile(k, lo, hi), gain[c][:, lo:hi], MULT)
 
         words_out = out_1[0].rearrange("p t i -> p (t i)").bitcast(I32)
         scales_out = out_2[0].bitcast(I32)
 
         def store_rows(b):
-            nc.sync.dma_start(out=out_0[P * b : P * (b + 1), :], in_=windows[b % 3][:])
+            nc.sync.dma_start(out=out_0[P * b : P * (b + 1), :], in_=windows[b][:])
 
         def turn(b, c, bank, copy, stage):
             turned = bank[:].rearrange("t (q n) -> t q n", q=4)
             for tq in range(4):
                 t0 = HALF * tq + P * c
-                nc.tensor.transpose(turned[:, tq, :], windows[b % 3][:, t0 : t0 + P], ident[:])
+                nc.tensor.transpose(turned[:, tq, :], windows[b][:, t0 : t0 + P], ident[:])
             pairs = stage[:, 0 : 2 * P].bitcast(BF16).rearrange("t (u m e) -> t u m e", u=2, e=2)
             copy(out=pairs, in_=turned.rearrange("t q (p u e) -> t u (q p) e", u=2, e=2))
 
@@ -193,10 +201,10 @@ def tile_list_embg_mix_resP_kernel(
         def planes(b):
             rounded = ring.tile([P, 4, P, 2], F32, name="rounded", align_bytes=64)
             for h in range(2):
-                back = banks[(7, 3)[h]]
+                back = banks[6 + h]
                 for g in range(2):
                     c = 2 * h + g
-                    turn(b, c, banks[3 + c], nc.scalar.copy, pair_tiles[c])
+                    turn(b, c, banks[2 + c], nc.scalar.copy, pair_tiles[c])
                     turn_back(pair_tiles[c], back[:, 2 * P * g : 2 * P * (g + 1)])
                 nc.scalar.copy(
                     out=rounded[:, 2 * h : 2 * h + 2, :, :],
@@ -209,9 +217,9 @@ def tile_list_embg_mix_resP_kernel(
             copies = (nc.vector.tensor_copy, nc.scalar.copy)
             stages = [keep.tile([P, 2 * P], F32, name=f"last{c}", align_bytes=64) for c in range(4)]
             for c in range(4):
-                turn(b, c, banks[(3, 4, 5, 6)[c]], copies[c % 2], stages[c])
+                turn(b, c, banks[2 + c], copies[c % 2], stages[c])
             for c in range(4):
-                back = banks[(7, 0, 1, 2)[c]]
+                back = banks[(0, 1, 6, 7)[c]]
                 turn_back(stages[c], back[:, 0 : 2 * P])
                 copies[c % 2](out=rounded[:, c, :, :], in_=back[:, 0 : 2 * P].rearrange("m (u t) -> m t u", u=2))
             return rounded
@@ -232,50 +240,52 @@ def tile_list_embg_mix_resP_kernel(
                     in_=y_codes[32 * tq : 32 * (tq + 1), :].bitcast(I32),
                 )
 
-        round_dy(0, 0, 0, 0)
-        round_dy(0, 0, 1, 0)
+        round_dy(0, 0, 0, VEC_COLS)
+        round_dy(0, 0, 1, VEC_COLS)
         quant_dy(0, 0, 0)
         round_dy(0, 1, 0, VEC_COLS)
         quant_dy(0, 0, 1)
         round_dy(0, 1, 1, VEC_COLS)
         quant_dy(0, 1, 0)
         quant_dy(0, 1, 1)
+        nc.gpsimd.memset(windows[1][:].bitcast(U32), 0)
+        nc.gpsimd.memset(windows[2][:].bitcast(U32), 0)
         add_res(0)
         add_res(1)
         for a in range(2):
             for h in range(2):
                 round_dy(1, a, h, 0)
-        probe0 = keep.tile([P, 8], I32, name="probe0")
-        nc.gpsimd.tensor_copy(out=probe0[:, 0:1], in_=wsc[:, N : N + 4].bitcast(I32))
         scatter(0)
         quant_dy(1, 0, 0)
         quant_dy(1, 0, 1)
         scatter(1)
         quant_dy(1, 1, 0)
         quant_dy(1, 1, 1)
+        nc.gpsimd.memset(windows[3][:].bitcast(U32), 0)
         add_res(2)
-        scatter(2)
+        scatter(2, 0, PIECE)
         add_res(3)
         add_res(4)
         scatter(3)
         store_rows(0)
         made0 = planes(0)
-        add_res(5)
         scatter(4)
         store_rows(1)
         made1 = planes(1)
+        add_res(5)
+        scatter(2, PIECE, HALF)
         add_res(6)
         scatter(5)
         store_rows(2)
         quant_out(0, made0, 1)
         made2 = planes(2)
+        add_res(7, 0, PIECE)
         scatter(6)
-        add_res(7)
         quant_out(1, made1, 1)
-        scatter(7)
+        scatter(7, 0, PIECE)
+        add_res(7, PIECE, HALF)
+        scatter(7, PIECE, HALF)
         store_rows(3)
-        probe = keep.tile([P, 8], F32, name="probe")
-        nc.gpsimd.tensor_copy(out=probe[:, 0:1], in_=windows[0][:, 0:1])
         quant_out(2, made2, 1)
         made3 = planes_last(3)
         quant_out(3, made3, 2)

@@ -47,12 +47,11 @@ def tile_list_embg_mix_resP_kernel(
         raw = {}
         resid = {}
 
-        def load_dy(c, a, h):
-            raw[c, a, h] = keep.tile([P, 4, PIECE], F32, name=f"raw{c}{a}{h}", align_bytes=64)
-            j0 = c * HALF + h * PIECE
+        def load_dy(c, a, lo, hi):
+            raw[c, a, lo] = keep.tile([P, 4, hi - lo], F32, name=f"raw{c}{a}{lo}", align_bytes=64)
             nc.sync.dma_start(
-                out=raw[c, a, h][:],
-                in_=dy[512 * a : 512 * (a + 1), j0 : j0 + PIECE].rearrange("(p i) j -> p i j", i=4),
+                out=raw[c, a, lo][:],
+                in_=dy[512 * a : 512 * (a + 1), c * HALF + lo : c * HALF + hi].rearrange("(p i) j -> p i j", i=4),
             )
 
         def load_res(b, c):
@@ -74,25 +73,22 @@ def tile_list_embg_mix_resP_kernel(
         warm2 = keep.tile([P, 8], BF16, name="warm2")
         nc.vector.memset(warm[:], 0.0)
         nc.scalar.copy(out=warm2[:], in_=warm[:])
-        load_dy(0, 0, 0)
-        load_dy(0, 0, 1)
+        load_dy(0, 0, 0, HALF)
         for s in range(4):
             load_scales(s)
-        load_dy(0, 1, 0)
+        load_dy(0, 1, 0, PIECE)
         nc.sync.dma_start(out=w8[:].bitcast(I32), in_=w8_words[0].rearrange("p n i -> p (n i)").bitcast(I32))
-        load_dy(0, 1, 1)
+        load_dy(0, 1, PIECE, HALF)
         for s in range(4, 8):
             load_scales(s)
         nc.sync.dma_start(out=w4[:].bitcast(I32), in_=w4_words[0].bitcast(I32))
         load_res(0, 0)
         load_gain(0)
         nc.sync.dma_start(offsets[:], offs)
+        load_dy(1, 0, 0, HALF)
         load_res(1, 0)
-        for a in range(2):
-            for h in range(2):
-                load_dy(1, a, h)
-            if a == 0:
-                load_res(2, 0)
+        load_dy(1, 1, 0, HALF)
+        load_res(2, 0)
         load_res(0, 1)
         load_gain(1)
         load_res(1, 1)
@@ -106,33 +102,29 @@ def tile_list_embg_mix_resP_kernel(
         codes = {}
         scales = {}
         grouped = {}
+        place = {(0, 1, PIECE): 8 * T - 1024, (1, 0, 0): 16 * T - 2048, (1, 1, 0): 16 * T + 2048}
 
-        def cast(engine_copy, c, a, h, lo, hi):
-            dst = grouped[c, a, h][:, lo:hi, :].rearrange("p (g e) i -> p g i e", e=4)
-            src = raw[c, a, h][:, :, lo:hi].rearrange("p i (g e) -> p g i e", e=4)
-            engine_copy(out=dst, in_=src)
-
-        def round_dy(c, a, h, vec_cols):
-            if (c, a, h) == (0, 1, 1):
-                grouped[c, a, h] = wins.tile([P, PIECE, 4], BF16, name="grp011", align_bytes=64, offset=8 * T - 1024)
-            elif (c, a, h) == (1, 1, 0):
-                grouped[c, a, h] = wins.tile([P, PIECE, 4], BF16, name="grp110", align_bytes=64, offset=12 * T)
+        def round_dy(c, a, lo, hi, vec_cols):
+            key = (c, a, lo)
+            if key in place:
+                grouped[key] = wins.tile([P, hi - lo, 4], BF16, name=f"grp{c}{a}{lo}", align_bytes=64, offset=place[key])
             else:
-                grouped[c, a, h] = keep.tile([P, PIECE, 4], BF16, name=f"grp{c}{a}{h}", align_bytes=64)
-            if vec_cols < PIECE:
-                cast(nc.scalar.copy, c, a, h, vec_cols, PIECE)
-            if vec_cols > 0:
-                cast(nc.vector.tensor_copy, c, a, h, 0, vec_cols)
+                grouped[key] = keep.tile([P, hi - lo, 4], BF16, name=f"grp{c}{a}{lo}", align_bytes=64)
+            for copy, x, y in ((nc.scalar.copy, vec_cols, hi - lo), (nc.vector.tensor_copy, 0, vec_cols)):
+                if y > x:
+                    copy(
+                        out=grouped[key][:, x:y, :].rearrange("p (g e) i -> p g i e", e=4),
+                        in_=raw[key][:, :, x:y].rearrange("p i (g e) -> p g i e", e=4),
+                    )
 
-        def quant_dy(c, a, h):
-            if h == 0:
+        def quant_dy(c, a, lo, hi):
+            if lo == 0:
                 codes[c, a] = keep.tile([P, HALF], U32, name=f"dyc{c}{a}", align_bytes=64)
                 scales[c, a] = keep.tile([P, HALF], U8, name=f"dys{c}{a}", align_bytes=64)
-            cols = slice(h * PIECE, (h + 1) * PIECE)
             nc.vector.quantize_mx(
-                out=codes[c, a][:, cols].bitcast(E5M2),
-                scales=scales[c, a][:, cols],
-                in_=grouped[c, a, h][:].rearrange("p j i -> p (j i)"),
+                out=codes[c, a][:, lo:hi].bitcast(E5M2),
+                scales=scales[c, a][:, lo:hi],
+                in_=grouped[c, a, lo][:].rearrange("p j i -> p (j i)"),
             )
 
         def product(b, c, acc):
@@ -157,28 +149,45 @@ def tile_list_embg_mix_resP_kernel(
             return acc
 
         order = [(0, 0), (1, 0), (2, 0), (0, 1), (1, 1), (2, 1), (3, 0), (3, 1)]
-        sums = [keep.tile([P, HALF], F32, name=f"sum{i}", align_bytes=64) for i in range(3)]
-        pair_tiles = [keep.tile([P, HALF], F32, name=f"pairs{i}", align_bytes=64) for i in range(4)]
-
-        def sum_tile(k, lo, hi):
-            if k == 2:
-                return grouped[1, 1, 1][:].rearrange("p j i -> p (j i)").bitcast(F32)[:, lo:hi]
-            if k == 7 and lo > 0:
-                return pair_tiles[3][:, 0 : hi - lo]
-            return sums[k % 3][:, lo:hi]
-
+        pair_tiles = [keep.tile([P, 2 * P], F32, name=f"pairs{i}", align_bytes=64) for i in range(4)]
+        sums = {}
         accs = {}
 
-        def add_res(k, lo=0, hi=HALF):
+        def make_sum(k):
+            if k in (1, 2):
+                sums[k] = wins.tile([P, HALF], F32, name=f"sum{k}", align_bytes=64, offset=16 * T + 2048 * (k - 1))
+            else:
+                sums[k] = keep.tile([P, HALF], F32, name=f"sum{k}", align_bytes=64)
+
+        def add_res(k):
             b, c = order[k]
-            if k not in accs:
-                accs[k] = product(b, c, banks[k % 2])
-            nc.vector.tensor_tensor(sum_tile(k, lo, hi), accs[k][:, lo:hi], resid[b, c][:, lo:hi], ADD)
+            make_sum(k)
+            acc = accs[k] if k in accs else product(b, c, banks[k % 4])
+            nc.vector.tensor_tensor(sums[k][:], acc[:], resid[b, c][:], ADD)
 
         def scatter(k, lo=0, hi=HALF):
             b, c = order[k]
             where = offsets[:, (c * HALF + lo) // 16 : (c * HALF + hi) // 16]
-            nc.vector.tensor_tensor(windows[b][:].indirect(where), sum_tile(k, lo, hi), gain[c][:, lo:hi], MULT)
+            nc.vector.tensor_tensor(windows[b][:].indirect(where), sums[k][:, lo:hi], gain[c][:, lo:hi], MULT)
+
+        dx = {}
+
+        def leave_bank(k):
+            b, c = order[k]
+            acc = product(b, c, banks[(k - 4) % 3])
+            dx[k] = keep.tile([P, HALF], F32, name=f"dx{k}", align_bytes=64)
+            nc.scalar.copy(out=dx[k][:], in_=acc[:])
+            make_sum(k)
+
+        def finish(k, lo, hi, dst):
+            b, c = order[k]
+            nc.gpsimd.tensor_tensor(sums[k][:, lo:hi], dx[k][:, lo:hi], resid[b, c][:, lo:hi], ADD)
+            nc.gpsimd.tensor_tensor(dst, sums[k][:, lo:hi], gain[c][:, lo:hi], MULT)
+
+        def put(k, lo, hi, src):
+            b, c = order[k]
+            where = offsets[:, (c * HALF + lo) // 16 : (c * HALF + hi) // 16]
+            nc.vector.tensor_copy(windows[b][:].indirect(where), src)
 
         words_out = out_1[0].rearrange("p t i -> p (t i)").bitcast(I32)
         scales_out = out_2[0].bitcast(I32)
@@ -198,96 +207,78 @@ def tile_list_embg_mix_resP_kernel(
             for u in range(2):
                 nc.tensor.transpose(back[:, P * u : P * (u + 1)], stage[:, P * u : P * (u + 1)], ident[:])
 
-        def planes(b):
+        def planes(b, copies):
             rounded = ring.tile([P, 4, P, 2], F32, name="rounded", align_bytes=64)
-            for h in range(2):
-                back = banks[6 + h]
-                for g in range(2):
-                    c = 2 * h + g
-                    turn(b, c, banks[2 + c], nc.scalar.copy, pair_tiles[c])
-                    turn_back(pair_tiles[c], back[:, 2 * P * g : 2 * P * (g + 1)])
-                nc.scalar.copy(
-                    out=rounded[:, 2 * h : 2 * h + 2, :, :],
-                    in_=back[:].rearrange("m (g u t) -> m g t u", g=2, u=2),
-                )
+            there, back = (banks[4:], banks[:4]) if b % 2 == 0 else (banks[:4], banks[4:])
+            for c in range(4):
+                turn(b, c, there[c], copies[c % 2], pair_tiles[c])
+            for c in range(4):
+                turn_back(pair_tiles[c], back[c][:, 0 : 2 * P])
+            for c in range(4):
+                copies[c % 2](out=rounded[:, c, :, :], in_=back[c][:, 0 : 2 * P].rearrange("m (u t) -> m t u", u=2))
             return rounded
 
-        def planes_last(b):
-            rounded = ring.tile([P, 4, P, 2], F32, name="rounded", align_bytes=64)
-            copies = (nc.vector.tensor_copy, nc.scalar.copy)
-            stages = [keep.tile([P, 2 * P], F32, name=f"last{c}", align_bytes=64) for c in range(4)]
-            for c in range(4):
-                turn(b, c, banks[2 + c], copies[c % 2], stages[c])
-            for c in range(4):
-                back = banks[(0, 1, 6, 7)[c]]
-                turn_back(stages[c], back[:, 0 : 2 * P])
-                copies[c % 2](out=rounded[:, c, :, :], in_=back[:, 0 : 2 * P].rearrange("m (u t) -> m t u", u=2))
-            return rounded
+        y_codes = [keep.tile([P, 2 * HALF], U32, name=f"y_codes{i}", align_bytes=64) for i in range(2)]
 
         def quant_out(b, rounded, parts):
-            y_codes = ring.tile([P, HALF], U32, name="y_codes", align_bytes=64)
             flat = rounded[:].rearrange("m c t u -> m (c t u)").bitcast(BF16)
             w = HALF // parts
+            base = HALF * (b % 2)
             for s in range(parts):
                 nc.vector.quantize_mx(
-                    out=y_codes[:, s * w : (s + 1) * w].bitcast(E4M3),
+                    out=y_codes[b // 2][:, base + s * w : base + (s + 1) * w].bitcast(E4M3),
                     scales=out_scales[4 * b : P, s * w : (s + 1) * w],
                     in_=flat[:, 4 * s * w : 4 * (s + 1) * w],
                 )
-            for tq in range(4):
-                nc.sync.dma_start(
-                    out=words_out[32 * b : 32 * (b + 1), HALF * tq : HALF * (tq + 1)],
-                    in_=y_codes[32 * tq : 32 * (tq + 1), :].bitcast(I32),
-                )
+            if b % 2 == 1:
+                rows = words_out[32 * (b - 1) : 32 * (b + 1), :].rearrange("(d p) t -> p d t", d=2)
+                for tq in range(4):
+                    nc.sync.dma_start(
+                        out=rows[:, :, HALF * tq : HALF * (tq + 1)],
+                        in_=y_codes[b // 2][32 * tq : 32 * (tq + 1), :].bitcast(I32).rearrange("p (d t) -> p d t", d=2),
+                    )
 
-        round_dy(0, 0, 0, VEC_COLS)
-        round_dy(0, 0, 1, VEC_COLS)
-        quant_dy(0, 0, 0)
-        round_dy(0, 1, 0, VEC_COLS)
-        quant_dy(0, 0, 1)
-        round_dy(0, 1, 1, VEC_COLS)
-        quant_dy(0, 1, 0)
-        quant_dy(0, 1, 1)
+        round_dy(0, 0, 0, HALF, 2 * VEC_COLS)
+        quant_dy(0, 0, 0, HALF)
+        round_dy(0, 1, 0, PIECE, VEC_COLS)
+        round_dy(0, 1, PIECE, HALF, VEC_COLS)
+        quant_dy(0, 1, 0, PIECE)
+        quant_dy(0, 1, PIECE, HALF)
         nc.gpsimd.memset(windows[1][:].bitcast(U32), 0)
         nc.gpsimd.memset(windows[2][:].bitcast(U32), 0)
         add_res(0)
-        add_res(1)
-        for a in range(2):
-            for h in range(2):
-                round_dy(1, a, h, 0)
+        round_dy(1, 0, 0, HALF, 0)
+        round_dy(1, 1, 0, HALF, 0)
         scatter(0)
-        quant_dy(1, 0, 0)
-        quant_dy(1, 0, 1)
-        scatter(1)
-        quant_dy(1, 1, 0)
-        quant_dy(1, 1, 1)
+        quant_dy(1, 0, 0, HALF)
         nc.gpsimd.memset(windows[3][:].bitcast(U32), 0)
+        add_res(1)
+        scatter(1)
+        quant_dy(1, 1, 0, HALF)
         add_res(2)
-        scatter(2, 0, PIECE)
+        accs[3] = product(0, 1, banks[3])
+        for k in range(4, 8):
+            leave_bank(k)
+        for k in range(4, 8):
+            finish(k, 0, HALF, dx[k][:])
+        scatter(2)
         add_res(3)
-        add_res(4)
         scatter(3)
         store_rows(0)
-        made0 = planes(0)
-        scatter(4)
+        made0 = planes(0, (nc.scalar.copy, nc.scalar.copy))
+        put(4, 0, HALF, dx[4][:])
         store_rows(1)
-        made1 = planes(1)
-        add_res(5)
-        scatter(2, PIECE, HALF)
-        add_res(6)
-        scatter(5)
+        made1 = planes(1, (nc.scalar.copy, nc.scalar.copy))
+        put(5, 0, HALF, dx[5][:])
         store_rows(2)
+        made2 = planes(2, (nc.scalar.copy, nc.scalar.copy))
         quant_out(0, made0, 1)
-        made2 = planes(2)
-        add_res(7, 0, PIECE)
-        scatter(6)
+        put(6, 0, HALF, dx[6][:])
         quant_out(1, made1, 1)
-        scatter(7, 0, PIECE)
-        add_res(7, PIECE, HALF)
-        scatter(7, PIECE, HALF)
+        put(7, 0, HALF, dx[7][:])
         store_rows(3)
         quant_out(2, made2, 1)
-        made3 = planes_last(3)
+        made3 = planes(3, (nc.vector.tensor_copy, nc.scalar.copy))
         quant_out(3, made3, 2)
         for tq in range(4):
             nc.scalar.dma_start(

@@ -21,7 +21,11 @@ MULT = mybir.AluOpType.mult
 P = 128
 HALF = 512
 PIECE = 256
-VEC_COLS = 160
+QUAD = 32
+WINDOWS = 3
+VECTOR_FIRST = 192
+VECTOR_PIECE = 160
+TILES = [(0, 0), (1, 0), (2, 0), (0, 1), (1, 1), (2, 1), (3, 0), (3, 1)]
 
 
 def tile_list_embg_mix_resP_kernel(
@@ -30,19 +34,16 @@ def tile_list_embg_mix_resP_kernel(
     nc = tc.nc
     with ExitStack() as ctx:
         keep = ctx.enter_context(tc.tile_pool(name="keep", bufs=1))
-        ring = ctx.enter_context(tc.tile_pool(name="ring", bufs=4))
-        wins = ctx.enter_context(tc.tile_pool(name="wins", bufs=1))
         psum = ctx.enter_context(tc.psum_pool(name="psum", bufs=1))
         banks = [psum.tile([P, HALF], F32, name=f"bank{i}") for i in range(8)]
 
         offsets = keep.tile([P, J // 16], U16, name="offsets")
         w8 = keep.tile([P, N], U32, name="w8", align_bytes=64)
         w4 = keep.tile([P, 2 * N], U8, name="w4", align_bytes=64)
-        wsc = keep.tile([P, 2 * N], U8, name="wsc", align_bytes=64)
+        w_scales = keep.tile([P, 2 * N], U8, name="w_scales", align_bytes=64)
         gain = [keep.tile([P, HALF], F32, name=f"gain{c}", align_bytes=64) for c in range(2)]
         ident = keep.tile([P, P], F32, name="ident", align_bytes=64)
-        out_scales = keep.tile([P, HALF], U8, name="out_scales", align_bytes=64)
-        windows = [wins.tile([P, T], F32, name=f"win{w}", align_bytes=64, offset=4 * T * w) for w in range(4)]
+        windows = [keep.tile([P, T], F32, name=f"window{w}", align_bytes=64) for w in range(WINDOWS)]
 
         raw = {}
         resid = {}
@@ -61,32 +62,31 @@ def tile_list_embg_mix_resP_kernel(
         def load_gain(c):
             nc.sync.dma_start(out=gain[c][:], in_=wgo[:, c * HALF : (c + 1) * HALF])
 
-        nc.gpsimd.memset(wsc[:].bitcast(U32), 0)
-        def load_scales(s):
-            a, q = divmod(s, 4)
-            nc.sync.dma_start(
-                out=wsc[32 * q : 32 * q + 4, a * N : (a + 1) * N].bitcast(I32),
-                in_=(w8_scales, w4_scales)[a][0][4 * q : 4 * q + 4, :].bitcast(I32),
-            )
+        def load_scales(a, source):
+            for q in range(4):
+                nc.sync.dma_start(
+                    out=w_scales[QUAD * q : QUAD * q + 4, a * N : (a + 1) * N].bitcast(I32),
+                    in_=source[0][4 * q : 4 * q + 4, :].bitcast(I32),
+                )
 
-        warm = keep.tile([P, 8], F32, name="warm")
-        warm2 = keep.tile([P, 8], BF16, name="warm2")
-        nc.vector.memset(warm[:], 0.0)
-        nc.scalar.copy(out=warm2[:], in_=warm[:])
+        nc.gpsimd.memset(w_scales[:].bitcast(U32), 0)
+        warm_in = keep.tile([P, 8], F32, name="warm_in")
+        warm_out = keep.tile([P, 8], BF16, name="warm_out")
+        nc.vector.memset(warm_in[:], 0.0)
+        nc.scalar.copy(out=warm_out[:], in_=warm_in[:])
+
         load_dy(0, 0, 0, HALF)
-        for s in range(4):
-            load_scales(s)
+        load_scales(0, w8_scales)
         load_dy(0, 1, 0, PIECE)
         nc.sync.dma_start(out=w8[:].bitcast(I32), in_=w8_words[0].rearrange("p n i -> p (n i)").bitcast(I32))
         load_dy(0, 1, PIECE, HALF)
-        for s in range(4, 8):
-            load_scales(s)
+        load_scales(1, w4_scales)
         nc.sync.dma_start(out=w4[:].bitcast(I32), in_=w4_words[0].bitcast(I32))
         load_res(0, 0)
         load_gain(0)
         nc.sync.dma_start(offsets[:], offs)
-        load_dy(1, 0, 0, HALF)
         load_res(1, 0)
+        load_dy(1, 0, 0, HALF)
         load_dy(1, 1, 0, HALF)
         load_res(2, 0)
         load_res(0, 1)
@@ -96,192 +96,148 @@ def tile_list_embg_mix_resP_kernel(
         load_res(3, 0)
         load_res(3, 1)
 
-        nc.vector.memset(windows[0][:].bitcast(U32), 0)
+        for window in windows:
+            nc.vector.memset(window[:].bitcast(U32), 0)
         make_identity(nc, ident[:])
 
-        codes = {}
-        scales = {}
         grouped = {}
-        place = {(0, 1, PIECE): 8 * T - 1024, (1, 0, 0): 16 * T - 2048, (1, 1, 0): 16 * T + 2048}
+        dy_codes = {}
+        dy_scales = {}
 
-        def round_dy(c, a, lo, hi, vec_cols):
+        def round_dy(c, a, lo, hi, vector_cols):
             key = (c, a, lo)
-            if key in place:
-                grouped[key] = wins.tile([P, hi - lo, 4], BF16, name=f"grp{c}{a}{lo}", align_bytes=64, offset=place[key])
-            else:
-                grouped[key] = keep.tile([P, hi - lo, 4], BF16, name=f"grp{c}{a}{lo}", align_bytes=64)
-            for copy, x, y in ((nc.scalar.copy, vec_cols, hi - lo), (nc.vector.tensor_copy, 0, vec_cols)):
+            grouped[key] = keep.tile([P, hi - lo, 4], BF16, name=f"grouped{c}{a}{lo}", align_bytes=64)
+            for copy, x, y in ((nc.scalar.copy, vector_cols, hi - lo), (nc.vector.tensor_copy, 0, vector_cols)):
                 if y > x:
                     copy(
                         out=grouped[key][:, x:y, :].rearrange("p (g e) i -> p g i e", e=4),
                         in_=raw[key][:, :, x:y].rearrange("p i (g e) -> p g i e", e=4),
                     )
 
-        def quant_dy(c, a, lo, hi):
+        def quantise_dy(c, a, lo, hi):
             if lo == 0:
-                codes[c, a] = keep.tile([P, HALF], U32, name=f"dyc{c}{a}", align_bytes=64)
-                scales[c, a] = keep.tile([P, HALF], U8, name=f"dys{c}{a}", align_bytes=64)
+                dy_codes[c, a] = keep.tile([P, HALF], U32, name=f"dy_codes{c}{a}", align_bytes=64)
+                dy_scales[c, a] = keep.tile([P, HALF], U8, name=f"dy_scales{c}{a}", align_bytes=64)
             nc.vector.quantize_mx(
-                out=codes[c, a][:, lo:hi].bitcast(E5M2),
-                scales=scales[c, a][:, lo:hi],
+                out=dy_codes[c, a][:, lo:hi].bitcast(E5M2),
+                scales=dy_scales[c, a][:, lo:hi],
                 in_=grouped[c, a, lo][:].rearrange("p j i -> p (j i)"),
             )
 
-        def product(b, c, acc):
+        sums = {}
+
+        def product_plus_res(k, total):
+            b, c = TILES[k]
+            acc = banks[k % 4]
             nc.tensor.matmul_mx(
                 out=acc[:],
                 lhsT=w8[:, P * b : P * (b + 1)].bitcast(E4M3),
-                lhsT_scale=wsc[:, P * b : P * (b + 1)],
-                rhs=codes[c, 0][:].bitcast(E5M2),
-                rhs_scale=scales[c, 0][:],
+                lhsT_scale=w_scales[:, P * b : P * (b + 1)],
+                rhs=dy_codes[c, 0][:].bitcast(E5M2),
+                rhs_scale=dy_scales[c, 0][:],
                 start=True,
                 stop=False,
             )
             nc.tensor.matmul_mx(
                 out=acc[:],
                 lhsT=w4[:, 2 * P * b : 2 * P * (b + 1)].bitcast(E2M1),
-                lhsT_scale=wsc[:, N + P * b : N + P * (b + 1)],
-                rhs=codes[c, 1][:].bitcast(E5M2),
-                rhs_scale=scales[c, 1][:],
+                lhsT_scale=w_scales[:, N + P * b : N + P * (b + 1)],
+                rhs=dy_codes[c, 1][:].bitcast(E5M2),
+                rhs_scale=dy_scales[c, 1][:],
                 start=False,
                 stop=True,
             )
-            return acc
+            nc.vector.tensor_tensor(total, acc[:], resid[b, c][:], ADD)
+            sums[k] = total
 
-        order = [(0, 0), (1, 0), (2, 0), (0, 1), (1, 1), (2, 1), (3, 0), (3, 1)]
-        pair_tiles = [keep.tile([P, 2 * P], F32, name=f"pairs{i}", align_bytes=64) for i in range(4)]
-        sums = {}
-        accs = {}
+        def new_sum(k):
+            total = keep.tile([P, HALF], F32, name=f"sum{k}", align_bytes=64)
+            return total[:]
 
-        def make_sum(k):
-            if k in (1, 2):
-                sums[k] = wins.tile([P, HALF], F32, name=f"sum{k}", align_bytes=64, offset=16 * T + 2048 * (k - 1))
-            else:
-                sums[k] = keep.tile([P, HALF], F32, name=f"sum{k}", align_bytes=64)
-
-        def add_res(k):
-            b, c = order[k]
-            make_sum(k)
-            acc = accs[k] if k in accs else product(b, c, banks[k % 4])
-            nc.vector.tensor_tensor(sums[k][:], acc[:], resid[b, c][:], ADD)
-
-        def scatter(k, lo=0, hi=HALF):
-            b, c = order[k]
-            where = offsets[:, (c * HALF + lo) // 16 : (c * HALF + hi) // 16]
-            nc.vector.tensor_tensor(windows[b][:].indirect(where), sums[k][:, lo:hi], gain[c][:, lo:hi], MULT)
-
-        dx = {}
-
-        def leave_bank(k):
-            b, c = order[k]
-            acc = product(b, c, banks[(k - 4) % 3])
-            dx[k] = keep.tile([P, HALF], F32, name=f"dx{k}", align_bytes=64)
-            nc.scalar.copy(out=dx[k][:], in_=acc[:])
-            make_sum(k)
-
-        def finish(k, lo, hi, dst):
-            b, c = order[k]
-            nc.gpsimd.tensor_tensor(sums[k][:, lo:hi], dx[k][:, lo:hi], resid[b, c][:, lo:hi], ADD)
-            nc.gpsimd.tensor_tensor(dst, sums[k][:, lo:hi], gain[c][:, lo:hi], MULT)
-
-        def put(k, lo, hi, src):
-            b, c = order[k]
-            where = offsets[:, (c * HALF + lo) // 16 : (c * HALF + hi) // 16]
-            nc.vector.tensor_copy(windows[b][:].indirect(where), src)
+        def scatter(k):
+            b, c = TILES[k]
+            where = offsets[:, c * HALF // 16 : (c + 1) * HALF // 16]
+            nc.vector.tensor_tensor(windows[b % WINDOWS][:].indirect(where), sums[k], gain[c][:], MULT)
 
         words_out = out_1[0].rearrange("p t i -> p (t i)").bitcast(I32)
         scales_out = out_2[0].bitcast(I32)
+        pair_tiles = [keep.tile([P, 2 * P], F32, name=f"pairs{g}", align_bytes=64) for g in range(4)]
+        y_codes = [keep.tile([P, 2 * HALF], U32, name=f"y_codes{d}", align_bytes=64) for d in range(2)]
+        y_scales = keep.tile([P, HALF], U8, name="y_scales", align_bytes=64)
 
-        def store_rows(b):
-            nc.sync.dma_start(out=out_0[P * b : P * (b + 1), :], in_=windows[b][:])
-
-        def turn(b, c, bank, copy, stage):
-            turned = bank[:].rearrange("t (q n) -> t q n", q=4)
-            for tq in range(4):
-                t0 = HALF * tq + P * c
-                nc.tensor.transpose(turned[:, tq, :], windows[b][:, t0 : t0 + P], ident[:])
-            pairs = stage[:, 0 : 2 * P].bitcast(BF16).rearrange("t (u m e) -> t u m e", u=2, e=2)
-            copy(out=pairs, in_=turned.rearrange("t q (p u e) -> t u (q p) e", u=2, e=2))
-
-        def turn_back(stage, back):
-            for u in range(2):
-                nc.tensor.transpose(back[:, P * u : P * (u + 1)], stage[:, P * u : P * (u + 1)], ident[:])
-
-        def planes(b, copies):
-            rounded = ring.tile([P, 4, P, 2], F32, name="rounded", align_bytes=64)
+        def store_and_regroup(b, copies):
+            window = windows[b % WINDOWS]
+            nc.sync.dma_start(out=out_0[P * b : P * (b + 1), :], in_=window[:])
+            rounded = keep.tile([P, 4, P, 2], F32, name=f"rounded{b}", align_bytes=64)
             there, back = (banks[4:], banks[:4]) if b % 2 == 0 else (banks[:4], banks[4:])
-            for c in range(4):
-                turn(b, c, there[c], copies[c % 2], pair_tiles[c])
-            for c in range(4):
-                turn_back(pair_tiles[c], back[c][:, 0 : 2 * P])
-            for c in range(4):
-                copies[c % 2](out=rounded[:, c, :, :], in_=back[c][:, 0 : 2 * P].rearrange("m (u t) -> m t u", u=2))
+            for g in range(4):
+                turned = there[g][:].rearrange("s (q r) -> s q r", q=4)
+                for tq in range(4):
+                    t0 = HALF * tq + P * g
+                    nc.tensor.transpose(turned[:, tq, :], window[:, t0 : t0 + P], ident[:])
+                copies[g % 2](
+                    out=pair_tiles[g][:].bitcast(BF16).rearrange("s (u m e) -> s u m e", u=2, e=2),
+                    in_=turned.rearrange("s q (p u e) -> s u (q p) e", u=2, e=2),
+                )
+            for g in range(4):
+                for u in range(2):
+                    cols = slice(P * u, P * (u + 1))
+                    nc.tensor.transpose(back[g][:, cols], pair_tiles[g][:, cols], ident[:])
+            for g in range(4):
+                copies[g % 2](out=rounded[:, g, :, :], in_=back[g][:, 0 : 2 * P].rearrange("m (u s) -> m s u", u=2))
             return rounded
 
-        y_codes = [keep.tile([P, 2 * HALF], U32, name=f"y_codes{i}", align_bytes=64) for i in range(2)]
-
-        def quant_out(b, rounded, parts):
-            flat = rounded[:].rearrange("m c t u -> m (c t u)").bitcast(BF16)
-            w = HALF // parts
+        def quantise_out(b, rounded, parts):
+            flat = rounded[:].rearrange("m g s u -> m (g s u)").bitcast(BF16)
+            width = HALF // parts
             base = HALF * (b % 2)
-            for s in range(parts):
+            for part in range(parts):
+                lo, hi = part * width, (part + 1) * width
                 nc.vector.quantize_mx(
-                    out=y_codes[b // 2][:, base + s * w : base + (s + 1) * w].bitcast(E4M3),
-                    scales=out_scales[4 * b : P, s * w : (s + 1) * w],
-                    in_=flat[:, 4 * s * w : 4 * (s + 1) * w],
+                    out=y_codes[b // 2][:, base + lo : base + hi].bitcast(E4M3),
+                    scales=y_scales[4 * b : P, lo:hi],
+                    in_=flat[:, 4 * lo : 4 * hi],
                 )
             if b % 2 == 1:
-                rows = words_out[32 * (b - 1) : 32 * (b + 1), :].rearrange("(d p) t -> p d t", d=2)
+                rows = words_out[QUAD * (b - 1) : QUAD * (b + 1), :].rearrange("(d p) t -> p d t", d=2)
                 for tq in range(4):
+                    quarter = y_codes[b // 2][QUAD * tq : QUAD * (tq + 1), :].bitcast(I32)
                     nc.sync.dma_start(
                         out=rows[:, :, HALF * tq : HALF * (tq + 1)],
-                        in_=y_codes[b // 2][32 * tq : 32 * (tq + 1), :].bitcast(I32).rearrange("p (d t) -> p d t", d=2),
+                        in_=quarter.rearrange("p (d s) -> p d s", d=2),
                     )
 
-        round_dy(0, 0, 0, HALF, 2 * VEC_COLS)
-        quant_dy(0, 0, 0, HALF)
-        round_dy(0, 1, 0, PIECE, VEC_COLS)
-        round_dy(0, 1, PIECE, HALF, VEC_COLS)
-        quant_dy(0, 1, 0, PIECE)
-        quant_dy(0, 1, PIECE, HALF)
-        nc.gpsimd.memset(windows[1][:].bitcast(U32), 0)
-        nc.gpsimd.memset(windows[2][:].bitcast(U32), 0)
-        add_res(0)
-        round_dy(1, 0, 0, HALF, 0)
-        round_dy(1, 1, 0, HALF, 0)
-        scatter(0)
-        quant_dy(1, 0, 0, HALF)
-        nc.gpsimd.memset(windows[3][:].bitcast(U32), 0)
-        add_res(1)
-        scatter(1)
-        quant_dy(1, 1, 0, HALF)
-        add_res(2)
-        accs[3] = product(0, 1, banks[3])
-        for k in range(4, 8):
-            leave_bank(k)
-        for k in range(4, 8):
-            finish(k, 0, HALF, dx[k][:])
+        round_dy(0, 0, 0, HALF, VECTOR_FIRST)
+        quantise_dy(0, 0, 0, HALF)
+        round_dy(0, 1, 0, PIECE, VECTOR_PIECE)
+        round_dy(0, 1, PIECE, HALF, VECTOR_PIECE)
+        quantise_dy(0, 1, 0, PIECE)
+        quantise_dy(0, 1, PIECE, HALF)
+        for a in range(2):
+            round_dy(1, a, 0, HALF, 0)
+        for k in range(2):
+            product_plus_res(k, new_sum(k))
+        for k in range(2):
+            scatter(k)
+        for a in range(2):
+            quantise_dy(1, a, 0, HALF)
+        spent = grouped[1, 1, 0][:].rearrange("p j i -> p (j i)").bitcast(F32)
+        product_plus_res(2, spent[:, 0:HALF])
         scatter(2)
-        add_res(3)
-        scatter(3)
-        store_rows(0)
-        made0 = planes(0, (nc.scalar.copy, nc.scalar.copy))
-        put(4, 0, HALF, dx[4][:])
-        store_rows(1)
-        made1 = planes(1, (nc.scalar.copy, nc.scalar.copy))
-        put(5, 0, HALF, dx[5][:])
-        store_rows(2)
-        made2 = planes(2, (nc.scalar.copy, nc.scalar.copy))
-        quant_out(0, made0, 1)
-        put(6, 0, HALF, dx[6][:])
-        quant_out(1, made1, 1)
-        put(7, 0, HALF, dx[7][:])
-        store_rows(3)
-        quant_out(2, made2, 1)
-        made3 = planes(3, (nc.vector.tensor_copy, nc.scalar.copy))
-        quant_out(3, made3, 2)
+        for k in range(3, 8):
+            product_plus_res(k, new_sum(k))
+        on_scalar = (nc.scalar.copy, nc.scalar.copy)
+        regrouped = []
+        for b in range(3):
+            scatter(3 + b)
+            regrouped.append(store_and_regroup(b, on_scalar))
+        for b in range(2):
+            quantise_out(b, regrouped[b], 1)
+            scatter(6 + b)
+        quantise_out(2, regrouped[2], 1)
+        quantise_out(3, store_and_regroup(3, (nc.vector.tensor_copy, nc.scalar.copy)), 2)
         for tq in range(4):
             nc.scalar.dma_start(
                 out=scales_out[:, P * tq : P * (tq + 1)],
-                in_=out_scales[32 * tq : 32 * tq + 16, :].bitcast(I32),
+                in_=y_scales[QUAD * tq : QUAD * tq + 16, :].bitcast(I32),
             )

@@ -22,9 +22,9 @@ P = 128
 HALF = 512
 PIECE = 256
 QUAD = 32
-WINDOWS = 3
-VECTOR_FIRST = 192
+VECTOR_FIRST = 96
 VECTOR_PIECE = 160
+PRODUCT_BANK = [0, 1, 2, 0, 1, 2, 3, 3]
 TILES = [(0, 0), (1, 0), (2, 0), (0, 1), (1, 1), (2, 1), (3, 0), (3, 1)]
 
 
@@ -41,9 +41,9 @@ def tile_list_embg_mix_resP_kernel(
         w8 = keep.tile([P, N], U32, name="w8", align_bytes=64)
         w4 = keep.tile([P, 2 * N], U8, name="w4", align_bytes=64)
         w_scales = keep.tile([P, 2 * N], U8, name="w_scales", align_bytes=64)
-        gain = [keep.tile([P, HALF], F32, name=f"gain{c}", align_bytes=64) for c in range(2)]
+        gain = keep.tile([P, J], F32, name="gain", align_bytes=64)
         ident = keep.tile([P, P], F32, name="ident", align_bytes=64)
-        windows = [keep.tile([P, T], F32, name=f"window{w}", align_bytes=64) for w in range(WINDOWS)]
+        windows = {b: keep.tile([P, T], F32, name=f"window{b}", align_bytes=64) for b in range(2)}
 
         raw = {}
         resid = {}
@@ -60,11 +60,11 @@ def tile_list_embg_mix_resP_kernel(
             nc.sync.dma_start(out=resid[b, c][:], in_=res[P * b : P * (b + 1), c * HALF : (c + 1) * HALF])
 
         def load_gain(c):
-            nc.sync.dma_start(out=gain[c][:], in_=wgo[:, c * HALF : (c + 1) * HALF])
+            nc.sync.dma_start(out=gain[:, c * HALF : (c + 1) * HALF], in_=wgo[:, c * HALF : (c + 1) * HALF])
 
-        def load_scales(a, source):
+        def load_scales(a, source, queue):
             for q in range(4):
-                nc.sync.dma_start(
+                queue.dma_start(
                     out=w_scales[QUAD * q : QUAD * q + 4, a * N : (a + 1) * N].bitcast(I32),
                     in_=source[0][4 * q : 4 * q + 4, :].bitcast(I32),
                 )
@@ -75,38 +75,40 @@ def tile_list_embg_mix_resP_kernel(
         nc.vector.memset(warm_in[:], 0.0)
         nc.scalar.copy(out=warm_out[:], in_=warm_in[:])
 
-        load_dy(0, 0, 0, HALF)
-        load_scales(0, w8_scales)
+        nc.sync.dma_start(offsets[:], offs)
         load_dy(0, 1, 0, PIECE)
-        nc.sync.dma_start(out=w8[:].bitcast(I32), in_=w8_words[0].rearrange("p n i -> p (n i)").bitcast(I32))
-        load_dy(0, 1, PIECE, HALF)
-        load_scales(1, w4_scales)
+        load_scales(1, w4_scales, nc.sync)
         nc.sync.dma_start(out=w4[:].bitcast(I32), in_=w4_words[0].bitcast(I32))
+        load_dy(0, 1, PIECE, HALF)
+        load_dy(0, 0, 0, PIECE)
+        load_dy(0, 0, PIECE, HALF)
+        load_scales(0, w8_scales, nc.sync)
+        nc.sync.dma_start(out=w8[:].bitcast(I32), in_=w8_words[0].rearrange("p n i -> p (n i)").bitcast(I32))
         load_res(0, 0)
         load_gain(0)
-        nc.sync.dma_start(offsets[:], offs)
         load_res(1, 0)
-        load_dy(1, 0, 0, HALF)
-        load_dy(1, 1, 0, HALF)
         load_res(2, 0)
+        load_res(3, 0)
+        load_dy(1, 1, 0, HALF)
+        load_dy(1, 0, 0, HALF)
         load_res(0, 1)
         load_gain(1)
         load_res(1, 1)
         load_res(2, 1)
-        load_res(3, 0)
         load_res(3, 1)
 
-        for window in windows:
-            nc.vector.memset(window[:].bitcast(U32), 0)
+        for b in range(2):
+            nc.vector.memset(windows[b][:].bitcast(U32), 0)
         make_identity(nc, ident[:])
 
         grouped = {}
         dy_codes = {}
         dy_scales = {}
 
-        def round_dy(c, a, lo, hi, vector_cols):
+        def round_dy(c, a, lo, hi, vector_cols, tag=None):
             key = (c, a, lo)
-            grouped[key] = keep.tile([P, hi - lo, 4], BF16, name=f"grouped{c}{a}{lo}", align_bytes=64)
+            name = f"grouped{c}{a}{lo}"
+            grouped[key] = keep.tile([P, hi - lo, 4], BF16, name=name, tag=tag or name, align_bytes=64)
             for copy, x, y in ((nc.scalar.copy, vector_cols, hi - lo), (nc.vector.tensor_copy, 0, vector_cols)):
                 if y > x:
                     copy(
@@ -126,47 +128,64 @@ def tile_list_embg_mix_resP_kernel(
 
         sums = {}
 
-        def product_plus_res(k, total):
+        def mx_pass(k, a):
             b, c = TILES[k]
-            acc = banks[k % 4]
+            if a == 0:
+                words = w8[:, P * b : P * (b + 1)].bitcast(E4M3)
+            else:
+                words = w4[:, 2 * P * b : 2 * P * (b + 1)].bitcast(E2M1)
             nc.tensor.matmul_mx(
-                out=acc[:],
-                lhsT=w8[:, P * b : P * (b + 1)].bitcast(E4M3),
-                lhsT_scale=w_scales[:, P * b : P * (b + 1)],
-                rhs=dy_codes[c, 0][:].bitcast(E5M2),
-                rhs_scale=dy_scales[c, 0][:],
-                start=True,
-                stop=False,
+                out=banks[PRODUCT_BANK[k]][:],
+                lhsT=words,
+                lhsT_scale=w_scales[:, a * N + P * b : a * N + P * (b + 1)],
+                rhs=dy_codes[c, a][:].bitcast(E5M2),
+                rhs_scale=dy_scales[c, a][:],
+                start=(a == 1),
+                stop=(a == 0),
             )
-            nc.tensor.matmul_mx(
-                out=acc[:],
-                lhsT=w4[:, 2 * P * b : 2 * P * (b + 1)].bitcast(E2M1),
-                lhsT_scale=w_scales[:, N + P * b : N + P * (b + 1)],
-                rhs=dy_codes[c, 1][:].bitcast(E5M2),
-                rhs_scale=dy_scales[c, 1][:],
-                start=False,
-                stop=True,
-            )
-            nc.vector.tensor_tensor(total, acc[:], resid[b, c][:], ADD)
+
+        def add_res(k, total):
+            b, c = TILES[k]
+            nc.vector.tensor_tensor(total, banks[PRODUCT_BANK[k]][:], resid[b, c][:], ADD)
             sums[k] = total
 
-        def new_sum(k):
-            total = keep.tile([P, HALF], F32, name=f"sum{k}", align_bytes=64)
+        def add_res_by_transposes(k, total, there, back):
+            b, c = TILES[k]
+            product = keep.tile([P, HALF], F32, name=f"product{k}", align_bytes=64)
+            turned_sum = keep.tile([P, HALF], F32, name=f"turned_sum{k}", align_bytes=64)
+            nc.scalar.copy(out=product[:], in_=banks[PRODUCT_BANK[k]][:])
+            for j0 in range(0, HALF, P):
+                cols = slice(j0, j0 + P)
+                nc.tensor.matmul(there[:, cols], product[:, cols], ident[:], start=True, stop=False, is_transpose=True)
+                nc.tensor.matmul(there[:, cols], resid[b, c][:, cols], ident[:], start=False, stop=True, is_transpose=True)
+            nc.scalar.copy(out=turned_sum[:], in_=there[:])
+            for j0 in range(0, HALF, P):
+                cols = slice(j0, j0 + P)
+                nc.tensor.transpose(back[:, cols], turned_sum[:, cols], ident[:])
+            nc.scalar.copy(out=total, in_=back[:])
+            sums[k] = total
+
+        def new_sum(k, tag=None):
+            total = keep.tile([P, HALF], F32, name=f"sum{k}", tag=tag or f"sum{k}", align_bytes=64)
             return total[:]
 
         def scatter(k):
             b, c = TILES[k]
             where = offsets[:, c * HALF // 16 : (c + 1) * HALF // 16]
-            nc.vector.tensor_tensor(windows[b % WINDOWS][:].indirect(where), sums[k], gain[c][:], MULT)
+            nc.vector.tensor_tensor(windows[b][:].indirect(where), sums[k], gain[:, c * HALF : (c + 1) * HALF], MULT)
+
+        def late_window(b, tag):
+            windows[b] = keep.tile([P, T], F32, name=f"window{b}", tag=tag, align_bytes=64)
+            nc.gpsimd.memset(windows[b][:].bitcast(U32), 0)
 
         words_out = out_1[0].rearrange("p t i -> p (t i)").bitcast(I32)
         scales_out = out_2[0].bitcast(I32)
         pair_tiles = [keep.tile([P, 2 * P], F32, name=f"pairs{g}", align_bytes=64) for g in range(4)]
-        y_codes = [keep.tile([P, 2 * HALF], U32, name=f"y_codes{d}", align_bytes=64) for d in range(2)]
+        y_codes = keep.tile([P, 4 * HALF], U32, name="y_codes", align_bytes=64)
         y_scales = keep.tile([P, HALF], U8, name="y_scales", align_bytes=64)
 
-        def store_and_regroup(b, copies):
-            window = windows[b % WINDOWS]
+        def store_and_regroup(b, copies, back_copies):
+            window = windows[b]
             nc.sync.dma_start(out=out_0[P * b : P * (b + 1), :], in_=window[:])
             rounded = keep.tile([P, 4, P, 2], F32, name=f"rounded{b}", align_bytes=64)
             there, back = (banks[4:], banks[:4]) if b % 2 == 0 else (banks[:4], banks[4:])
@@ -184,58 +203,75 @@ def tile_list_embg_mix_resP_kernel(
                     cols = slice(P * u, P * (u + 1))
                     nc.tensor.transpose(back[g][:, cols], pair_tiles[g][:, cols], ident[:])
             for g in range(4):
-                copies[g % 2](out=rounded[:, g, :, :], in_=back[g][:, 0 : 2 * P].rearrange("m (u s) -> m s u", u=2))
+                back_copies[g % 2](out=rounded[:, g, :, :], in_=back[g][:, 0 : 2 * P].rearrange("m (u s) -> m s u", u=2))
             return rounded
 
         def quantise_out(b, rounded, parts):
             flat = rounded[:].rearrange("m g s u -> m (g s u)").bitcast(BF16)
             width = HALF // parts
-            base = HALF * (b % 2)
+            base = HALF * b
             for part in range(parts):
                 lo, hi = part * width, (part + 1) * width
                 nc.vector.quantize_mx(
-                    out=y_codes[b // 2][:, base + lo : base + hi].bitcast(E4M3),
+                    out=y_codes[:, base + lo : base + hi].bitcast(E4M3),
                     scales=y_scales[4 * b : P, lo:hi],
                     in_=flat[:, 4 * lo : 4 * hi],
                 )
-            if b % 2 == 1:
-                rows = words_out[QUAD * (b - 1) : QUAD * (b + 1), :].rearrange("(d p) t -> p d t", d=2)
-                for tq in range(4):
-                    quarter = y_codes[b // 2][QUAD * tq : QUAD * (tq + 1), :].bitcast(I32)
-                    nc.sync.dma_start(
-                        out=rows[:, :, HALF * tq : HALF * (tq + 1)],
-                        in_=quarter.rearrange("p (d s) -> p d s", d=2),
-                    )
 
-        round_dy(0, 0, 0, HALF, VECTOR_FIRST)
-        quantise_dy(0, 0, 0, HALF)
-        round_dy(0, 1, 0, PIECE, VECTOR_PIECE)
-        round_dy(0, 1, PIECE, HALF, VECTOR_PIECE)
+        def store_codes(b0, b1):
+            rows = words_out[QUAD * b0 : QUAD * b1, :].rearrange("(d p) t -> p d t", p=QUAD)
+            for tq in range(4):
+                quarter = y_codes[QUAD * tq : QUAD * (tq + 1), HALF * b0 : HALF * b1].bitcast(I32)
+                nc.sync.dma_start(
+                    out=rows[:, :, HALF * tq : HALF * (tq + 1)],
+                    in_=quarter.rearrange("p (d s) -> p d s", s=HALF),
+                )
+
+        round_dy(0, 1, 0, PIECE, 0)
+        round_dy(0, 1, PIECE, HALF, VECTOR_FIRST)
         quantise_dy(0, 1, 0, PIECE)
         quantise_dy(0, 1, PIECE, HALF)
-        for a in range(2):
+        for k in (0, 1, 2, 6):
+            mx_pass(k, 1)
+        round_dy(0, 0, 0, PIECE, VECTOR_PIECE)
+        round_dy(0, 0, PIECE, HALF, VECTOR_PIECE, tag="head_end")
+        quantise_dy(0, 0, 0, PIECE)
+        quantise_dy(0, 0, PIECE, HALF)
+        late_window(2, "head_end")
+        for a in (1, 0):
             round_dy(1, a, 0, HALF, 0)
+        for k in (0, 1, 2, 6):
+            mx_pass(k, 0)
         for k in range(2):
-            product_plus_res(k, new_sum(k))
+            add_res(k, new_sum(k))
         for k in range(2):
             scatter(k)
-        for a in range(2):
+        for a in (1, 0):
             quantise_dy(1, a, 0, HALF)
-        spent = grouped[1, 1, 0][:].rearrange("p j i -> p (j i)").bitcast(F32)
-        product_plus_res(2, spent[:, 0:HALF])
+        last_sums = keep.tile([P, J], F32, name="last_sums", align_bytes=64)
+        add_res_by_transposes(2, raw[1, 0, 0][:, 0, :], banks[4], banks[5])
+        add_res_by_transposes(6, last_sums[:, 0:HALF], banks[6], banks[7])
         scatter(2)
-        for k in range(3, 8):
-            product_plus_res(k, new_sum(k))
+        for k in (3, 4, 5, 7):
+            mx_pass(k, 1)
+            mx_pass(k, 0)
+        add_res(3, new_sum(3, "third"))
+        add_res(4, new_sum(4))
+        add_res_by_transposes(5, new_sum(5), banks[4], banks[5])
+        add_res_by_transposes(7, last_sums[:, HALF:J], banks[6], banks[7])
         on_scalar = (nc.scalar.copy, nc.scalar.copy)
         regrouped = []
         for b in range(3):
             scatter(3 + b)
-            regrouped.append(store_and_regroup(b, on_scalar))
-        for b in range(2):
+            if b == 0:
+                late_window(3, "third")
+            regrouped.append(store_and_regroup(b, on_scalar, on_scalar))
+        nc.vector.tensor_tensor(windows[3][:].indirect(offsets[:]), last_sums[:], gain[:], MULT)
+        for b in range(3):
             quantise_out(b, regrouped[b], 1)
-            scatter(6 + b)
-        quantise_out(2, regrouped[2], 1)
-        quantise_out(3, store_and_regroup(3, (nc.vector.tensor_copy, nc.scalar.copy)), 2)
+        store_codes(0, 3)
+        quantise_out(3, store_and_regroup(3, on_scalar, (nc.vector.tensor_copy, nc.scalar.copy)), 2)
+        store_codes(3, 4)
         for tq in range(4):
             nc.scalar.dma_start(
                 out=scales_out[:, P * tq : P * (tq + 1)],

@@ -25,6 +25,7 @@ QUAD = 32
 VECTOR_FIRST = 96
 VECTOR_PIECE = 160
 PRODUCT_BANK = [0, 1, 2, 0, 1, 2, 3, 3]
+LAST_RAW = 8 * T
 TILES = [(0, 0), (1, 0), (2, 0), (0, 1), (1, 1), (2, 1), (3, 0), (3, 1)]
 
 
@@ -34,6 +35,7 @@ def tile_list_embg_mix_resP_kernel(
     nc = tc.nc
     with ExitStack() as ctx:
         keep = ctx.enter_context(tc.tile_pool(name="keep", bufs=1))
+        shared = ctx.enter_context(tc.tile_pool(name="shared", bufs=1))
         psum = ctx.enter_context(tc.psum_pool(name="psum", bufs=1))
         banks = [psum.tile([P, HALF], F32, name=f"bank{i}") for i in range(8)]
 
@@ -48,8 +50,12 @@ def tile_list_embg_mix_resP_kernel(
         raw = {}
         resid = {}
 
-        def load_dy(c, a, lo, hi):
-            raw[c, a, lo] = keep.tile([P, 4, hi - lo], F32, name=f"raw{c}{a}{lo}", align_bytes=64)
+        def load_dy(c, a, lo, hi, offset=None):
+            name = f"raw{c}{a}{lo}"
+            if offset is None:
+                raw[c, a, lo] = keep.tile([P, 4, hi - lo], F32, name=name, align_bytes=64)
+            else:
+                raw[c, a, lo] = shared.tile([P, 4, hi - lo], F32, name=name, align_bytes=64, offset=offset)
             nc.sync.dma_start(
                 out=raw[c, a, lo][:],
                 in_=dy[512 * a : 512 * (a + 1), c * HALF + lo : c * HALF + hi].rearrange("(p i) j -> p i j", i=4),
@@ -85,12 +91,13 @@ def tile_list_embg_mix_resP_kernel(
         load_scales(0, w8_scales, nc.sync)
         nc.sync.dma_start(out=w8[:].bitcast(I32), in_=w8_words[0].rearrange("p n i -> p (n i)").bitcast(I32))
         load_res(0, 0)
-        load_gain(0)
         load_res(1, 0)
-        load_res(2, 0)
-        load_res(3, 0)
+        load_gain(0)
         load_dy(1, 1, 0, HALF)
-        load_dy(1, 0, 0, HALF)
+        load_res(2, 0)
+        load_dy(1, 0, 0, PIECE)
+        load_dy(1, 0, PIECE, HALF, offset=LAST_RAW)
+        load_res(3, 0)
         load_res(0, 1)
         load_gain(1)
         load_res(1, 1)
@@ -105,10 +112,13 @@ def tile_list_embg_mix_resP_kernel(
         dy_codes = {}
         dy_scales = {}
 
-        def round_dy(c, a, lo, hi, vector_cols, tag=None):
+        def round_dy(c, a, lo, hi, vector_cols, offset=None):
             key = (c, a, lo)
             name = f"grouped{c}{a}{lo}"
-            grouped[key] = keep.tile([P, hi - lo, 4], BF16, name=name, tag=tag or name, align_bytes=64)
+            if offset is None:
+                grouped[key] = keep.tile([P, hi - lo, 4], BF16, name=name, align_bytes=64)
+            else:
+                grouped[key] = shared.tile([P, hi - lo, 4], BF16, name=name, align_bytes=64, offset=offset)
             for copy, x, y in ((nc.scalar.copy, vector_cols, hi - lo), (nc.vector.tensor_copy, 0, vector_cols)):
                 if y > x:
                     copy(
@@ -149,7 +159,7 @@ def tile_list_embg_mix_resP_kernel(
             nc.vector.tensor_tensor(total, banks[PRODUCT_BANK[k]][:], resid[b, c][:], ADD)
             sums[k] = total
 
-        def add_res_by_transposes(k, total, there, back):
+        def add_res_by_transposes(k, there, back):
             b, c = TILES[k]
             product = keep.tile([P, HALF], F32, name=f"product{k}", align_bytes=64)
             turned_sum = keep.tile([P, HALF], F32, name=f"turned_sum{k}", align_bytes=64)
@@ -162,11 +172,16 @@ def tile_list_embg_mix_resP_kernel(
             for j0 in range(0, HALF, P):
                 cols = slice(j0, j0 + P)
                 nc.tensor.transpose(back[:, cols], turned_sum[:, cols], ident[:])
+
+        def fetch_sum(k, total, back):
             nc.scalar.copy(out=total, in_=back[:])
             sums[k] = total
 
-        def new_sum(k, tag=None):
-            total = keep.tile([P, HALF], F32, name=f"sum{k}", tag=tag or f"sum{k}", align_bytes=64)
+        def new_sum(k, offset=None):
+            if offset is None:
+                total = keep.tile([P, HALF], F32, name=f"sum{k}", align_bytes=64)
+            else:
+                total = shared.tile([P, HALF], F32, name=f"sum{k}", align_bytes=64, offset=offset)
             return total[:]
 
         def scatter(k):
@@ -174,8 +189,8 @@ def tile_list_embg_mix_resP_kernel(
             where = offsets[:, c * HALF // 16 : (c + 1) * HALF // 16]
             nc.vector.tensor_tensor(windows[b][:].indirect(where), sums[k], gain[:, c * HALF : (c + 1) * HALF], MULT)
 
-        def late_window(b, tag):
-            windows[b] = keep.tile([P, T], F32, name=f"window{b}", tag=tag, align_bytes=64)
+        def late_window(b, offset):
+            windows[b] = shared.tile([P, T], F32, name=f"window{b}", align_bytes=64, offset=offset)
             nc.gpsimd.memset(windows[b][:].bitcast(U32), 0)
 
         words_out = out_1[0].rearrange("p t i -> p (t i)").bitcast(I32)
@@ -208,10 +223,8 @@ def tile_list_embg_mix_resP_kernel(
 
         def quantise_out(b, rounded, parts):
             flat = rounded[:].rearrange("m g s u -> m (g s u)").bitcast(BF16)
-            width = HALF // parts
             base = HALF * b
-            for part in range(parts):
-                lo, hi = part * width, (part + 1) * width
+            for lo, hi in parts:
                 nc.vector.quantize_mx(
                     out=y_codes[:, base + lo : base + hi].bitcast(E4M3),
                     scales=y_scales[4 * b : P, lo:hi],
@@ -231,47 +244,66 @@ def tile_list_embg_mix_resP_kernel(
         round_dy(0, 1, PIECE, HALF, VECTOR_FIRST)
         quantise_dy(0, 1, 0, PIECE)
         quantise_dy(0, 1, PIECE, HALF)
-        for k in (0, 1, 2, 6):
+        for k in range(3):
             mx_pass(k, 1)
         round_dy(0, 0, 0, PIECE, VECTOR_PIECE)
-        round_dy(0, 0, PIECE, HALF, VECTOR_PIECE, tag="head_end")
+        round_dy(0, 0, PIECE, HALF, VECTOR_PIECE, offset=0)
         quantise_dy(0, 0, 0, PIECE)
         quantise_dy(0, 0, PIECE, HALF)
-        late_window(2, "head_end")
-        for a in (1, 0):
-            round_dy(1, a, 0, HALF, 0)
-        for k in (0, 1, 2, 6):
+        late_window(2, 0)
+        for k in range(3):
             mx_pass(k, 0)
+        add_res_by_transposes(2, banks[4], banks[5])
+        second = keep.tile([P, 2, HALF, 4], BF16, name="second", align_bytes=64)
+        for a, lo, hi in ((1, 0, HALF), (0, 0, PIECE), (0, PIECE, HALF)):
+            nc.scalar.copy(
+                out=second[:, a, lo:hi, :].rearrange("p (g e) i -> p g i e", e=4),
+                in_=raw[1, a, lo][:].rearrange("p i (g e) -> p g i e", e=4),
+            )
+        fetch_sum(2, new_sum(2, LAST_RAW + 2 * HALF), banks[5])
+        mx_pass(6, 1)
+        mx_pass(6, 0)
         for k in range(2):
             add_res(k, new_sum(k))
         for k in range(2):
             scatter(k)
-        for a in (1, 0):
-            quantise_dy(1, a, 0, HALF)
+        second_codes = keep.tile([P, 2 * HALF], U32, name="second_codes", align_bytes=64)
+        second_scales = keep.tile([P, 2 * HALF], U8, name="second_scales", align_bytes=64)
+        nc.vector.quantize_mx(
+            out=second_codes[:].bitcast(E5M2),
+            scales=second_scales[:],
+            in_=second[:].rearrange("p a j i -> p (a j i)"),
+        )
+        for a in range(2):
+            dy_codes[1, a] = second_codes[:, a * HALF : (a + 1) * HALF]
+            dy_scales[1, a] = second_scales[:, a * HALF : (a + 1) * HALF]
         last_sums = keep.tile([P, J], F32, name="last_sums", align_bytes=64)
-        add_res_by_transposes(2, raw[1, 0, 0][:, 0, :], banks[4], banks[5])
-        add_res_by_transposes(6, last_sums[:, 0:HALF], banks[6], banks[7])
+        add_res_by_transposes(6, banks[6], banks[7])
+        fetch_sum(6, last_sums[:, 0:HALF], banks[7])
         scatter(2)
         for k in (3, 4, 5, 7):
             mx_pass(k, 1)
             mx_pass(k, 0)
-        add_res(3, new_sum(3, "third"))
-        add_res(4, new_sum(4))
-        add_res_by_transposes(5, new_sum(5), banks[4], banks[5])
-        add_res_by_transposes(7, last_sums[:, HALF:J], banks[6], banks[7])
+        add_res(3, new_sum(3, LAST_RAW))
+        add_res(4, new_sum(4, LAST_RAW + 4 * HALF))
+        add_res_by_transposes(5, banks[6], banks[7])
+        fetch_sum(5, new_sum(5), banks[7])
+        add_res_by_transposes(7, banks[4], banks[5])
+        fetch_sum(7, last_sums[:, HALF:J], banks[5])
         on_scalar = (nc.scalar.copy, nc.scalar.copy)
         regrouped = []
         for b in range(3):
             scatter(3 + b)
             if b == 0:
-                late_window(3, "third")
+                late_window(3, LAST_RAW + 2 * HALF - 4 * T)
             regrouped.append(store_and_regroup(b, on_scalar, on_scalar))
         nc.vector.tensor_tensor(windows[3][:].indirect(offsets[:]), last_sums[:], gain[:], MULT)
         for b in range(3):
-            quantise_out(b, regrouped[b], 1)
-        store_codes(0, 3)
-        quantise_out(3, store_and_regroup(3, on_scalar, (nc.vector.tensor_copy, nc.scalar.copy)), 2)
-        store_codes(3, 4)
+            quantise_out(b, regrouped[b], [(0, HALF)])
+            if b == 1:
+                store_codes(0, 2)
+        quantise_out(3, store_and_regroup(3, on_scalar, (nc.vector.tensor_copy, nc.scalar.copy)), [(0, 2 * P), (2 * P, HALF)])
+        store_codes(2, 4)
         for tq in range(4):
             nc.scalar.dma_start(
                 out=scales_out[:, P * tq : P * (tq + 1)],

@@ -17,6 +17,7 @@ E5M2 = mybir.dt.float8_e5m2_x4
 E2M1 = mybir.dt.float4_e2m1fn_x4
 ADD = mybir.AluOpType.add
 MULT = mybir.AluOpType.mult
+COPY = mybir.ActivationFunctionType.Copy
 
 P = 128
 HALF = 512
@@ -76,6 +77,9 @@ def tile_list_embg_mix_resP_kernel(
                 )
 
         nc.gpsimd.memset(w_scales[:].bitcast(U32), 0)
+        gain_rows = keep.tile([P, P], F32, name="gain_rows", align_bytes=64)
+        gain_cols = keep.tile([P, J // P], F32, name="gain_cols", align_bytes=64)
+        nc.gpsimd.memset(gain_rows[:], 0.0)
         warm_in = keep.tile([P, 8], F32, name="warm_in")
         warm_out = keep.tile([P, 8], BF16, name="warm_out")
         nc.vector.memset(warm_in[:], 0.0)
@@ -93,6 +97,7 @@ def tile_list_embg_mix_resP_kernel(
         load_res(0, 0)
         load_res(1, 0)
         load_gain(0)
+        nc.sync.dma_start(out=gain_rows[0 : J // P, :], in_=wgo[0].rearrange("(h q) -> h q", q=P))
         load_dy(1, 1, 0, HALF)
         load_res(2, 0)
         load_dy(1, 0, 0, PIECE)
@@ -168,7 +173,11 @@ def tile_list_embg_mix_resP_kernel(
                 cols = slice(j0, j0 + P)
                 nc.tensor.matmul(there[:, cols], product[:, cols], ident[:], start=True, stop=False, is_transpose=True)
                 nc.tensor.matmul(there[:, cols], resid[b, c][:, cols], ident[:], start=False, stop=True, is_transpose=True)
-            nc.scalar.copy(out=turned_sum[:], in_=there[:])
+            for j0 in range(0, HALF, P):
+                h = (c * HALF + j0) // P
+                nc.scalar.activation(
+                    turned_sum[:, j0 : j0 + P], there[:, j0 : j0 + P], COPY, scale=gain_cols[:, h : h + 1]
+                )
             for j0 in range(0, HALF, P):
                 cols = slice(j0, j0 + P)
                 nc.tensor.transpose(back[:, cols], turned_sum[:, cols], ident[:])
@@ -187,7 +196,10 @@ def tile_list_embg_mix_resP_kernel(
         def scatter(k):
             b, c = TILES[k]
             where = offsets[:, c * HALF // 16 : (c + 1) * HALF // 16]
-            nc.vector.tensor_tensor(windows[b][:].indirect(where), sums[k], gain[:, c * HALF : (c + 1) * HALF], MULT)
+            if k in (2, 5):
+                nc.vector.tensor_copy(windows[b][:].indirect(where), sums[k])
+            else:
+                nc.vector.tensor_tensor(windows[b][:].indirect(where), sums[k], gain[:, c * HALF : (c + 1) * HALF], MULT)
 
         def late_window(b, offset):
             windows[b] = shared.tile([P, T], F32, name=f"window{b}", align_bytes=64, offset=offset)
@@ -253,6 +265,8 @@ def tile_list_embg_mix_resP_kernel(
         late_window(2, 0)
         for k in range(3):
             mx_pass(k, 0)
+        nc.tensor.transpose(banks[6][:, 0:P], gain_rows[:], ident[:])
+        nc.scalar.copy(out=gain_cols[:], in_=banks[6][:, 0 : J // P])
         add_res_by_transposes(2, banks[4], banks[5])
         second = keep.tile([P, 2, HALF, 4], BF16, name="second", align_bytes=64)
         for a, lo, hi in ((1, 0, HALF), (0, 0, PIECE), (0, PIECE, HALF)):
@@ -297,7 +311,7 @@ def tile_list_embg_mix_resP_kernel(
             if b == 0:
                 late_window(3, LAST_RAW + 2 * HALF - 4 * T)
             regrouped.append(store_and_regroup(b, on_scalar, on_scalar))
-        nc.vector.tensor_tensor(windows[3][:].indirect(offsets[:]), last_sums[:], gain[:], MULT)
+        nc.vector.tensor_copy(windows[3][:].indirect(offsets[:]), last_sums[:])
         for b in range(3):
             quantise_out(b, regrouped[b], [(0, HALF)])
             if b == 1:

@@ -221,7 +221,7 @@ def tile_list_embg_mix_resP_kernel(
                 for tq in range(4):
                     t0 = HALF * tq + P * g
                     nc.tensor.transpose(turned[:, tq, :], window[:, t0 : t0 + P], ident[:])
-                copies[g % 2](
+                copies[g](
                     out=pair_tiles[g][:].bitcast(BF16).rearrange("s (u m e) -> s u m e", u=2, e=2),
                     in_=turned.rearrange("s q (p u e) -> s u (q p) e", u=2, e=2),
                 )
@@ -230,7 +230,7 @@ def tile_list_embg_mix_resP_kernel(
                     cols = slice(P * u, P * (u + 1))
                     nc.tensor.transpose(back[g][:, cols], pair_tiles[g][:, cols], ident[:])
             for g in range(4):
-                back_copies[g % 2](out=rounded[:, g, :, :], in_=back[g][:, 0 : 2 * P].rearrange("m (u s) -> m s u", u=2))
+                back_copies[g](out=rounded[:, g, :, :], in_=back[g][:, 0 : 2 * P].rearrange("m (u s) -> m s u", u=2))
             return rounded
 
         def quantise_out(b, rounded, parts):
@@ -243,11 +243,11 @@ def tile_list_embg_mix_resP_kernel(
                     in_=flat[:, 4 * lo : 4 * hi],
                 )
 
-        def store_codes(b0, b1):
+        def store_codes(b0, b1, upper_queue):
             rows = words_out[QUAD * b0 : QUAD * b1, :].rearrange("(d p) t -> p d t", p=QUAD)
-            for tq in range(4):
+            for tq in (0, 2, 1, 3):
                 quarter = y_codes[QUAD * tq : QUAD * (tq + 1), HALF * b0 : HALF * b1].bitcast(I32)
-                nc.sync.dma_start(
+                (nc.sync if tq < 2 else upper_queue).dma_start(
                     out=rows[:, :, HALF * tq : HALF * (tq + 1)],
                     in_=quarter.rearrange("p (d s) -> p d s", s=HALF),
                 )
@@ -304,7 +304,8 @@ def tile_list_embg_mix_resP_kernel(
         fetch_sum(5, new_sum(5), banks[7])
         add_res_by_transposes(7, banks[4], banks[5])
         fetch_sum(7, last_sums[:, HALF:J], banks[5])
-        on_scalar = (nc.scalar.copy, nc.scalar.copy)
+        on_scalar = [nc.scalar.copy] * 4
+        on_s, on_v = nc.scalar.copy, nc.vector.tensor_copy
         regrouped = []
         for b in range(3):
             scatter(3 + b)
@@ -314,12 +315,11 @@ def tile_list_embg_mix_resP_kernel(
         nc.vector.tensor_copy(windows[3][:].indirect(offsets[:]), last_sums[:])
         for b in range(3):
             quantise_out(b, regrouped[b], [(0, HALF)])
-            if b == 1:
-                store_codes(0, 2)
-        quantise_out(3, store_and_regroup(3, on_scalar, (nc.vector.tensor_copy, nc.scalar.copy)), [(0, 2 * P), (2 * P, HALF)])
-        store_codes(2, 4)
+        store_codes(0, 3, nc.scalar)
+        quantise_out(3, store_and_regroup(3, [on_s, on_s, on_s, on_v], [on_v, on_s, on_v, on_s]), [(0, 2 * P), (2 * P, HALF)])
+        store_codes(3, 4, nc.scalar)
         for tq in range(4):
-            nc.scalar.dma_start(
+            (nc.sync if tq < 2 else nc.scalar).dma_start(
                 out=scales_out[:, P * tq : P * (tq + 1)],
                 in_=y_scales[QUAD * tq : QUAD * tq + 16, :].bitcast(I32),
             )

@@ -103,11 +103,11 @@ def tile_list_embg_mix_resP_kernel(
         load_dy(1, 0, 0, PIECE)
         load_dy(1, 0, PIECE, HALF, offset=LAST_RAW)
         load_res(3, 0)
+        load_res(3, 1)
+        load_res(2, 1)
         load_res(0, 1)
         load_gain(1)
         load_res(1, 1)
-        load_res(2, 1)
-        load_res(3, 1)
 
         for b in range(2):
             nc.vector.memset(windows[b][:].bitcast(U32), 0)
@@ -164,6 +164,12 @@ def tile_list_embg_mix_resP_kernel(
             nc.vector.tensor_tensor(total, banks[PRODUCT_BANK[k]][:], resid[b, c][:], ADD)
             sums[k] = total
 
+        def turn_res(k, there):
+            b, c = TILES[k]
+            for j0 in range(0, HALF, P):
+                cols = slice(j0, j0 + P)
+                nc.tensor.matmul(there[:, cols], resid[b, c][:, cols], ident[:], start=(j0 == 0), stop=False, is_transpose=True)
+
         def add_res_by_transposes(k, there, back):
             b, c = TILES[k]
             product = keep.tile([P, HALF], F32, name=f"product{k}", align_bytes=64)
@@ -171,8 +177,7 @@ def tile_list_embg_mix_resP_kernel(
             nc.scalar.copy(out=product[:], in_=banks[PRODUCT_BANK[k]][:])
             for j0 in range(0, HALF, P):
                 cols = slice(j0, j0 + P)
-                nc.tensor.matmul(there[:, cols], product[:, cols], ident[:], start=True, stop=False, is_transpose=True)
-                nc.tensor.matmul(there[:, cols], resid[b, c][:, cols], ident[:], start=False, stop=True, is_transpose=True)
+                nc.tensor.matmul(there[:, cols], product[:, cols], ident[:], start=False, stop=(j0 == HALF - P), is_transpose=True)
             for j0 in range(0, HALF, P):
                 h = (c * HALF + j0) // P
                 nc.scalar.activation(
@@ -267,6 +272,7 @@ def tile_list_embg_mix_resP_kernel(
             mx_pass(k, 0)
         nc.tensor.transpose(banks[6][:, 0:P], gain_rows[:], ident[:])
         nc.scalar.copy(out=gain_cols[:], in_=banks[6][:, 0 : J // P])
+        turn_res(2, banks[4])
         add_res_by_transposes(2, banks[4], banks[5])
         second = keep.tile([P, 2, HALF, 4], BF16, name="second", align_bytes=64)
         for a, lo, hi in ((1, 0, HALF), (0, 0, PIECE), (0, PIECE, HALF)):
@@ -292,8 +298,11 @@ def tile_list_embg_mix_resP_kernel(
             dy_codes[1, a] = second_codes[:, a * HALF : (a + 1) * HALF]
             dy_scales[1, a] = second_scales[:, a * HALF : (a + 1) * HALF]
         last_sums = keep.tile([P, J], F32, name="last_sums", align_bytes=64)
+        turn_res(6, banks[6])
         add_res_by_transposes(6, banks[6], banks[7])
         fetch_sum(6, last_sums[:, 0:HALF], banks[7])
+        turn_res(7, banks[4])
+        turn_res(5, banks[6])
         scatter(2)
         for k in (3, 4, 5, 7):
             mx_pass(k, 1)

@@ -17,7 +17,6 @@ E5M2 = mybir.dt.float8_e5m2_x4
 E2M1 = mybir.dt.float4_e2m1fn_x4
 ADD = mybir.AluOpType.add
 MULT = mybir.AluOpType.mult
-COPY = mybir.ActivationFunctionType.Copy
 
 P = 128
 HALF = 512
@@ -27,6 +26,7 @@ VECTOR_FIRST = 96
 VECTOR_PIECE = 160
 PRODUCT_BANK = [0, 1, 2, 0, 1, 2, 3, 3]
 LAST_RAW = 8 * T
+SECOND = 10 * T
 TILES = [(0, 0), (1, 0), (2, 0), (0, 1), (1, 1), (2, 1), (3, 0), (3, 1)]
 
 
@@ -77,9 +77,6 @@ def tile_list_embg_mix_resP_kernel(
                 )
 
         nc.gpsimd.memset(w_scales[:].bitcast(U32), 0)
-        gain_rows = keep.tile([P, P], F32, name="gain_rows", align_bytes=64)
-        gain_cols = keep.tile([P, J // P], F32, name="gain_cols", align_bytes=64)
-        nc.gpsimd.memset(gain_rows[:], 0.0)
         warm_in = keep.tile([P, 8], F32, name="warm_in")
         warm_out = keep.tile([P, 8], BF16, name="warm_out")
         nc.vector.memset(warm_in[:], 0.0)
@@ -97,17 +94,16 @@ def tile_list_embg_mix_resP_kernel(
         load_res(0, 0)
         load_res(1, 0)
         load_gain(0)
-        nc.sync.dma_start(out=gain_rows[0 : J // P, :], in_=wgo[0].rearrange("(h q) -> h q", q=P))
         load_dy(1, 1, 0, HALF)
         load_res(2, 0)
         load_dy(1, 0, 0, PIECE)
         load_dy(1, 0, PIECE, HALF, offset=LAST_RAW)
         load_res(3, 0)
-        load_res(3, 1)
+        load_res(1, 1)
         load_res(2, 1)
         load_res(0, 1)
+        load_res(3, 1)
         load_gain(1)
-        load_res(1, 1)
 
         for b in range(2):
             nc.vector.memset(windows[b][:].bitcast(U32), 0)
@@ -164,31 +160,30 @@ def tile_list_embg_mix_resP_kernel(
             nc.vector.tensor_tensor(total, banks[PRODUCT_BANK[k]][:], resid[b, c][:], ADD)
             sums[k] = total
 
-        def turn_res(k, there):
+        def turn_res(k, there, lo=0, hi=HALF):
             b, c = TILES[k]
-            for j0 in range(0, HALF, P):
+            for j0 in range(lo, hi, P):
                 cols = slice(j0, j0 + P)
-                nc.tensor.matmul(there[:, cols], resid[b, c][:, cols], ident[:], start=(j0 == 0), stop=False, is_transpose=True)
+                nc.tensor.matmul(there[:, cols], resid[b, c][:, cols], ident[:], start=(j0 == lo), stop=False, is_transpose=True)
 
-        def add_res_by_transposes(k, there, back):
-            b, c = TILES[k]
+        def turn_product(k, there):
             product = keep.tile([P, HALF], F32, name=f"product{k}", align_bytes=64)
-            turned_sum = keep.tile([P, HALF], F32, name=f"turned_sum{k}", align_bytes=64)
             nc.scalar.copy(out=product[:], in_=banks[PRODUCT_BANK[k]][:])
             for j0 in range(0, HALF, P):
                 cols = slice(j0, j0 + P)
                 nc.tensor.matmul(there[:, cols], product[:, cols], ident[:], start=False, stop=(j0 == HALF - P), is_transpose=True)
-            for j0 in range(0, HALF, P):
-                h = (c * HALF + j0) // P
-                nc.scalar.activation(
-                    turned_sum[:, j0 : j0 + P], there[:, j0 : j0 + P], COPY, scale=gain_cols[:, h : h + 1]
-                )
-            for j0 in range(0, HALF, P):
-                cols = slice(j0, j0 + P)
-                nc.tensor.transpose(back[:, cols], turned_sum[:, cols], ident[:])
 
-        def fetch_sum(k, total, back):
-            nc.scalar.copy(out=total, in_=back[:])
+        def turn_back(k, there, back, lo=0, hi=HALF, offset=None):
+            if offset is None:
+                turned_sum = keep.tile([P, hi - lo], F32, name=f"turned_sum{k}{lo}", align_bytes=64)
+            else:
+                turned_sum = shared.tile([P, hi - lo], F32, name=f"turned_sum{k}{lo}", align_bytes=64, offset=offset)
+            nc.scalar.copy(out=turned_sum[:], in_=there[:, lo:hi])
+            for j0 in range(lo, hi, P):
+                nc.tensor.transpose(back[:, j0 : j0 + P], turned_sum[:, j0 - lo : j0 - lo + P], ident[:])
+
+        def fetch_sum(k, total, back, lo=0, hi=HALF):
+            nc.scalar.copy(out=total, in_=back[:, lo:hi])
             sums[k] = total
 
         def new_sum(k, offset=None):
@@ -198,13 +193,10 @@ def tile_list_embg_mix_resP_kernel(
                 total = shared.tile([P, HALF], F32, name=f"sum{k}", align_bytes=64, offset=offset)
             return total[:]
 
-        def scatter(k):
+        def scatter(k, lo=0, hi=HALF):
             b, c = TILES[k]
-            where = offsets[:, c * HALF // 16 : (c + 1) * HALF // 16]
-            if k in (2, 5):
-                nc.vector.tensor_copy(windows[b][:].indirect(where), sums[k])
-            else:
-                nc.vector.tensor_tensor(windows[b][:].indirect(where), sums[k], gain[:, c * HALF : (c + 1) * HALF], MULT)
+            where = offsets[:, (c * HALF + lo) // 16 : (c * HALF + hi) // 16]
+            nc.vector.tensor_tensor(windows[b][:].indirect(where), sums[k], gain[:, c * HALF + lo : c * HALF + hi], MULT)
 
         def late_window(b, offset):
             windows[b] = shared.tile([P, T], F32, name=f"window{b}", align_bytes=64, offset=offset)
@@ -216,13 +208,12 @@ def tile_list_embg_mix_resP_kernel(
         y_codes = keep.tile([P, 4 * HALF], U32, name="y_codes", align_bytes=64)
         y_scales = keep.tile([P, HALF], U8, name="y_scales", align_bytes=64)
 
-        def store_and_regroup(b, copies, back_copies):
+        def store_and_regroup(b, there, back, copies, back_copies):
             window = windows[b]
             nc.sync.dma_start(out=out_0[P * b : P * (b + 1), :], in_=window[:])
             rounded = keep.tile([P, 4, P, 2], F32, name=f"rounded{b}", align_bytes=64)
-            there, back = (banks[4:], banks[:4]) if b % 2 == 0 else (banks[:4], banks[4:])
             for g in range(4):
-                turned = there[g][:].rearrange("s (q r) -> s q r", q=4)
+                turned = banks[there[g % len(there)]][:].rearrange("s (q r) -> s q r", q=4)
                 for tq in range(4):
                     t0 = HALF * tq + P * g
                     nc.tensor.transpose(turned[:, tq, :], window[:, t0 : t0 + P], ident[:])
@@ -230,12 +221,14 @@ def tile_list_embg_mix_resP_kernel(
                     out=pair_tiles[g][:].bitcast(BF16).rearrange("s (u m e) -> s u m e", u=2, e=2),
                     in_=turned.rearrange("s q (p u e) -> s u (q p) e", u=2, e=2),
                 )
+            share = 4 // len(back_copies)
             for g in range(4):
                 for u in range(2):
-                    cols = slice(P * u, P * (u + 1))
-                    nc.tensor.transpose(back[g][:, cols], pair_tiles[g][:, cols], ident[:])
-            for g in range(4):
-                back_copies[g](out=rounded[:, g, :, :], in_=back[g][:, 0 : 2 * P].rearrange("m (u s) -> m s u", u=2))
+                    col = 2 * P * (g % share) + P * u
+                    nc.tensor.transpose(banks[back[g // share]][:, col : col + P], pair_tiles[g][:, P * u : P * (u + 1)], ident[:])
+            for h, copy in enumerate(back_copies):
+                words = banks[back[h]][:, 0 : 2 * P * share].rearrange("m (g u s) -> m g s u", g=share, u=2)
+                copy(out=rounded[:, share * h : share * (h + 1), :, :], in_=words)
             return rounded
 
         def quantise_out(b, rounded, parts):
@@ -270,23 +263,28 @@ def tile_list_embg_mix_resP_kernel(
         late_window(2, 0)
         for k in range(3):
             mx_pass(k, 0)
-        nc.tensor.transpose(banks[6][:, 0:P], gain_rows[:], ident[:])
-        nc.scalar.copy(out=gain_cols[:], in_=banks[6][:, 0 : J // P])
         turn_res(2, banks[4])
-        add_res_by_transposes(2, banks[4], banks[5])
-        second = keep.tile([P, 2, HALF, 4], BF16, name="second", align_bytes=64)
+        turn_product(2, banks[4])
+        turn_back(2, banks[4], banks[5], 0, PIECE)
+        second = shared.tile([P, 2, HALF, 4], BF16, name="second", align_bytes=64, offset=SECOND)
         for a, lo, hi in ((1, 0, HALF), (0, 0, PIECE), (0, PIECE, HALF)):
             nc.scalar.copy(
                 out=second[:, a, lo:hi, :].rearrange("p (g e) i -> p g i e", e=4),
                 in_=raw[1, a, lo][:].rearrange("p i (g e) -> p g i e", e=4),
             )
-        fetch_sum(2, new_sum(2, LAST_RAW + 2 * HALF), banks[5])
+        early = shared.tile([P, PIECE], F32, name="sum2_early", align_bytes=64, offset=LAST_RAW + 4 * HALF)
+        fetch_sum(2, early[:], banks[5], 0, PIECE)
         mx_pass(6, 1)
         mx_pass(6, 0)
         for k in range(2):
             add_res(k, new_sum(k))
         for k in range(2):
             scatter(k)
+        last_sums = keep.tile([P, J], F32, name="last_sums", align_bytes=64)
+        turn_res(6, banks[6])
+        turn_product(6, banks[6])
+        turn_back(6, banks[6], banks[7])
+        fetch_sum(6, last_sums[:, 0:HALF], banks[7])
         second_codes = keep.tile([P, 2 * HALF], U32, name="second_codes", align_bytes=64)
         second_scales = keep.tile([P, 2 * HALF], U8, name="second_scales", align_bytes=64)
         nc.vector.quantize_mx(
@@ -297,35 +295,35 @@ def tile_list_embg_mix_resP_kernel(
         for a in range(2):
             dy_codes[1, a] = second_codes[:, a * HALF : (a + 1) * HALF]
             dy_scales[1, a] = second_scales[:, a * HALF : (a + 1) * HALF]
-        last_sums = keep.tile([P, J], F32, name="last_sums", align_bytes=64)
-        turn_res(6, banks[6])
-        add_res_by_transposes(6, banks[6], banks[7])
-        fetch_sum(6, last_sums[:, 0:HALF], banks[7])
-        turn_res(7, banks[4])
-        turn_res(5, banks[6])
-        scatter(2)
-        for k in (3, 4, 5, 7):
+        scatter(2, 0, PIECE)
+        mx_pass(3, 1)
+        mx_pass(3, 0)
+        add_res(3, new_sum(3, LAST_RAW))
+        turn_back(2, banks[4], banks[5], PIECE, HALF, offset=SECOND)
+        late = keep.tile([P, PIECE], F32, name="sum2_late", align_bytes=64)
+        fetch_sum(2, late[:], banks[5], PIECE, HALF)
+        scatter(2, PIECE, HALF)
+        for k, there in ((4, banks[6]), (5, banks[7]), (7, banks[4])):
+            turn_res(k, there)
             mx_pass(k, 1)
             mx_pass(k, 0)
-        add_res(3, new_sum(3, LAST_RAW))
-        add_res(4, new_sum(4, LAST_RAW + 4 * HALF))
-        add_res_by_transposes(5, banks[6], banks[7])
-        fetch_sum(5, new_sum(5), banks[7])
-        add_res_by_transposes(7, banks[4], banks[5])
-        fetch_sum(7, last_sums[:, HALF:J], banks[5])
+            turn_product(k, there)
+            turn_back(k, there, banks[PRODUCT_BANK[k]])
+            fetch_sum(k, new_sum(k) if k < 7 else last_sums[:, HALF:J], banks[PRODUCT_BANK[k]])
         on_scalar = [nc.scalar.copy] * 4
         on_s, on_v = nc.scalar.copy, nc.vector.tensor_copy
         regrouped = []
+        plane_banks = [(7, 2), (0, 5), (7, 2), (4, 3, 6, 1), (7, 2, 0, 5)]
         for b in range(3):
             scatter(3 + b)
             if b == 0:
                 late_window(3, LAST_RAW + 2 * HALF - 4 * T)
-            regrouped.append(store_and_regroup(b, on_scalar, on_scalar))
-        nc.vector.tensor_copy(windows[3][:].indirect(offsets[:]), last_sums[:])
+            regrouped.append(store_and_regroup(b, plane_banks[b], plane_banks[b + 1], on_scalar, on_scalar[: len(plane_banks[b + 1])]))
+        nc.vector.tensor_tensor(windows[3][:].indirect(offsets[:]), last_sums[:], gain[:], MULT)
         for b in range(3):
             quantise_out(b, regrouped[b], [(0, HALF)])
         store_codes(0, 3, nc.scalar)
-        quantise_out(3, store_and_regroup(3, [on_s, on_s, on_s, on_v], [on_v, on_s, on_v, on_s]), [(0, 2 * P), (2 * P, HALF)])
+        quantise_out(3, store_and_regroup(3, plane_banks[3], plane_banks[4], [on_s, on_s, on_s, on_v], [on_v, on_s, on_v, on_s]), [(0, 2 * P), (2 * P, HALF)])
         store_codes(3, 4, nc.scalar)
         for tq in range(4):
             (nc.sync if tq < 2 else nc.scalar).dma_start(

@@ -17,6 +17,7 @@ E5M2 = mybir.dt.float8_e5m2_x4
 E2M1 = mybir.dt.float4_e2m1fn_x4
 ADD = mybir.AluOpType.add
 MULT = mybir.AluOpType.mult
+COPY = mybir.ActivationFunctionType.Copy
 
 P = 128
 HALF = 512
@@ -24,9 +25,9 @@ PIECE = 256
 QUAD = 32
 VECTOR_FIRST = 96
 VECTOR_PIECE = 160
-PRODUCT_BANK = [0, 1, 2, 0, 1, 2, 3, 3]
-LAST_RAW = 8 * T
-SECOND = 10 * T
+PRODUCT_BANK = [0, 1, 2, 0, 2, 3, 3, 1]
+LAST_RAW = 4 * T
+SECOND = 6 * T
 TILES = [(0, 0), (1, 0), (2, 0), (0, 1), (1, 1), (2, 1), (3, 0), (3, 1)]
 
 
@@ -62,9 +63,10 @@ def tile_list_embg_mix_resP_kernel(
                 in_=dy[512 * a : 512 * (a + 1), c * HALF + lo : c * HALF + hi].rearrange("(p i) j -> p i j", i=4),
             )
 
-        def load_res(b, c):
-            resid[b, c] = keep.tile([P, HALF], F32, name=f"res{b}{c}", align_bytes=64)
-            nc.sync.dma_start(out=resid[b, c][:], in_=res[P * b : P * (b + 1), c * HALF : (c + 1) * HALF])
+        def load_res(b, c, lo=0, hi=HALF):
+            if lo == 0:
+                resid[b, c] = keep.tile([P, HALF], F32, name=f"res{b}{c}", align_bytes=64)
+            nc.sync.dma_start(out=resid[b, c][:, lo:hi], in_=res[P * b : P * (b + 1), c * HALF + lo : c * HALF + hi])
 
         def load_gain(c):
             nc.sync.dma_start(out=gain[:, c * HALF : (c + 1) * HALF], in_=wgo[:, c * HALF : (c + 1) * HALF])
@@ -77,6 +79,9 @@ def tile_list_embg_mix_resP_kernel(
                 )
 
         nc.gpsimd.memset(w_scales[:].bitcast(U32), 0)
+        gain_rows = keep.tile([P, P], F32, name="gain_rows", align_bytes=64)
+        gain_cols = keep.tile([P, J // P], F32, name="gain_cols", align_bytes=64)
+        nc.gpsimd.memset(gain_rows[:], 0.0)
         warm_in = keep.tile([P, 8], F32, name="warm_in")
         warm_out = keep.tile([P, 8], BF16, name="warm_out")
         nc.vector.memset(warm_in[:], 0.0)
@@ -92,17 +97,20 @@ def tile_list_embg_mix_resP_kernel(
         load_scales(0, w8_scales, nc.sync)
         nc.sync.dma_start(out=w8[:].bitcast(I32), in_=w8_words[0].rearrange("p n i -> p (n i)").bitcast(I32))
         load_res(0, 0)
-        load_res(1, 0)
+        load_res(1, 0, 0, PIECE)
         load_gain(0)
-        load_dy(1, 1, 0, HALF)
+        nc.sync.dma_start(out=gain_rows[0 : J // P, :], in_=wgo[0].rearrange("(h q) -> h q", q=P))
+        load_dy(1, 1, 0, PIECE)
+        load_dy(1, 1, PIECE, HALF)
         load_res(2, 0)
+        load_res(1, 0, PIECE, HALF)
         load_dy(1, 0, 0, PIECE)
         load_dy(1, 0, PIECE, HALF, offset=LAST_RAW)
         load_res(3, 0)
-        load_res(1, 1)
         load_res(2, 1)
-        load_res(0, 1)
         load_res(3, 1)
+        load_res(0, 1)
+        load_res(1, 1)
         load_gain(1)
 
         for b in range(2):
@@ -155,9 +163,9 @@ def tile_list_embg_mix_resP_kernel(
                 stop=(a == 0),
             )
 
-        def add_res(k, total):
+        def add_res(k, total, lo=0, hi=HALF):
             b, c = TILES[k]
-            nc.vector.tensor_tensor(total, banks[PRODUCT_BANK[k]][:], resid[b, c][:], ADD)
+            nc.vector.tensor_tensor(total[:, lo:hi], banks[PRODUCT_BANK[k]][:, lo:hi], resid[b, c][:, lo:hi], ADD)
             sums[k] = total
 
         def turn_res(k, there, lo=0, hi=HALF):
@@ -178,7 +186,11 @@ def tile_list_embg_mix_resP_kernel(
                 turned_sum = keep.tile([P, hi - lo], F32, name=f"turned_sum{k}{lo}", align_bytes=64)
             else:
                 turned_sum = shared.tile([P, hi - lo], F32, name=f"turned_sum{k}{lo}", align_bytes=64, offset=offset)
-            nc.scalar.copy(out=turned_sum[:], in_=there[:, lo:hi])
+            for j0 in range(lo, hi, P):
+                h = (TILES[k][1] * HALF + j0) // P
+                nc.scalar.activation(
+                    turned_sum[:, j0 - lo : j0 - lo + P], there[:, j0 : j0 + P], COPY, scale=gain_cols[:, h : h + 1]
+                )
             for j0 in range(lo, hi, P):
                 nc.tensor.transpose(back[:, j0 : j0 + P], turned_sum[:, j0 - lo : j0 - lo + P], ident[:])
 
@@ -196,7 +208,10 @@ def tile_list_embg_mix_resP_kernel(
         def scatter(k, lo=0, hi=HALF):
             b, c = TILES[k]
             where = offsets[:, (c * HALF + lo) // 16 : (c * HALF + hi) // 16]
-            nc.vector.tensor_tensor(windows[b][:].indirect(where), sums[k], gain[:, c * HALF + lo : c * HALF + hi], MULT)
+            if k in (2, 5):
+                nc.vector.tensor_copy(windows[b][:].indirect(where), sums[k])
+            else:
+                nc.vector.tensor_tensor(windows[b][:].indirect(where), sums[k], gain[:, c * HALF + lo : c * HALF + hi], MULT)
 
         def late_window(b, offset):
             windows[b] = shared.tile([P, T], F32, name=f"window{b}", align_bytes=64, offset=offset)
@@ -263,63 +278,59 @@ def tile_list_embg_mix_resP_kernel(
         late_window(2, 0)
         for k in range(3):
             mx_pass(k, 0)
+        nc.tensor.transpose(banks[6][:, 0:P], gain_rows[:], ident[:])
+        nc.scalar.copy(out=gain_cols[:], in_=banks[6][:, 0 : J // P])
         turn_res(2, banks[4])
         turn_product(2, banks[4])
-        turn_back(2, banks[4], banks[5], 0, PIECE)
-        second = shared.tile([P, 2, HALF, 4], BF16, name="second", align_bytes=64, offset=SECOND)
-        for a, lo, hi in ((1, 0, HALF), (0, 0, PIECE), (0, PIECE, HALF)):
-            nc.scalar.copy(
-                out=second[:, a, lo:hi, :].rearrange("p (g e) i -> p g i e", e=4),
-                in_=raw[1, a, lo][:].rearrange("p i (g e) -> p g i e", e=4),
-            )
-        early = shared.tile([P, PIECE], F32, name="sum2_early", align_bytes=64, offset=LAST_RAW + 4 * HALF)
-        fetch_sum(2, early[:], banks[5], 0, PIECE)
+        turn_back(2, banks[4], banks[5])
         mx_pass(6, 1)
         mx_pass(6, 0)
-        for k in range(2):
-            add_res(k, new_sum(k))
-        for k in range(2):
-            scatter(k)
+
+        def round_second(a, tile):
+            grouped[1, a, 0] = tile
+            for lo in (0, PIECE):
+                nc.scalar.copy(
+                    out=tile[:, lo : lo + PIECE, :].rearrange("p (g e) i -> p g i e", e=4),
+                    in_=raw[1, a, lo][:].rearrange("p i (g e) -> p g i e", e=4),
+                )
+
+        round_second(1, keep.tile([P, HALF, 4], BF16, name="second1", align_bytes=64))
+        round_second(0, shared.tile([P, HALF, 4], BF16, name="second0", align_bytes=64, offset=SECOND))
+        fetch_sum(2, new_sum(2, LAST_RAW), banks[5])
+        add_res(0, new_sum(0))
+        add_res(1, new_sum(1), 0, PIECE)
+        scatter(0)
+        add_res(1, sums[1], PIECE, HALF)
+        quantise_dy(1, 1, 0, HALF)
+        scatter(1)
         last_sums = keep.tile([P, J], F32, name="last_sums", align_bytes=64)
         turn_res(6, banks[6])
         turn_product(6, banks[6])
         turn_back(6, banks[6], banks[7])
         fetch_sum(6, last_sums[:, 0:HALF], banks[7])
-        second_codes = keep.tile([P, 2 * HALF], U32, name="second_codes", align_bytes=64)
-        second_scales = keep.tile([P, 2 * HALF], U8, name="second_scales", align_bytes=64)
-        nc.vector.quantize_mx(
-            out=second_codes[:].bitcast(E5M2),
-            scales=second_scales[:],
-            in_=second[:].rearrange("p a j i -> p (a j i)"),
-        )
-        for a in range(2):
-            dy_codes[1, a] = second_codes[:, a * HALF : (a + 1) * HALF]
-            dy_scales[1, a] = second_scales[:, a * HALF : (a + 1) * HALF]
-        scatter(2, 0, PIECE)
-        mx_pass(3, 1)
-        mx_pass(3, 0)
-        add_res(3, new_sum(3, LAST_RAW))
-        turn_back(2, banks[4], banks[5], PIECE, HALF, offset=SECOND)
-        late = keep.tile([P, PIECE], F32, name="sum2_late", align_bytes=64)
-        fetch_sum(2, late[:], banks[5], PIECE, HALF)
-        scatter(2, PIECE, HALF)
-        for k, there in ((4, banks[6]), (5, banks[7]), (7, banks[4])):
-            turn_res(k, there)
+        for k in (3, 4, 5, 7):
             mx_pass(k, 1)
+        turn_res(5, banks[4])
+        turn_res(7, banks[5])
+        quantise_dy(1, 0, 0, HALF)
+        late_window(3, SECOND)
+        scatter(2)
+        for k in (3, 4):
+            mx_pass(k, 0)
+            add_res(k, new_sum(k))
+        for k, there in ((5, banks[4]), (7, banks[5])):
             mx_pass(k, 0)
             turn_product(k, there)
             turn_back(k, there, banks[PRODUCT_BANK[k]])
-            fetch_sum(k, new_sum(k) if k < 7 else last_sums[:, HALF:J], banks[PRODUCT_BANK[k]])
+            fetch_sum(k, new_sum(k) if k < 7 else last_sums[:, HALF:], banks[PRODUCT_BANK[k]])
         on_scalar = [nc.scalar.copy] * 4
         on_s, on_v = nc.scalar.copy, nc.vector.tensor_copy
         regrouped = []
-        plane_banks = [(7, 2), (0, 5), (7, 2), (4, 3, 6, 1), (7, 2, 0, 5)]
+        plane_banks = [(5, 1), (0, 2, 3, 4), (5, 1, 6, 7), (0, 2, 3, 4), (5, 1, 6, 7)]
         for b in range(3):
             scatter(3 + b)
-            if b == 0:
-                late_window(3, LAST_RAW + 2 * HALF - 4 * T)
             regrouped.append(store_and_regroup(b, plane_banks[b], plane_banks[b + 1], on_scalar, on_scalar[: len(plane_banks[b + 1])]))
-        nc.vector.tensor_tensor(windows[3][:].indirect(offsets[:]), last_sums[:], gain[:], MULT)
+        nc.vector.tensor_copy(windows[3][:].indirect(offsets[:]), last_sums[:])
         for b in range(3):
             quantise_out(b, regrouped[b], [(0, HALF)])
         store_codes(0, 3, nc.scalar)

@@ -92,8 +92,8 @@ def tile_list_embg_mix_resP_kernel(
         load_scales(1, w4_scales, nc.sync)
         nc.sync.dma_start(out=w4[:].bitcast(I32), in_=w4_words[0].bitcast(I32))
         load_dy(0, 1, PIECE, HALF)
-        load_dy(0, 0, 0, PIECE)
-        load_dy(0, 0, PIECE, HALF)
+        load_dy(0, 0, 0, HALF - P)
+        load_dy(0, 0, HALF - P, HALF)
         load_scales(0, w8_scales, nc.sync)
         nc.sync.dma_start(out=w8[:].bitcast(I32), in_=w8_words[0].rearrange("p n i -> p (n i)").bitcast(I32))
         load_res(0, 0)
@@ -107,11 +107,11 @@ def tile_list_embg_mix_resP_kernel(
         load_dy(1, 0, 0, PIECE)
         load_dy(1, 0, PIECE, HALF, offset=LAST_RAW)
         load_res(3, 0)
-        load_res(2, 1)
-        load_res(3, 1)
-        load_res(0, 1)
         load_res(1, 1)
+        load_res(0, 1)
+        load_res(2, 1)
         load_gain(1)
+        load_res(3, 1)
 
         for b in range(2):
             nc.vector.memset(windows[b][:].bitcast(U32), 0)
@@ -147,7 +147,7 @@ def tile_list_embg_mix_resP_kernel(
 
         sums = {}
 
-        def mx_pass(k, a):
+        def mx_pass(k, a, first=1):
             b, c = TILES[k]
             if a == 0:
                 words = w8[:, P * b : P * (b + 1)].bitcast(E4M3)
@@ -159,8 +159,8 @@ def tile_list_embg_mix_resP_kernel(
                 lhsT_scale=w_scales[:, a * N + P * b : a * N + P * (b + 1)],
                 rhs=dy_codes[c, a][:].bitcast(E5M2),
                 rhs_scale=dy_scales[c, a][:],
-                start=(a == 1),
-                stop=(a == 0),
+                start=(a == first),
+                stop=(a != first),
             )
 
         def add_res(k, total, lo=0, hi=HALF):
@@ -208,7 +208,7 @@ def tile_list_embg_mix_resP_kernel(
         def scatter(k, lo=0, hi=HALF):
             b, c = TILES[k]
             where = offsets[:, (c * HALF + lo) // 16 : (c * HALF + hi) // 16]
-            if k in (2, 5):
+            if k in (2, 4, 5):
                 nc.vector.tensor_copy(windows[b][:].indirect(where), sums[k])
             else:
                 nc.vector.tensor_tensor(windows[b][:].indirect(where), sums[k], gain[:, c * HALF + lo : c * HALF + hi], MULT)
@@ -271,8 +271,15 @@ def tile_list_embg_mix_resP_kernel(
         quantise_dy(0, 1, PIECE, HALF)
         for k in range(3):
             mx_pass(k, 1)
-        round_dy(0, 0, 0, PIECE, VECTOR_PIECE)
-        round_dy(0, 0, PIECE, HALF, VECTOR_PIECE, offset=0)
+        front = keep.tile([P, PIECE, 4], BF16, name="front", align_bytes=64)
+        rear = shared.tile([P, PIECE, 4], BF16, name="rear", align_bytes=64, offset=0)
+        grouped[0, 0, 0], grouped[0, 0, PIECE] = front, rear
+        for copy, dst, src in (
+            (nc.vector.tensor_copy, front[:], raw[0, 0, 0][:, :, 0:PIECE]),
+            (nc.scalar.copy, rear[:, 0:P, :], raw[0, 0, 0][:, :, PIECE : HALF - P]),
+            (nc.scalar.copy, rear[:, P:PIECE, :], raw[0, 0, HALF - P][:]),
+        ):
+            copy(out=dst.rearrange("p (g e) i -> p g i e", e=4), in_=src.rearrange("p i (g e) -> p g i e", e=4))
         quantise_dy(0, 0, 0, PIECE)
         quantise_dy(0, 0, PIECE, HALF)
         late_window(2, 0)
@@ -283,8 +290,8 @@ def tile_list_embg_mix_resP_kernel(
         turn_res(2, banks[4])
         turn_product(2, banks[4])
         turn_back(2, banks[4], banks[5])
-        mx_pass(6, 1)
-        mx_pass(6, 0)
+        mx_pass(6, 0, first=0)
+        mx_pass(6, 1, first=0)
 
         def round_second(a, tile):
             grouped[1, a, 0] = tile
@@ -296,7 +303,8 @@ def tile_list_embg_mix_resP_kernel(
 
         round_second(1, keep.tile([P, HALF, 4], BF16, name="second1", align_bytes=64))
         round_second(0, shared.tile([P, HALF, 4], BF16, name="second0", align_bytes=64, offset=SECOND))
-        fetch_sum(2, new_sum(2, LAST_RAW), banks[5])
+        early = shared.tile([P, PIECE], F32, name="sum2_early", align_bytes=64, offset=LAST_RAW)
+        fetch_sum(2, early[:], banks[5], 0, PIECE)
         add_res(0, new_sum(0))
         add_res(1, new_sum(1), 0, PIECE)
         scatter(0)
@@ -310,15 +318,18 @@ def tile_list_embg_mix_resP_kernel(
         fetch_sum(6, last_sums[:, 0:HALF], banks[7])
         for k in (3, 4, 5, 7):
             mx_pass(k, 1)
-        turn_res(5, banks[4])
-        turn_res(7, banks[5])
+        turn_res(4, banks[4])
         quantise_dy(1, 0, 0, HALF)
-        late_window(3, SECOND)
-        scatter(2)
-        for k in (3, 4):
-            mx_pass(k, 0)
-            add_res(k, new_sum(k))
-        for k, there in ((5, banks[4]), (7, banks[5])):
+        late_window(3, SECOND + T)
+        scatter(2, 0, PIECE)
+        mx_pass(3, 0)
+        add_res(3, new_sum(3))
+        late = shared.tile([P, PIECE], F32, name="sum2_late", align_bytes=64, offset=SECOND)
+        fetch_sum(2, late[:], banks[5], PIECE, HALF)
+        scatter(2, PIECE, HALF)
+        for k, there in ((4, banks[4]), (5, banks[6]), (7, banks[5])):
+            if k > 4:
+                turn_res(k, there)
             mx_pass(k, 0)
             turn_product(k, there)
             turn_back(k, there, banks[PRODUCT_BANK[k]])

@@ -23,12 +23,19 @@ P = 128
 HALF = 512
 PIECE = 256
 QUAD = 32
-VECTOR_FIRST = 96
-VECTOR_PIECE = 160
-PRODUCT_BANK = [0, 1, 2, 0, 2, 3, 3, 1]
-LAST_RAW = 4 * T
-SECOND = 6 * T
+VECTOR_COLUMNS = 96
+
 TILES = [(0, 0), (1, 0), (2, 0), (0, 1), (1, 1), (2, 1), (3, 0), (3, 1)]
+ADDED_BY_VECTOR = (0, 1, 3)
+PRODUCT_BANK = [0, 1, 2, 0, 2, 3, 3, 1]
+SUM_BANK = {2: 4, 6: 6, 4: 4, 5: 6, 7: 5}
+RETURN_BANK = {2: 5, 6: 7, 4: 2, 5: 3, 7: 1}
+PLANE_BANKS = [(6, 3, 5, 1), (0, 2, 4, 7)]
+
+HEAD_REAR = 0
+LAST_RAW = 4 * T
+SECOND_ROUNDED = 6 * T
+LAST_WINDOW = 7 * T
 
 
 def tile_list_embg_mix_resP_kernel(
@@ -71,9 +78,9 @@ def tile_list_embg_mix_resP_kernel(
         def load_gain(c):
             nc.sync.dma_start(out=gain[:, c * HALF : (c + 1) * HALF], in_=wgo[:, c * HALF : (c + 1) * HALF])
 
-        def load_scales(a, source, queue):
+        def load_scales(a, source):
             for q in range(4):
-                queue.dma_start(
+                nc.sync.dma_start(
                     out=w_scales[QUAD * q : QUAD * q + 4, a * N : (a + 1) * N].bitcast(I32),
                     in_=source[0][4 * q : 4 * q + 4, :].bitcast(I32),
                 )
@@ -89,12 +96,12 @@ def tile_list_embg_mix_resP_kernel(
 
         nc.sync.dma_start(offsets[:], offs)
         load_dy(0, 1, 0, PIECE)
-        load_scales(1, w4_scales, nc.sync)
+        load_scales(1, w4_scales)
         nc.sync.dma_start(out=w4[:].bitcast(I32), in_=w4_words[0].bitcast(I32))
         load_dy(0, 1, PIECE, HALF)
         load_dy(0, 0, 0, HALF - P)
         load_dy(0, 0, HALF - P, HALF)
-        load_scales(0, w8_scales, nc.sync)
+        load_scales(0, w8_scales)
         nc.sync.dma_start(out=w8[:].bitcast(I32), in_=w8_words[0].rearrange("p n i -> p (n i)").bitcast(I32))
         load_res(0, 0)
         load_res(1, 0, 0, PIECE)
@@ -117,23 +124,19 @@ def tile_list_embg_mix_resP_kernel(
             nc.vector.memset(windows[b][:].bitcast(U32), 0)
         make_identity(nc, ident[:])
 
+        def clear_window(b, offset):
+            windows[b] = shared.tile([P, T], F32, name=f"window{b}", align_bytes=64, offset=offset)
+            nc.gpsimd.memset(windows[b][:].bitcast(U32), 0)
+
         grouped = {}
         dy_codes = {}
         dy_scales = {}
 
-        def round_dy(c, a, lo, hi, vector_cols, offset=None):
-            key = (c, a, lo)
-            name = f"grouped{c}{a}{lo}"
-            if offset is None:
-                grouped[key] = keep.tile([P, hi - lo, 4], BF16, name=name, align_bytes=64)
-            else:
-                grouped[key] = shared.tile([P, hi - lo, 4], BF16, name=name, align_bytes=64, offset=offset)
-            for copy, x, y in ((nc.scalar.copy, vector_cols, hi - lo), (nc.vector.tensor_copy, 0, vector_cols)):
-                if y > x:
-                    copy(
-                        out=grouped[key][:, x:y, :].rearrange("p (g e) i -> p g i e", e=4),
-                        in_=raw[key][:, :, x:y].rearrange("p i (g e) -> p g i e", e=4),
-                    )
+        def round_dy(copy, columns, rows):
+            copy(
+                out=columns.rearrange("p (g e) i -> p g i e", e=4),
+                in_=rows.rearrange("p i (g e) -> p g i e", e=4),
+            )
 
         def quantise_dy(c, a, lo, hi):
             if lo == 0:
@@ -145,7 +148,7 @@ def tile_list_embg_mix_resP_kernel(
                 in_=grouped[c, a, lo][:].rearrange("p j i -> p (j i)"),
             )
 
-        sums = {}
+        values = {}
 
         def mx_pass(k, a, first=1):
             b, c = TILES[k]
@@ -163,59 +166,50 @@ def tile_list_embg_mix_resP_kernel(
                 stop=(a != first),
             )
 
-        def add_res(k, total, lo=0, hi=HALF):
-            b, c = TILES[k]
-            nc.vector.tensor_tensor(total[:, lo:hi], banks[PRODUCT_BANK[k]][:, lo:hi], resid[b, c][:, lo:hi], ADD)
-            sums[k] = total
+        def new_values(k):
+            return keep.tile([P, HALF], F32, name=f"sum{k}", align_bytes=64)[:]
 
-        def turn_res(k, there, lo=0, hi=HALF):
-            b, c = TILES[k]
-            for j0 in range(lo, hi, P):
-                cols = slice(j0, j0 + P)
-                nc.tensor.matmul(there[:, cols], resid[b, c][:, cols], ident[:], start=(j0 == lo), stop=False, is_transpose=True)
+        def add_res(k, lo=0, hi=HALF):
+            if lo == 0:
+                values[k] = new_values(k)
+            product, rows = banks[PRODUCT_BANK[k]], resid[TILES[k]]
+            nc.vector.tensor_tensor(values[k][:, lo:hi], product[:, lo:hi], rows[:, lo:hi], ADD)
 
-        def turn_product(k, there):
-            product = keep.tile([P, HALF], F32, name=f"product{k}", align_bytes=64)
-            nc.scalar.copy(out=product[:], in_=banks[PRODUCT_BANK[k]][:])
+        def turn_into_sum(k, source, opens):
             for j0 in range(0, HALF, P):
                 cols = slice(j0, j0 + P)
-                nc.tensor.matmul(there[:, cols], product[:, cols], ident[:], start=False, stop=(j0 == HALF - P), is_transpose=True)
-
-        def turn_back(k, there, back, lo=0, hi=HALF, offset=None):
-            if offset is None:
-                turned_sum = keep.tile([P, hi - lo], F32, name=f"turned_sum{k}{lo}", align_bytes=64)
-            else:
-                turned_sum = shared.tile([P, hi - lo], F32, name=f"turned_sum{k}{lo}", align_bytes=64, offset=offset)
-            for j0 in range(lo, hi, P):
-                h = (TILES[k][1] * HALF + j0) // P
-                nc.scalar.activation(
-                    turned_sum[:, j0 - lo : j0 - lo + P], there[:, j0 : j0 + P], COPY, scale=gain_cols[:, h : h + 1]
+                start, stop = opens and j0 == 0, not opens and j0 == HALF - P
+                nc.tensor.matmul(
+                    banks[SUM_BANK[k]][:, cols], source[:, cols], ident[:], start=start, stop=stop, is_transpose=True
                 )
-            for j0 in range(lo, hi, P):
-                nc.tensor.transpose(back[:, j0 : j0 + P], turned_sum[:, j0 - lo : j0 - lo + P], ident[:])
 
-        def fetch_sum(k, total, back, lo=0, hi=HALF):
-            nc.scalar.copy(out=total, in_=back[:, lo:hi])
-            sums[k] = total
+        def turn_res(k):
+            turn_into_sum(k, resid[TILES[k]], opens=True)
 
-        def new_sum(k, offset=None):
-            if offset is None:
-                total = keep.tile([P, HALF], F32, name=f"sum{k}", align_bytes=64)
-            else:
-                total = shared.tile([P, HALF], F32, name=f"sum{k}", align_bytes=64, offset=offset)
-            return total[:]
+        def turn_product_and_back(k):
+            product = keep.tile([P, HALF], F32, name=f"product{k}", align_bytes=64)
+            nc.scalar.copy(out=product[:], in_=banks[PRODUCT_BANK[k]][:])
+            turn_into_sum(k, product, opens=False)
+            turned_sum = keep.tile([P, HALF], F32, name=f"turned_sum{k}", align_bytes=64)
+            for j0 in range(0, HALF, P):
+                h = (TILES[k][1] * HALF + j0) // P
+                cols = slice(j0, j0 + P)
+                nc.scalar.activation(turned_sum[:, cols], banks[SUM_BANK[k]][:, cols], COPY, scale=gain_cols[:, h : h + 1])
+            for j0 in range(0, HALF, P):
+                cols = slice(j0, j0 + P)
+                nc.tensor.transpose(banks[RETURN_BANK[k]][:, cols], turned_sum[:, cols], ident[:])
+
+        def fetch_values(k, target, lo=0, hi=HALF):
+            nc.scalar.copy(out=target, in_=banks[RETURN_BANK[k]][:, lo:hi])
+            values[k] = target
 
         def scatter(k, lo=0, hi=HALF):
             b, c = TILES[k]
-            where = offsets[:, (c * HALF + lo) // 16 : (c * HALF + hi) // 16]
-            if k in (2, 4, 5):
-                nc.vector.tensor_copy(windows[b][:].indirect(where), sums[k])
+            places = windows[b][:].indirect(offsets[:, (c * HALF + lo) // 16 : (c * HALF + hi) // 16])
+            if k in ADDED_BY_VECTOR:
+                nc.vector.tensor_tensor(places, values[k], gain[:, c * HALF + lo : c * HALF + hi], MULT)
             else:
-                nc.vector.tensor_tensor(windows[b][:].indirect(where), sums[k], gain[:, c * HALF + lo : c * HALF + hi], MULT)
-
-        def late_window(b, offset):
-            windows[b] = shared.tile([P, T], F32, name=f"window{b}", align_bytes=64, offset=offset)
-            nc.gpsimd.memset(windows[b][:].bitcast(U32), 0)
+                nc.vector.tensor_copy(places, values[k])
 
         words_out = out_1[0].rearrange("p t i -> p (t i)").bitcast(I32)
         scales_out = out_2[0].bitcast(I32)
@@ -223,132 +217,132 @@ def tile_list_embg_mix_resP_kernel(
         y_codes = keep.tile([P, 4 * HALF], U32, name="y_codes", align_bytes=64)
         y_scales = keep.tile([P, HALF], U8, name="y_scales", align_bytes=64)
 
-        def store_and_regroup(b, there, back, copies, back_copies):
+        def store_and_regroup(b, first_copies, second_copies):
             window = windows[b]
+            first_banks, second_banks = PLANE_BANKS[b % 2], PLANE_BANKS[1 - b % 2]
             nc.sync.dma_start(out=out_0[P * b : P * (b + 1), :], in_=window[:])
             rounded = keep.tile([P, 4, P, 2], F32, name=f"rounded{b}", align_bytes=64)
             for g in range(4):
-                turned = banks[there[g % len(there)]][:].rearrange("s (q r) -> s q r", q=4)
+                turned = banks[first_banks[g]][:].rearrange("s (q r) -> s q r", q=4)
                 for tq in range(4):
                     t0 = HALF * tq + P * g
                     nc.tensor.transpose(turned[:, tq, :], window[:, t0 : t0 + P], ident[:])
-                copies[g](
+                first_copies[g](
                     out=pair_tiles[g][:].bitcast(BF16).rearrange("s (u m e) -> s u m e", u=2, e=2),
                     in_=turned.rearrange("s q (p u e) -> s u (q p) e", u=2, e=2),
                 )
-            share = 4 // len(back_copies)
             for g in range(4):
                 for u in range(2):
-                    col = 2 * P * (g % share) + P * u
-                    nc.tensor.transpose(banks[back[g // share]][:, col : col + P], pair_tiles[g][:, P * u : P * (u + 1)], ident[:])
-            for h, copy in enumerate(back_copies):
-                words = banks[back[h]][:, 0 : 2 * P * share].rearrange("m (g u s) -> m g s u", g=share, u=2)
-                copy(out=rounded[:, share * h : share * (h + 1), :, :], in_=words)
+                    cols = slice(P * u, P * (u + 1))
+                    nc.tensor.transpose(banks[second_banks[g]][:, cols], pair_tiles[g][:, cols], ident[:])
+            for g in range(4):
+                words = banks[second_banks[g]][:, 0 : 2 * P].rearrange("m (g u s) -> m g s u", g=1, u=2)
+                second_copies[g](out=rounded[:, g : g + 1, :, :], in_=words)
             return rounded
 
-        def quantise_out(b, rounded, parts):
+        def quantise_out(b, rounded, lo, hi):
             flat = rounded[:].rearrange("m g s u -> m (g s u)").bitcast(BF16)
-            base = HALF * b
-            for lo, hi in parts:
-                nc.vector.quantize_mx(
-                    out=y_codes[:, base + lo : base + hi].bitcast(E4M3),
-                    scales=y_scales[4 * b : P, lo:hi],
-                    in_=flat[:, 4 * lo : 4 * hi],
-                )
+            nc.vector.quantize_mx(
+                out=y_codes[:, HALF * b + lo : HALF * b + hi].bitcast(E4M3),
+                scales=y_scales[4 * b : P, lo:hi],
+                in_=flat[:, 4 * lo : 4 * hi],
+            )
 
-        def store_codes(b0, b1, upper_queue):
+        def queue_of(tq):
+            return nc.sync if tq < 2 else nc.scalar
+
+        def store_codes(b0, b1):
             rows = words_out[QUAD * b0 : QUAD * b1, :].rearrange("(d p) t -> p d t", p=QUAD)
             for tq in (0, 2, 1, 3):
                 quarter = y_codes[QUAD * tq : QUAD * (tq + 1), HALF * b0 : HALF * b1].bitcast(I32)
-                (nc.sync if tq < 2 else upper_queue).dma_start(
+                queue_of(tq).dma_start(
                     out=rows[:, :, HALF * tq : HALF * (tq + 1)],
                     in_=quarter.rearrange("p (d s) -> p d s", s=HALF),
                 )
 
-        round_dy(0, 1, 0, PIECE, 0)
-        round_dy(0, 1, PIECE, HALF, VECTOR_FIRST)
-        quantise_dy(0, 1, 0, PIECE)
-        quantise_dy(0, 1, PIECE, HALF)
+        on_scalar, on_vector = nc.scalar.copy, nc.vector.tensor_copy
+
+        for lo in (0, PIECE):
+            grouped[0, 1, lo] = keep.tile([P, PIECE, 4], BF16, name=f"grouped01{lo}", align_bytes=64)
+            split = 0 if lo == 0 else VECTOR_COLUMNS
+            round_dy(on_scalar, grouped[0, 1, lo][:, split:PIECE, :], raw[0, 1, lo][:, :, split:PIECE])
+            if split:
+                round_dy(on_vector, grouped[0, 1, lo][:, 0:split, :], raw[0, 1, lo][:, :, 0:split])
+        for lo in (0, PIECE):
+            quantise_dy(0, 1, lo, lo + PIECE)
         for k in range(3):
             mx_pass(k, 1)
         front = keep.tile([P, PIECE, 4], BF16, name="front", align_bytes=64)
-        rear = shared.tile([P, PIECE, 4], BF16, name="rear", align_bytes=64, offset=0)
+        rear = shared.tile([P, PIECE, 4], BF16, name="rear", align_bytes=64, offset=HEAD_REAR)
         grouped[0, 0, 0], grouped[0, 0, PIECE] = front, rear
-        for copy, dst, src in (
-            (nc.vector.tensor_copy, front[:], raw[0, 0, 0][:, :, 0:PIECE]),
-            (nc.scalar.copy, rear[:, 0:P, :], raw[0, 0, 0][:, :, PIECE : HALF - P]),
-            (nc.scalar.copy, rear[:, P:PIECE, :], raw[0, 0, HALF - P][:]),
-        ):
-            copy(out=dst.rearrange("p (g e) i -> p g i e", e=4), in_=src.rearrange("p i (g e) -> p g i e", e=4))
-        quantise_dy(0, 0, 0, PIECE)
-        quantise_dy(0, 0, PIECE, HALF)
-        late_window(2, 0)
+        round_dy(on_vector, front[:], raw[0, 0, 0][:, :, 0:PIECE])
+        round_dy(on_scalar, rear[:, 0:P, :], raw[0, 0, 0][:, :, PIECE : HALF - P])
+        round_dy(on_scalar, rear[:, P:PIECE, :], raw[0, 0, HALF - P][:])
+        for lo in (0, PIECE):
+            quantise_dy(0, 0, lo, lo + PIECE)
+        clear_window(2, HEAD_REAR)
         for k in range(3):
             mx_pass(k, 0)
-        nc.tensor.transpose(banks[6][:, 0:P], gain_rows[:], ident[:])
-        nc.scalar.copy(out=gain_cols[:], in_=banks[6][:, 0 : J // P])
-        turn_res(2, banks[4])
-        turn_product(2, banks[4])
-        turn_back(2, banks[4], banks[5])
+        nc.tensor.transpose(banks[SUM_BANK[6]][:, 0:P], gain_rows[:], ident[:])
+        nc.scalar.copy(out=gain_cols[:], in_=banks[SUM_BANK[6]][:, 0 : J // P])
+        turn_res(2)
+        turn_product_and_back(2)
         mx_pass(6, 0, first=0)
         mx_pass(6, 1, first=0)
 
-        def round_second(a, tile):
-            grouped[1, a, 0] = tile
-            for lo in (0, PIECE):
-                nc.scalar.copy(
-                    out=tile[:, lo : lo + PIECE, :].rearrange("p (g e) i -> p g i e", e=4),
-                    in_=raw[1, a, lo][:].rearrange("p i (g e) -> p g i e", e=4),
-                )
-
-        round_second(1, keep.tile([P, HALF, 4], BF16, name="second1", align_bytes=64))
-        round_second(0, shared.tile([P, HALF, 4], BF16, name="second0", align_bytes=64, offset=SECOND))
+        grouped[1, 1, 0] = keep.tile([P, HALF, 4], BF16, name="second1", align_bytes=64)
+        for lo in (0, PIECE):
+            round_dy(on_scalar, grouped[1, 1, 0][:, lo : lo + PIECE, :], raw[1, 1, lo][:])
+        grouped[1, 0, 0] = shared.tile([P, HALF, 4], BF16, name="second0", align_bytes=64, offset=SECOND_ROUNDED)
+        for lo in (0, PIECE):
+            round_dy(on_scalar, grouped[1, 0, 0][:, lo : lo + PIECE, :], raw[1, 0, lo][:])
         early = shared.tile([P, PIECE], F32, name="sum2_early", align_bytes=64, offset=LAST_RAW)
-        fetch_sum(2, early[:], banks[5], 0, PIECE)
-        add_res(0, new_sum(0))
-        add_res(1, new_sum(1), 0, PIECE)
+        fetch_values(2, early[:], 0, PIECE)
+        add_res(0)
+        add_res(1, 0, PIECE)
         scatter(0)
-        add_res(1, sums[1], PIECE, HALF)
+        add_res(1, PIECE, HALF)
         quantise_dy(1, 1, 0, HALF)
         scatter(1)
-        last_sums = keep.tile([P, J], F32, name="last_sums", align_bytes=64)
-        turn_res(6, banks[6])
-        turn_product(6, banks[6])
-        turn_back(6, banks[6], banks[7])
-        fetch_sum(6, last_sums[:, 0:HALF], banks[7])
+        last_values = keep.tile([P, J], F32, name="last_sums", align_bytes=64)
+        turn_res(6)
+        turn_product_and_back(6)
+        fetch_values(6, last_values[:, 0:HALF])
         for k in (3, 4, 5, 7):
             mx_pass(k, 1)
-        turn_res(4, banks[4])
+        turn_res(4)
+
         quantise_dy(1, 0, 0, HALF)
-        late_window(3, SECOND + T)
+        clear_window(3, LAST_WINDOW)
         scatter(2, 0, PIECE)
         mx_pass(3, 0)
-        add_res(3, new_sum(3))
-        late = shared.tile([P, PIECE], F32, name="sum2_late", align_bytes=64, offset=SECOND)
-        fetch_sum(2, late[:], banks[5], PIECE, HALF)
+        add_res(3)
+        late = shared.tile([P, PIECE], F32, name="sum2_late", align_bytes=64, offset=SECOND_ROUNDED)
+        fetch_values(2, late[:], PIECE, HALF)
         scatter(2, PIECE, HALF)
-        for k, there in ((4, banks[4]), (5, banks[6]), (7, banks[5])):
-            if k > 4:
-                turn_res(k, there)
+        mx_pass(4, 0)
+        turn_product_and_back(4)
+        fetch_values(4, new_values(4))
+        for k in (5, 7):
+            turn_res(k)
             mx_pass(k, 0)
-            turn_product(k, there)
-            turn_back(k, there, banks[PRODUCT_BANK[k]])
-            fetch_sum(k, new_sum(k) if k < 7 else last_sums[:, HALF:], banks[PRODUCT_BANK[k]])
-        on_scalar = [nc.scalar.copy] * 4
-        on_s, on_v = nc.scalar.copy, nc.vector.tensor_copy
+            turn_product_and_back(k)
+            fetch_values(k, new_values(k) if k == 5 else last_values[:, HALF:J])
+
         regrouped = []
-        plane_banks = [(5, 1), (0, 2, 3, 4), (5, 1, 6, 7), (0, 2, 3, 4), (5, 1, 6, 7)]
         for b in range(3):
             scatter(3 + b)
-            regrouped.append(store_and_regroup(b, plane_banks[b], plane_banks[b + 1], on_scalar, on_scalar[: len(plane_banks[b + 1])]))
-        nc.vector.tensor_copy(windows[3][:].indirect(offsets[:]), last_sums[:])
+            regrouped.append(store_and_regroup(b, [on_scalar] * 4, [on_scalar] * 4))
+        nc.vector.tensor_copy(windows[3][:].indirect(offsets[:]), last_values[:])
         for b in range(3):
-            quantise_out(b, regrouped[b], [(0, HALF)])
-        store_codes(0, 3, nc.scalar)
-        quantise_out(3, store_and_regroup(3, plane_banks[3], plane_banks[4], [on_s, on_s, on_s, on_v], [on_v, on_s, on_v, on_s]), [(0, 2 * P), (2 * P, HALF)])
-        store_codes(3, 4, nc.scalar)
+            quantise_out(b, regrouped[b], 0, HALF)
+        store_codes(0, 3)
+        last = store_and_regroup(3, [on_scalar] * 3 + [on_vector], [on_vector, on_scalar] * 2)
+        for lo in (0, PIECE):
+            quantise_out(3, last, lo, lo + PIECE)
+        store_codes(3, 4)
         for tq in range(4):
-            (nc.sync if tq < 2 else nc.scalar).dma_start(
+            queue_of(tq).dma_start(
                 out=scales_out[:, P * tq : P * (tq + 1)],
                 in_=y_scales[QUAD * tq : QUAD * tq + 16, :].bitcast(I32),
             )

@@ -20,22 +20,20 @@ MULT = mybir.AluOpType.mult
 COPY = mybir.ActivationFunctionType.Copy
 
 P = 128
-HALF = 512
-PIECE = 256
+BANK = 512
+CHUNK = 256
 QUAD = 32
-VECTOR_COLUMNS = 96
+VECTOR_COLUMNS = 160
 
-TILES = [(0, 0), (1, 0), (2, 0), (0, 1), (1, 1), (2, 1), (3, 0), (3, 1)]
-ADDED_BY_VECTOR = (0, 1, 3)
-PRODUCT_BANK = [0, 1, 2, 0, 2, 3, 3, 1]
-SUM_BANK = {2: 4, 6: 6, 4: 4, 5: 6, 7: 5}
-RETURN_BANK = {2: 5, 6: 7, 4: 2, 5: 3, 7: 1}
-PLANE_BANKS = [(6, 3, 5, 1), (0, 2, 4, 7)]
+PLANE_BANKS = [(5, 2, 7, 1), (0, 3, 4, 6)]
 
-HEAD_REAR = 0
-LAST_RAW = 4 * T
-SECOND_ROUNDED = 6 * T
-LAST_WINDOW = 7 * T
+KIB = 1024
+HEAD_ROUNDED = 7 * KIB
+ROUNDED_1 = 16 * KIB
+RAW_10 = 24 * KIB
+RAW_30 = 40 * KIB
+RAW_31 = 44 * KIB
+RAW_20 = 32 * KIB
 
 
 def tile_list_embg_mix_resP_kernel(
@@ -46,37 +44,44 @@ def tile_list_embg_mix_resP_kernel(
         keep = ctx.enter_context(tc.tile_pool(name="keep", bufs=1))
         shared = ctx.enter_context(tc.tile_pool(name="shared", bufs=1))
         psum = ctx.enter_context(tc.psum_pool(name="psum", bufs=1))
-        banks = [psum.tile([P, HALF], F32, name=f"bank{i}") for i in range(8)]
+        banks = [psum.tile([P, BANK], F32, name=f"bank{i}") for i in range(8)]
+
+        def new_tile(name, shape, dtype, offset=None):
+            if offset is None:
+                return keep.tile(shape, dtype, name=name, align_bytes=64)
+            return shared.tile(shape, dtype, name=name, align_bytes=64, offset=offset)
 
         offsets = keep.tile([P, J // 16], U16, name="offsets")
-        w8 = keep.tile([P, N], U32, name="w8", align_bytes=64)
-        w4 = keep.tile([P, 2 * N], U8, name="w4", align_bytes=64)
-        w_scales = keep.tile([P, 2 * N], U8, name="w_scales", align_bytes=64)
-        gain = keep.tile([P, J], F32, name="gain", align_bytes=64)
-        ident = keep.tile([P, P], F32, name="ident", align_bytes=64)
-        windows = {b: keep.tile([P, T], F32, name=f"window{b}", align_bytes=64) for b in range(2)}
+        w8 = new_tile("w8", [P, N], U32)
+        w4 = new_tile("w4", [P, 2 * N], U8)
+        w_scales = new_tile("w_scales", [P, 2 * N], U8)
+        ident = new_tile("ident", [P, P], F32)
+        windows = {0: new_tile("window0", [P, T], F32)}
 
         raw = {}
         resid = {}
+        gain = {}
 
-        def load_dy(c, a, lo, hi, offset=None):
-            name = f"raw{c}{a}{lo}"
-            if offset is None:
-                raw[c, a, lo] = keep.tile([P, 4, hi - lo], F32, name=name, align_bytes=64)
-            else:
-                raw[c, a, lo] = shared.tile([P, 4, hi - lo], F32, name=name, align_bytes=64, offset=offset)
+        def load_dy(c, a, offset=None):
+            raw[c, a] = new_tile(f"raw{c}{a}", [P, 4, CHUNK], F32, offset)
             nc.sync.dma_start(
-                out=raw[c, a, lo][:],
-                in_=dy[512 * a : 512 * (a + 1), c * HALF + lo : c * HALF + hi].rearrange("(p i) j -> p i j", i=4),
+                out=raw[c, a][:],
+                in_=dy[512 * a : 512 * (a + 1), c * CHUNK : (c + 1) * CHUNK].rearrange("(p i) j -> p i j", i=4),
             )
 
-        def load_res(b, c, lo=0, hi=HALF):
-            if lo == 0:
-                resid[b, c] = keep.tile([P, HALF], F32, name=f"res{b}{c}", align_bytes=64)
-            nc.sync.dma_start(out=resid[b, c][:, lo:hi], in_=res[P * b : P * (b + 1), c * HALF + lo : c * HALF + hi])
+        def load_res(b0, b1, c0, c1):
+            rows = new_tile(f"res{b0}{c0}", [P, b1 - b0, (c1 - c0) * CHUNK], F32)
+            nc.sync.dma_start(
+                out=rows[:],
+                in_=res[P * b0 : P * b1, c0 * CHUNK : c1 * CHUNK].rearrange("(d p) j -> p d j", p=P),
+            )
+            for b in range(b0, b1):
+                for c in range(c0, c1):
+                    resid[b, c] = rows[:, b - b0, (c - c0) * CHUNK : (c - c0 + 1) * CHUNK]
 
         def load_gain(c):
-            nc.sync.dma_start(out=gain[:, c * HALF : (c + 1) * HALF], in_=wgo[:, c * HALF : (c + 1) * HALF])
+            gain[c] = new_tile(f"gain{c}", [P, CHUNK], F32)
+            nc.sync.dma_start(out=gain[c][:], in_=wgo[:, c * CHUNK : (c + 1) * CHUNK])
 
         def load_scales(a, source):
             for q in range(4):
@@ -86,8 +91,7 @@ def tile_list_embg_mix_resP_kernel(
                 )
 
         nc.gpsimd.memset(w_scales[:].bitcast(U32), 0)
-        gain_rows = keep.tile([P, P], F32, name="gain_rows", align_bytes=64)
-        gain_cols = keep.tile([P, J // P], F32, name="gain_cols", align_bytes=64)
+        gain_rows = new_tile("gain_rows", [P, P], F32)
         nc.gpsimd.memset(gain_rows[:], 0.0)
         warm_in = keep.tile([P, 8], F32, name="warm_in")
         warm_out = keep.tile([P, 8], BF16, name="warm_out")
@@ -95,42 +99,38 @@ def tile_list_embg_mix_resP_kernel(
         nc.scalar.copy(out=warm_out[:], in_=warm_in[:])
 
         nc.sync.dma_start(offsets[:], offs)
-        load_dy(0, 1, 0, PIECE)
+        load_dy(0, 1)
         load_scales(1, w4_scales)
+        load_dy(0, 0)
         nc.sync.dma_start(out=w4[:].bitcast(I32), in_=w4_words[0].bitcast(I32))
-        load_dy(0, 1, PIECE, HALF)
-        load_dy(0, 0, 0, HALF - P)
-        load_dy(0, 0, HALF - P, HALF)
-        load_scales(0, w8_scales)
         nc.sync.dma_start(out=w8[:].bitcast(I32), in_=w8_words[0].rearrange("p n i -> p (n i)").bitcast(I32))
-        load_res(0, 0)
-        load_res(1, 0, 0, PIECE)
+        load_scales(0, w8_scales)
+        load_res(0, 2, 0, 1)
         load_gain(0)
+        load_dy(1, 1)
+        load_dy(1, 0, RAW_10)
         nc.sync.dma_start(out=gain_rows[0 : J // P, :], in_=wgo[0].rearrange("(h q) -> h q", q=P))
-        load_dy(1, 1, 0, PIECE)
-        load_dy(1, 1, PIECE, HALF)
-        load_res(2, 0)
-        load_res(1, 0, PIECE, HALF)
-        load_dy(1, 0, 0, PIECE)
-        load_dy(1, 0, PIECE, HALF, offset=LAST_RAW)
-        load_res(3, 0)
-        load_res(1, 1)
-        load_res(0, 1)
-        load_res(2, 1)
+        load_res(2, 4, 0, 1)
+        load_dy(2, 1)
+        load_dy(2, 0, RAW_20)
+        load_res(2, 4, 1, 2)
+        load_res(0, 2, 1, 2)
         load_gain(1)
-        load_res(3, 1)
+        load_res(0, 2, 2, 3)
+        load_dy(3, 1, RAW_31)
+        load_dy(3, 0, RAW_30)
+        load_res(0, 2, 3, 4)
+        load_res(2, 4, 2, 4)
 
-        for b in range(2):
-            nc.vector.memset(windows[b][:].bitcast(U32), 0)
+        nc.vector.memset(windows[0][:].bitcast(U32), 0)
         make_identity(nc, ident[:])
 
         def clear_window(b, offset):
-            windows[b] = shared.tile([P, T], F32, name=f"window{b}", align_bytes=64, offset=offset)
+            windows[b] = new_tile(f"window{b}", [P, T], F32, offset)
             nc.gpsimd.memset(windows[b][:].bitcast(U32), 0)
 
-        grouped = {}
-        dy_codes = {}
-        dy_scales = {}
+        dy_codes = {c: new_tile(f"dy_codes{c}", [P, 2 * CHUNK], U32) for c in range(4)}
+        dy_scales = {c: new_tile(f"dy_scales{c}", [P, 2 * CHUNK], U8) for c in range(4)}
 
         def round_dy(copy, columns, rows):
             copy(
@@ -138,94 +138,102 @@ def tile_list_embg_mix_resP_kernel(
                 in_=rows.rearrange("p i (g e) -> p g i e", e=4),
             )
 
-        def quantise_dy(c, a, lo, hi):
-            if lo == 0:
-                dy_codes[c, a] = keep.tile([P, HALF], U32, name=f"dy_codes{c}{a}", align_bytes=64)
-                dy_scales[c, a] = keep.tile([P, HALF], U8, name=f"dy_scales{c}{a}", align_bytes=64)
+        def quantise_dy(c, lo, hi, grouped):
             nc.vector.quantize_mx(
-                out=dy_codes[c, a][:, lo:hi].bitcast(E5M2),
-                scales=dy_scales[c, a][:, lo:hi],
-                in_=grouped[c, a, lo][:].rearrange("p j i -> p (j i)"),
+                out=dy_codes[c][:, lo:hi].bitcast(E5M2),
+                scales=dy_scales[c][:, lo:hi],
+                in_=grouped.rearrange("p j i -> p (j i)"),
             )
 
-        values = {}
+        def round_chunk(c, offset=None):
+            grouped = new_tile(f"grouped{c}", [P, 2 * CHUNK, 4], BF16, offset)
+            for a in (1, 0):
+                round_dy(nc.scalar.copy, grouped[:, a * CHUNK : (a + 1) * CHUNK, :], raw[c, a][:])
+            return grouped
 
-        def mx_pass(k, a, first=1):
-            b, c = TILES[k]
+        def mx_pass(b, c, a, target, first=1):
             if a == 0:
                 words = w8[:, P * b : P * (b + 1)].bitcast(E4M3)
             else:
                 words = w4[:, 2 * P * b : 2 * P * (b + 1)].bitcast(E2M1)
+            cols = slice(a * CHUNK, (a + 1) * CHUNK)
             nc.tensor.matmul_mx(
-                out=banks[PRODUCT_BANK[k]][:],
+                out=target,
                 lhsT=words,
                 lhsT_scale=w_scales[:, a * N + P * b : a * N + P * (b + 1)],
-                rhs=dy_codes[c, a][:].bitcast(E5M2),
-                rhs_scale=dy_scales[c, a][:],
+                rhs=dy_codes[c][:, cols].bitcast(E5M2),
+                rhs_scale=dy_scales[c][:, cols],
                 start=(a == first),
                 stop=(a != first),
             )
 
-        def new_values(k):
-            return keep.tile([P, HALF], F32, name=f"sum{k}", align_bytes=64)[:]
+        def half(bank, u):
+            return banks[bank][:, u * CHUNK : (u + 1) * CHUNK]
 
-        def add_res(k, lo=0, hi=HALF):
-            if lo == 0:
-                values[k] = new_values(k)
-            product, rows = banks[PRODUCT_BANK[k]], resid[TILES[k]]
-            nc.vector.tensor_tensor(values[k][:, lo:hi], product[:, lo:hi], rows[:, lo:hi], ADD)
+        def products(units, bank, first_half=0):
+            for u, (b, c) in enumerate(units, first_half):
+                for a in (0, 1):
+                    mx_pass(b, c, a, half(bank, u), first=0)
 
-        def turn_into_sum(k, source, opens):
-            for j0 in range(0, HALF, P):
-                cols = slice(j0, j0 + P)
-                start, stop = opens and j0 == 0, not opens and j0 == HALF - P
+        def places(b, lo, hi):
+            return windows[b][:].indirect(offsets[:, lo // 16 : hi // 16])
+
+        def add_res(b, c, product, target):
+            nc.vector.tensor_tensor(target, product, resid[b, c], ADD)
+
+        def scatter_times_gain(b, c, values):
+            nc.vector.tensor_tensor(places(b, c * CHUNK, (c + 1) * CHUNK), values, gain[c][:], MULT)
+
+        def blocks_of(units):
+            return sorted((2 * c + h, u, h) for u, (b, c) in enumerate(units) for h in range(2))
+
+        def turn_res(units, sum_bank):
+            for s, (col, u, h) in enumerate(blocks_of(units)):
                 nc.tensor.matmul(
-                    banks[SUM_BANK[k]][:, cols], source[:, cols], ident[:], start=start, stop=stop, is_transpose=True
+                    banks[sum_bank][:, P * s : P * (s + 1)], resid[units[u]][:, P * h : P * (h + 1)], ident[:],
+                    start=(s == 0), stop=False, is_transpose=True,
                 )
 
-        def turn_res(k):
-            turn_into_sum(k, resid[TILES[k]], opens=True)
+        def turn_product(units, product_bank, sum_bank, product):
+            nc.scalar.copy(out=product[:], in_=banks[product_bank][:])
+            for s, (col, u, h) in enumerate(blocks_of(units)):
+                j0 = CHUNK * u + P * h
+                nc.tensor.matmul(
+                    banks[sum_bank][:, P * s : P * (s + 1)], product[:, j0 : j0 + P], ident[:],
+                    start=False, stop=(s == 3), is_transpose=True,
+                )
 
-        def turn_product_and_back(k):
-            product = keep.tile([P, HALF], F32, name=f"product{k}", align_bytes=64)
-            nc.scalar.copy(out=product[:], in_=banks[PRODUCT_BANK[k]][:])
-            turn_into_sum(k, product, opens=False)
-            turned_sum = keep.tile([P, HALF], F32, name=f"turned_sum{k}", align_bytes=64)
-            for j0 in range(0, HALF, P):
-                h = (TILES[k][1] * HALF + j0) // P
-                cols = slice(j0, j0 + P)
-                nc.scalar.activation(turned_sum[:, cols], banks[SUM_BANK[k]][:, cols], COPY, scale=gain_cols[:, h : h + 1])
-            for j0 in range(0, HALF, P):
-                cols = slice(j0, j0 + P)
-                nc.tensor.transpose(banks[RETURN_BANK[k]][:, cols], turned_sum[:, cols], ident[:])
+        def turn_back(units, product_bank, sum_bank, offset=None):
+            blocks = blocks_of(units)
+            turned = new_tile(f"turned{product_bank}", [P, BANK], F32, offset)
+            for col in sorted(set(block[0] for block in blocks)):
+                mine = [s for s, block in enumerate(blocks) if block[0] == col]
+                cols = slice(P * mine[0], P * (mine[-1] + 1))
+                nc.scalar.activation(turned[:, cols], banks[sum_bank][:, cols], COPY, scale=gain_cols[:, col : col + 1])
+            for s, (col, u, h) in enumerate(blocks):
+                j0 = CHUNK * u + P * h
+                nc.tensor.transpose(banks[product_bank][:, j0 : j0 + P], turned[:, P * s : P * (s + 1)], ident[:])
 
-        def fetch_values(k, target, lo=0, hi=HALF):
-            nc.scalar.copy(out=target, in_=banks[RETURN_BANK[k]][:, lo:hi])
-            values[k] = target
-
-        def scatter(k, lo=0, hi=HALF):
-            b, c = TILES[k]
-            places = windows[b][:].indirect(offsets[:, (c * HALF + lo) // 16 : (c * HALF + hi) // 16])
-            if k in ADDED_BY_VECTOR:
-                nc.vector.tensor_tensor(places, values[k], gain[:, c * HALF + lo : c * HALF + hi], MULT)
-            else:
-                nc.vector.tensor_copy(places, values[k])
+        def fetch(product_bank, targets):
+            width = BANK // len(targets)
+            for u, target in enumerate(targets):
+                nc.scalar.copy(out=target, in_=banks[product_bank][:, u * width : (u + 1) * width])
 
         words_out = out_1[0].rearrange("p t i -> p (t i)").bitcast(I32)
         scales_out = out_2[0].bitcast(I32)
-        pair_tiles = [keep.tile([P, 2 * P], F32, name=f"pairs{g}", align_bytes=64) for g in range(4)]
-        y_codes = keep.tile([P, 4 * HALF], U32, name="y_codes", align_bytes=64)
-        y_scales = keep.tile([P, HALF], U8, name="y_scales", align_bytes=64)
+        pair_tiles = [new_tile(f"pairs{g}", [P, 2 * P], F32) for g in range(4)]
+        y_codes = new_tile("y_codes", [P, 4 * BANK], U32)
+        y_scales = new_tile("y_scales", [P, BANK], U8)
 
         def store_and_regroup(b, first_copies, second_copies):
             window = windows[b]
-            first_banks, second_banks = PLANE_BANKS[b % 2], PLANE_BANKS[1 - b % 2]
+            first_banks, second_banks = PLANE_BANKS if b < 3 else reversed(PLANE_BANKS)
             nc.sync.dma_start(out=out_0[P * b : P * (b + 1), :], in_=window[:])
-            rounded = keep.tile([P, 4, P, 2], F32, name=f"rounded{b}", align_bytes=64)
+            rounded = new_tile(f"rounded{b}", [P, 4, P, 2], F32)
             for g in range(4):
                 turned = banks[first_banks[g]][:].rearrange("s (q r) -> s q r", q=4)
                 for tq in range(4):
-                    t0 = HALF * tq + P * g
+                    t0 = BANK * tq + P * g
                     nc.tensor.transpose(turned[:, tq, :], window[:, t0 : t0 + P], ident[:])
                 first_copies[g](
                     out=pair_tiles[g][:].bitcast(BF16).rearrange("s (u m e) -> s u m e", u=2, e=2),
@@ -243,7 +251,7 @@ def tile_list_embg_mix_resP_kernel(
         def quantise_out(b, rounded, lo, hi):
             flat = rounded[:].rearrange("m g s u -> m (g s u)").bitcast(BF16)
             nc.vector.quantize_mx(
-                out=y_codes[:, HALF * b + lo : HALF * b + hi].bitcast(E4M3),
+                out=y_codes[:, BANK * b + lo : BANK * b + hi].bitcast(E4M3),
                 scales=y_scales[4 * b : P, lo:hi],
                 in_=flat[:, 4 * lo : 4 * hi],
             )
@@ -254,92 +262,107 @@ def tile_list_embg_mix_resP_kernel(
         def store_codes(b0, b1):
             rows = words_out[QUAD * b0 : QUAD * b1, :].rearrange("(d p) t -> p d t", p=QUAD)
             for tq in (0, 2, 1, 3):
-                quarter = y_codes[QUAD * tq : QUAD * (tq + 1), HALF * b0 : HALF * b1].bitcast(I32)
+                quarter = y_codes[QUAD * tq : QUAD * (tq + 1), BANK * b0 : BANK * b1].bitcast(I32)
                 queue_of(tq).dma_start(
-                    out=rows[:, :, HALF * tq : HALF * (tq + 1)],
-                    in_=quarter.rearrange("p (d s) -> p d s", s=HALF),
+                    out=rows[:, :, BANK * tq : BANK * (tq + 1)],
+                    in_=quarter.rearrange("p (d s) -> p d s", s=BANK),
                 )
 
         on_scalar, on_vector = nc.scalar.copy, nc.vector.tensor_copy
 
-        for lo in (0, PIECE):
-            grouped[0, 1, lo] = keep.tile([P, PIECE, 4], BF16, name=f"grouped01{lo}", align_bytes=64)
-            split = 0 if lo == 0 else VECTOR_COLUMNS
-            round_dy(on_scalar, grouped[0, 1, lo][:, split:PIECE, :], raw[0, 1, lo][:, :, split:PIECE])
-            if split:
-                round_dy(on_vector, grouped[0, 1, lo][:, 0:split, :], raw[0, 1, lo][:, :, 0:split])
-        for lo in (0, PIECE):
-            quantise_dy(0, 1, lo, lo + PIECE)
-        for k in range(3):
-            mx_pass(k, 1)
-        front = keep.tile([P, PIECE, 4], BF16, name="front", align_bytes=64)
-        rear = shared.tile([P, PIECE, 4], BF16, name="rear", align_bytes=64, offset=HEAD_REAR)
-        grouped[0, 0, 0], grouped[0, 0, PIECE] = front, rear
-        round_dy(on_vector, front[:], raw[0, 0, 0][:, :, 0:PIECE])
-        round_dy(on_scalar, rear[:, 0:P, :], raw[0, 0, 0][:, :, PIECE : HALF - P])
-        round_dy(on_scalar, rear[:, P:PIECE, :], raw[0, 0, HALF - P][:])
-        for lo in (0, PIECE):
-            quantise_dy(0, 0, lo, lo + PIECE)
-        clear_window(2, HEAD_REAR)
-        for k in range(3):
-            mx_pass(k, 0)
-        nc.tensor.transpose(banks[SUM_BANK[6]][:, 0:P], gain_rows[:], ident[:])
-        nc.scalar.copy(out=gain_cols[:], in_=banks[SUM_BANK[6]][:, 0 : J // P])
-        turn_res(2)
-        turn_product_and_back(2)
-        mx_pass(6, 0, first=0)
-        mx_pass(6, 1, first=0)
+        head1 = new_tile("head1", [P, CHUNK, 4], BF16)
+        round_dy(on_vector, head1[:, 0:VECTOR_COLUMNS, :], raw[0, 1][:, :, 0:VECTOR_COLUMNS])
+        round_dy(on_scalar, head1[:, VECTOR_COLUMNS:CHUNK, :], raw[0, 1][:, :, VECTOR_COLUMNS:CHUNK])
+        quantise_dy(0, CHUNK, 2 * CHUNK, head1[:])
+        for b in range(2):
+            mx_pass(b, 0, 1, half(b, 0))
+        head0 = new_tile("head0", [P, CHUNK, 4], BF16, HEAD_ROUNDED)
+        round_dy(on_vector, head0[:, 0:VECTOR_COLUMNS, :], raw[0, 0][:, :, 0:VECTOR_COLUMNS])
+        round_dy(on_scalar, head0[:, VECTOR_COLUMNS:CHUNK, :], raw[0, 0][:, :, VECTOR_COLUMNS:CHUNK])
+        quantise_dy(0, 0, CHUNK, head0[:])
+        clear_window(1, 0)
+        clear_window(2, 8 * KIB)
+        for b in range(2):
+            mx_pass(b, 0, 0, half(b, 0))
+        products([(2, 0), (3, 0)], 2)
+        first_sums = new_tile("first_sums", [P, 2, CHUNK], F32)
+        for b in range(2):
+            add_res(b, 0, half(b, 0), first_sums[:, b, :])
+        for b in range(2):
+            scatter_times_gain(b, 0, first_sums[:, b, :])
 
-        grouped[1, 1, 0] = keep.tile([P, HALF, 4], BF16, name="second1", align_bytes=64)
-        for lo in (0, PIECE):
-            round_dy(on_scalar, grouped[1, 1, 0][:, lo : lo + PIECE, :], raw[1, 1, lo][:])
-        grouped[1, 0, 0] = shared.tile([P, HALF, 4], BF16, name="second0", align_bytes=64, offset=SECOND_ROUNDED)
-        for lo in (0, PIECE):
-            round_dy(on_scalar, grouped[1, 0, 0][:, lo : lo + PIECE, :], raw[1, 0, lo][:])
-        early = shared.tile([P, PIECE], F32, name="sum2_early", align_bytes=64, offset=LAST_RAW)
-        fetch_values(2, early[:], 0, PIECE)
-        add_res(0)
-        add_res(1, 0, PIECE)
-        scatter(0)
-        add_res(1, PIECE, HALF)
-        quantise_dy(1, 1, 0, HALF)
-        scatter(1)
-        last_values = keep.tile([P, J], F32, name="last_sums", align_bytes=64)
-        turn_res(6)
-        turn_product_and_back(6)
-        fetch_values(6, last_values[:, 0:HALF])
-        for k in (3, 4, 5, 7):
-            mx_pass(k, 1)
-        turn_res(4)
+        grouped = round_chunk(1, ROUNDED_1)
+        sum_20 = new_tile("sum_20", [P, CHUNK], F32, RAW_10)
+        add_res(2, 0, half(2, 0), sum_20[:])
+        quantise_dy(1, 0, 2 * CHUNK, grouped[:])
+        products([(0, 1)], 4)
+        sum_c = [(2, 1), (3, 1)]
+        products(sum_c, 3)
+        scatter_times_gain(2, 0, sum_20[:])
+        clear_window(3, ROUNDED_1)
 
-        quantise_dy(1, 0, 0, HALF)
-        clear_window(3, LAST_WINDOW)
-        scatter(2, 0, PIECE)
-        mx_pass(3, 0)
-        add_res(3)
-        late = shared.tile([P, PIECE], F32, name="sum2_late", align_bytes=64, offset=SECOND_ROUNDED)
-        fetch_values(2, late[:], PIECE, HALF)
-        scatter(2, PIECE, HALF)
-        mx_pass(4, 0)
-        turn_product_and_back(4)
-        fetch_values(4, new_values(4))
-        for k in (5, 7):
-            turn_res(k)
-            mx_pass(k, 0)
-            turn_product_and_back(k)
-            fetch_values(k, new_values(k) if k == 5 else last_values[:, HALF:J])
+        grouped = round_chunk(2)
+        sum_30 = new_tile("sum_30", [P, CHUNK], F32, RAW_20 + KIB)
+        add_res(3, 0, half(2, 1), sum_30[:])
+        quantise_dy(2, 0, 2 * CHUNK, grouped[:])
+        third_sums = {0: new_tile("third_sum0", [P, CHUNK], F32, RAW_20), 1: new_tile("third_sum1", [P, CHUNK], F32, RAW_30 + KIB)}
+        add_res(0, 1, half(4, 0), third_sums[0][:])
+        products([(1, 1)], 4, 1)
+        scatter_times_gain(3, 0, sum_30[:])
+        scatter_times_gain(0, 1, third_sums[0][:])
+
+        gain_cols = new_tile("gain_cols", [P, J // P], F32)
+        nc.tensor.transpose(banks[7][:, 0:P], gain_rows[:], ident[:])
+        nc.scalar.copy(out=gain_cols[:], in_=banks[7][:, 0 : J // P])
+        late = {b: new_tile(f"late{b}", [P, 3 * CHUNK], F32) for b in (2, 3)}
+        turn_res(sum_c, 5)
+        turn_product(sum_c, 3, 5, new_tile("product_c", [P, BANK], F32, RAW_20 + 2 * KIB))
+        sum_a = [(0, 2), (1, 2)]
+        products(sum_a, 0)
+        turn_res(sum_a, 6)
+
+        grouped = new_tile("grouped3", [P, 2 * CHUNK, 4], BF16)
+        round_dy(nc.scalar.copy, grouped[:, CHUNK : 2 * CHUNK, :], raw[3, 1][:])
+        product = new_tile("product", [P, BANK], F32, RAW_31)
+        turn_product(sum_a, 0, 6, product)
+        round_dy(nc.scalar.copy, grouped[:, 0:CHUNK, :], raw[3, 0][:])
+        add_res(1, 1, half(4, 1), third_sums[1][:])
+        quantise_dy(3, 0, 2 * CHUNK, grouped[:])
+        scatter_times_gain(1, 1, third_sums[1][:])
+        early = {c: new_tile(f"early{c}", [P, BANK], F32) for c in (2, 3)}
+        turn_back(sum_a, 0, 6)
+        fetch(0, [early[2][:]])
+        turn_back(sum_c, 3, 5, RAW_30 - KIB)
+        fetch(3, [late[b][:, 0:CHUNK] for b in (2, 3)])
+        sum_b = [(0, 3), (1, 3)]
+        products(sum_b, 6)
+        turn_res(sum_b, 1)
+        turn_product(sum_b, 6, 1, product)
+        turn_back(sum_b, 6, 1)
+        fetch(6, [early[3][:]])
+        for b in (2, 3):
+            units, product_bank, sum_bank = [(b, 2), (b, 3)], 4 - b, 2 * b + 1
+            products(units, product_bank)
+            turn_res(units, sum_bank)
+            turn_product(units, product_bank, sum_bank, product)
+            turn_back(units, product_bank, sum_bank)
+            fetch(product_bank, [late[b][:, CHUNK : 3 * CHUNK]])
+        for b in range(2):
+            nc.vector.tensor_copy(places(b, 2 * CHUNK, 3 * CHUNK), early[2][:, b * CHUNK : (b + 1) * CHUNK])
 
         regrouped = []
+        for b in range(2):
+            nc.vector.tensor_copy(places(b, 3 * CHUNK, J), early[3][:, b * CHUNK : (b + 1) * CHUNK])
+        nc.vector.tensor_copy(places(2, CHUNK, J), late[2][:])
         for b in range(3):
-            scatter(3 + b)
             regrouped.append(store_and_regroup(b, [on_scalar] * 4, [on_scalar] * 4))
-        nc.vector.tensor_copy(windows[3][:].indirect(offsets[:]), last_values[:])
+        nc.vector.tensor_copy(places(3, CHUNK, J), late[3][:])
         for b in range(3):
-            quantise_out(b, regrouped[b], 0, HALF)
+            quantise_out(b, regrouped[b], 0, BANK)
         store_codes(0, 3)
         last = store_and_regroup(3, [on_scalar] * 3 + [on_vector], [on_vector, on_scalar] * 2)
-        for lo in (0, PIECE):
-            quantise_out(3, last, lo, lo + PIECE)
+        for lo in (0, CHUNK):
+            quantise_out(3, last, lo, lo + CHUNK)
         store_codes(3, 4)
         for tq in range(4):
             queue_of(tq).dma_start(

@@ -25,15 +25,13 @@ CHUNK = 256
 QUAD = 32
 VECTOR_COLUMNS = 160
 
-PLANE_BANKS = [(5, 2, 7, 1), (0, 3, 4, 6)]
 
 KIB = 1024
 HEAD_ROUNDED = 7 * KIB
-ROUNDED_1 = 16 * KIB
 RAW_10 = 24 * KIB
-RAW_30 = 40 * KIB
-RAW_31 = 44 * KIB
-RAW_20 = 32 * KIB
+RAW_21 = 28 * KIB
+RAW_20 = 36 * KIB
+SPANS = [(0, 256), (256, 512), (512, 1024)]
 
 
 def tile_list_embg_mix_resP_kernel(
@@ -56,32 +54,31 @@ def tile_list_embg_mix_resP_kernel(
         w4 = new_tile("w4", [P, 2 * N], U8)
         w_scales = new_tile("w_scales", [P, 2 * N], U8)
         ident = new_tile("ident", [P, P], F32)
-        windows = {0: new_tile("window0", [P, T], F32)}
+        windows = {b: new_tile(f"window{b}", [P, T], F32) for b in range(2)}
 
         raw = {}
         resid = {}
         gain = {}
 
         def load_dy(c, a, offset=None):
-            raw[c, a] = new_tile(f"raw{c}{a}", [P, 4, CHUNK], F32, offset)
+            lo, hi = SPANS[c]
+            raw[c, a] = new_tile(f"raw{c}{a}", [P, 4, hi - lo], F32, offset)
             nc.sync.dma_start(
                 out=raw[c, a][:],
-                in_=dy[512 * a : 512 * (a + 1), c * CHUNK : (c + 1) * CHUNK].rearrange("(p i) j -> p i j", i=4),
+                in_=dy[512 * a : 512 * (a + 1), lo:hi].rearrange("(p i) j -> p i j", i=4),
             )
 
-        def load_res(b0, b1, c0, c1):
-            rows = new_tile(f"res{b0}{c0}", [P, b1 - b0, (c1 - c0) * CHUNK], F32)
-            nc.sync.dma_start(
-                out=rows[:],
-                in_=res[P * b0 : P * b1, c0 * CHUNK : c1 * CHUNK].rearrange("(d p) j -> p d j", p=P),
-            )
-            for b in range(b0, b1):
-                for c in range(c0, c1):
-                    resid[b, c] = rows[:, b - b0, (c - c0) * CHUNK : (c - c0 + 1) * CHUNK]
+        def load_res(b0, c):
+            lo, hi = SPANS[c]
+            rows = new_tile(f"res{b0}{c}", [P, 2, hi - lo], F32)
+            nc.sync.dma_start(out=rows[:], in_=res[P * b0 : P * (b0 + 2), lo:hi].rearrange("(d p) j -> p d j", p=P))
+            for d in range(2):
+                resid[b0 + d, c] = rows[:, d, :]
 
         def load_gain(c):
-            gain[c] = new_tile(f"gain{c}", [P, CHUNK], F32)
-            nc.sync.dma_start(out=gain[c][:], in_=wgo[:, c * CHUNK : (c + 1) * CHUNK])
+            lo, hi = SPANS[c]
+            gain[c] = new_tile(f"gain{c}", [P, hi - lo], F32)
+            nc.sync.dma_start(out=gain[c][:], in_=wgo[:, lo:hi])
 
         def load_scales(a, source):
             for q in range(4):
@@ -105,32 +102,31 @@ def tile_list_embg_mix_resP_kernel(
         nc.sync.dma_start(out=w4[:].bitcast(I32), in_=w4_words[0].bitcast(I32))
         nc.sync.dma_start(out=w8[:].bitcast(I32), in_=w8_words[0].rearrange("p n i -> p (n i)").bitcast(I32))
         load_scales(0, w8_scales)
-        load_res(0, 2, 0, 1)
+        load_res(0, 0)
         load_gain(0)
         load_dy(1, 1)
         load_dy(1, 0, RAW_10)
-        nc.sync.dma_start(out=gain_rows[0 : J // P, :], in_=wgo[0].rearrange("(h q) -> h q", q=P))
-        load_res(2, 4, 0, 1)
-        load_dy(2, 1)
-        load_dy(2, 0, RAW_20)
-        load_res(2, 4, 1, 2)
-        load_res(0, 2, 1, 2)
+        load_res(2, 0)
+        load_dy(2, 1, RAW_21)
+        load_res(0, 1)
         load_gain(1)
-        load_res(0, 2, 2, 3)
-        load_dy(3, 1, RAW_31)
-        load_dy(3, 0, RAW_30)
-        load_res(0, 2, 3, 4)
-        load_res(2, 4, 2, 4)
+        load_dy(2, 0, RAW_20)
+        nc.sync.dma_start(out=gain_rows[0 : J // P, :], in_=wgo[0].rearrange("(h q) -> h q", q=P))
+        load_res(2, 1)
+        load_res(0, 2)
+        load_gain(2)
+        load_res(2, 2)
 
-        nc.vector.memset(windows[0][:].bitcast(U32), 0)
+        for b in range(2):
+            nc.vector.memset(windows[b][:].bitcast(U32), 0)
         make_identity(nc, ident[:])
 
         def clear_window(b, offset):
             windows[b] = new_tile(f"window{b}", [P, T], F32, offset)
             nc.gpsimd.memset(windows[b][:].bitcast(U32), 0)
 
-        dy_codes = {c: new_tile(f"dy_codes{c}", [P, 2 * CHUNK], U32) for c in range(4)}
-        dy_scales = {c: new_tile(f"dy_scales{c}", [P, 2 * CHUNK], U8) for c in range(4)}
+        dy_codes = [new_tile(f"dy_codes{c}", [P, 2 * (hi - lo)], U32) for c, (lo, hi) in enumerate(SPANS)]
+        dy_scales = [new_tile(f"dy_scales{c}", [P, 2 * (hi - lo)], U8) for c, (lo, hi) in enumerate(SPANS)]
 
         def round_dy(copy, columns, rows):
             copy(
@@ -156,7 +152,8 @@ def tile_list_embg_mix_resP_kernel(
                 words = w8[:, P * b : P * (b + 1)].bitcast(E4M3)
             else:
                 words = w4[:, 2 * P * b : 2 * P * (b + 1)].bitcast(E2M1)
-            cols = slice(a * CHUNK, (a + 1) * CHUNK)
+            width = SPANS[c][1] - SPANS[c][0]
+            cols = slice(a * width, (a + 1) * width)
             nc.tensor.matmul_mx(
                 out=target,
                 lhsT=words,
@@ -182,22 +179,26 @@ def tile_list_embg_mix_resP_kernel(
             nc.vector.tensor_tensor(target, product, resid[b, c], ADD)
 
         def scatter_times_gain(b, c, values):
-            nc.vector.tensor_tensor(places(b, c * CHUNK, (c + 1) * CHUNK), values, gain[c][:], MULT)
+            nc.vector.tensor_tensor(places(b, *SPANS[c]), values, gain[c][:], MULT)
 
         def blocks_of(units):
-            return sorted((2 * c + h, u, h) for u, (b, c) in enumerate(units) for h in range(2))
+            blocks, j0 = [], 0
+            for b, c in units:
+                lo, hi = SPANS[c]
+                for j in range(lo, hi, P):
+                    blocks.append((j // P, j0, resid[b, c][:, j - lo : j - lo + P]))
+                    j0 = j0 + P
+            return sorted(blocks, key=lambda block: block[:2])
 
         def turn_res(units, sum_bank):
-            for s, (col, u, h) in enumerate(blocks_of(units)):
+            for s, (col, j0, rows) in enumerate(blocks_of(units)):
                 nc.tensor.matmul(
-                    banks[sum_bank][:, P * s : P * (s + 1)], resid[units[u]][:, P * h : P * (h + 1)], ident[:],
-                    start=(s == 0), stop=False, is_transpose=True,
+                    banks[sum_bank][:, P * s : P * (s + 1)], rows, ident[:], start=(s == 0), stop=False, is_transpose=True
                 )
 
         def turn_product(units, product_bank, sum_bank, product):
             nc.scalar.copy(out=product[:], in_=banks[product_bank][:])
-            for s, (col, u, h) in enumerate(blocks_of(units)):
-                j0 = CHUNK * u + P * h
+            for s, (col, j0, rows) in enumerate(blocks_of(units)):
                 nc.tensor.matmul(
                     banks[sum_bank][:, P * s : P * (s + 1)], product[:, j0 : j0 + P], ident[:],
                     start=False, stop=(s == 3), is_transpose=True,
@@ -210,8 +211,7 @@ def tile_list_embg_mix_resP_kernel(
                 mine = [s for s, block in enumerate(blocks) if block[0] == col]
                 cols = slice(P * mine[0], P * (mine[-1] + 1))
                 nc.scalar.activation(turned[:, cols], banks[sum_bank][:, cols], COPY, scale=gain_cols[:, col : col + 1])
-            for s, (col, u, h) in enumerate(blocks):
-                j0 = CHUNK * u + P * h
+            for s, (col, j0, rows) in enumerate(blocks):
                 nc.tensor.transpose(banks[product_bank][:, j0 : j0 + P], turned[:, P * s : P * (s + 1)], ident[:])
 
         def fetch(product_bank, targets):
@@ -227,7 +227,7 @@ def tile_list_embg_mix_resP_kernel(
 
         def store_and_regroup(b, first_copies, second_copies):
             window = windows[b]
-            first_banks, second_banks = PLANE_BANKS if b < 3 else reversed(PLANE_BANKS)
+            first_banks, second_banks = ((5, 6, 5, 6), (0, 1, 3, 4)) if b < 3 else ((0, 1, 3, 4), (5, 6, 7, 2))
             nc.sync.dma_start(out=out_0[P * b : P * (b + 1), :], in_=window[:])
             rounded = new_tile(f"rounded{b}", [P, 4, P, 2], F32)
             for g in range(4):
@@ -271,8 +271,7 @@ def tile_list_embg_mix_resP_kernel(
         on_scalar, on_vector = nc.scalar.copy, nc.vector.tensor_copy
 
         head1 = new_tile("head1", [P, CHUNK, 4], BF16)
-        round_dy(on_vector, head1[:, 0:VECTOR_COLUMNS, :], raw[0, 1][:, :, 0:VECTOR_COLUMNS])
-        round_dy(on_scalar, head1[:, VECTOR_COLUMNS:CHUNK, :], raw[0, 1][:, :, VECTOR_COLUMNS:CHUNK])
+        round_dy(on_scalar, head1[:], raw[0, 1][:])
         quantise_dy(0, CHUNK, 2 * CHUNK, head1[:])
         for b in range(2):
             mx_pass(b, 0, 1, half(b, 0))
@@ -280,8 +279,8 @@ def tile_list_embg_mix_resP_kernel(
         round_dy(on_vector, head0[:, 0:VECTOR_COLUMNS, :], raw[0, 0][:, :, 0:VECTOR_COLUMNS])
         round_dy(on_scalar, head0[:, VECTOR_COLUMNS:CHUNK, :], raw[0, 0][:, :, VECTOR_COLUMNS:CHUNK])
         quantise_dy(0, 0, CHUNK, head0[:])
-        clear_window(1, 0)
-        clear_window(2, 8 * KIB)
+        clear_window(2, 0)
+        clear_window(3, 8 * KIB)
         for b in range(2):
             mx_pass(b, 0, 0, half(b, 0))
         products([(2, 0), (3, 0)], 2)
@@ -291,68 +290,58 @@ def tile_list_embg_mix_resP_kernel(
         for b in range(2):
             scatter_times_gain(b, 0, first_sums[:, b, :])
 
-        grouped = round_chunk(1, ROUNDED_1)
+        grouped = round_chunk(1)
         sum_20 = new_tile("sum_20", [P, CHUNK], F32, RAW_10)
         add_res(2, 0, half(2, 0), sum_20[:])
         quantise_dy(1, 0, 2 * CHUNK, grouped[:])
-        products([(0, 1)], 4)
+        sum_30 = new_tile("sum_30", [P, CHUNK], F32, RAW_10 + KIB)
+        add_res(3, 0, half(2, 1), sum_30[:])
+        products([(0, 1), (1, 1)], 4)
         sum_c = [(2, 1), (3, 1)]
         products(sum_c, 3)
         scatter_times_gain(2, 0, sum_20[:])
-        clear_window(3, ROUNDED_1)
-
-        grouped = round_chunk(2)
-        sum_30 = new_tile("sum_30", [P, CHUNK], F32, RAW_20 + KIB)
-        add_res(3, 0, half(2, 1), sum_30[:])
-        quantise_dy(2, 0, 2 * CHUNK, grouped[:])
-        third_sums = {0: new_tile("third_sum0", [P, CHUNK], F32, RAW_20), 1: new_tile("third_sum1", [P, CHUNK], F32, RAW_30 + KIB)}
-        add_res(0, 1, half(4, 0), third_sums[0][:])
-        products([(1, 1)], 4, 1)
         scatter_times_gain(3, 0, sum_30[:])
-        scatter_times_gain(0, 1, third_sums[0][:])
 
-        gain_cols = new_tile("gain_cols", [P, J // P], F32)
+        rear_banks = (0, 1, 2, 6)
+        rear1 = new_tile("rear1", [P, BANK, 4], BF16)
+        round_dy(on_scalar, rear1[:], raw[2, 1][:])
+        sum_01 = new_tile("sum_01", [P, CHUNK], F32, RAW_21)
+        add_res(0, 1, half(4, 0), sum_01[:])
+        quantise_dy(2, BANK, 2 * BANK, rear1[:])
+        for b in range(4):
+            mx_pass(b, 2, 1, banks[rear_banks[b]][:])
+        scatter_times_gain(0, 1, sum_01[:])
+        turn_res(sum_c, 5)
+        turn_product(sum_c, 3, 5, new_tile("product_c", [P, BANK], F32, RAW_21 + 2 * KIB))
+
+        rear0 = new_tile("rear0", [P, BANK, 4], BF16)
+        round_dy(on_scalar, rear0[:], raw[2, 0][:])
+        sum_11 = new_tile("sum_11", [P, CHUNK], F32, RAW_20)
+        add_res(1, 1, half(4, 1), sum_11[:])
+        quantise_dy(2, 0, BANK, rear0[:])
+        for b in range(4):
+            mx_pass(b, 2, 0, banks[rear_banks[b]][:])
+        scatter_times_gain(1, 1, sum_11[:])
+        rear_sums = new_tile("rear_sums", [P, 2, BANK], F32)
+        for b in range(2):
+            add_res(b, 2, banks[b][:], rear_sums[:, b, :])
+        for b in range(2):
+            scatter_times_gain(b, 2, rear_sums[:, b, :])
+
+        gain_cols = new_tile("gain_cols", [P, J // P], F32, RAW_20 + KIB)
         nc.tensor.transpose(banks[7][:, 0:P], gain_rows[:], ident[:])
         nc.scalar.copy(out=gain_cols[:], in_=banks[7][:, 0 : J // P])
         late = {b: new_tile(f"late{b}", [P, 3 * CHUNK], F32) for b in (2, 3)}
-        turn_res(sum_c, 5)
-        turn_product(sum_c, 3, 5, new_tile("product_c", [P, BANK], F32, RAW_20 + 2 * KIB))
-        sum_a = [(0, 2), (1, 2)]
-        products(sum_a, 0)
-        turn_res(sum_a, 6)
-
-        grouped = new_tile("grouped3", [P, 2 * CHUNK, 4], BF16)
-        round_dy(nc.scalar.copy, grouped[:, CHUNK : 2 * CHUNK, :], raw[3, 1][:])
-        product = new_tile("product", [P, BANK], F32, RAW_31)
-        turn_product(sum_a, 0, 6, product)
-        round_dy(nc.scalar.copy, grouped[:, 0:CHUNK, :], raw[3, 0][:])
-        add_res(1, 1, half(4, 1), third_sums[1][:])
-        quantise_dy(3, 0, 2 * CHUNK, grouped[:])
-        scatter_times_gain(1, 1, third_sums[1][:])
-        early = {c: new_tile(f"early{c}", [P, BANK], F32) for c in (2, 3)}
-        turn_back(sum_a, 0, 6)
-        fetch(0, [early[2][:]])
-        turn_back(sum_c, 3, 5, RAW_30 - KIB)
+        turn_back(sum_c, 3, 5)
         fetch(3, [late[b][:, 0:CHUNK] for b in (2, 3)])
-        sum_b = [(0, 3), (1, 3)]
-        products(sum_b, 6)
-        turn_res(sum_b, 1)
-        turn_product(sum_b, 6, 1, product)
-        turn_back(sum_b, 6, 1)
-        fetch(6, [early[3][:]])
-        for b in (2, 3):
-            units, product_bank, sum_bank = [(b, 2), (b, 3)], 4 - b, 2 * b + 1
-            products(units, product_bank)
-            turn_res(units, sum_bank)
-            turn_product(units, product_bank, sum_bank, product)
-            turn_back(units, product_bank, sum_bank)
-            fetch(product_bank, [late[b][:, CHUNK : 3 * CHUNK]])
-        for b in range(2):
-            nc.vector.tensor_copy(places(b, 2 * CHUNK, 3 * CHUNK), early[2][:, b * CHUNK : (b + 1) * CHUNK])
+        product = new_tile("product", [P, BANK], F32)
+        for b, sum_bank in ((2, 7), (3, 5)):
+            turn_res([(b, 2)], sum_bank)
+            turn_product([(b, 2)], rear_banks[b], sum_bank, product)
+            turn_back([(b, 2)], rear_banks[b], sum_bank)
+            fetch(rear_banks[b], [late[b][:, CHUNK : 3 * CHUNK]])
 
         regrouped = []
-        for b in range(2):
-            nc.vector.tensor_copy(places(b, 3 * CHUNK, J), early[3][:, b * CHUNK : (b + 1) * CHUNK])
         nc.vector.tensor_copy(places(2, CHUNK, J), late[2][:])
         for b in range(3):
             regrouped.append(store_and_regroup(b, [on_scalar] * 4, [on_scalar] * 4))

@@ -26,6 +26,7 @@ QUAD = 32
 VECTOR_COLUMNS = 160
 
 
+PLANE_BANKS = [(7, 2, 5, 6), (0, 1, 3, 4)]
 KIB = 1024
 HEAD_ROUNDED = 7 * KIB
 RAW_10 = 24 * KIB
@@ -227,7 +228,7 @@ def tile_list_embg_mix_resP_kernel(
 
         def store_and_regroup(b, first_copies, second_copies):
             window = windows[b]
-            first_banks, second_banks = ((5, 6, 5, 6), (0, 1, 3, 4)) if b < 3 else ((0, 1, 3, 4), (5, 6, 7, 2))
+            first_banks, second_banks = PLANE_BANKS[b % 2], PLANE_BANKS[1 - b % 2]
             nc.sync.dma_start(out=out_0[P * b : P * (b + 1), :], in_=window[:])
             rounded = new_tile(f"rounded{b}", [P, 4, P, 2], F32)
             for g in range(4):

@@ -23,15 +23,14 @@ P = 128
 BANK = 512
 CHUNK = 256
 QUAD = 32
-VECTOR_COLUMNS = 160
+VECTOR_COLUMNS = 128
 
 
 PLANE_BANKS = [(7, 2, 5, 6), (0, 1, 3, 4)]
 KIB = 1024
-HEAD_ROUNDED = 7 * KIB
-RAW_10 = 24 * KIB
-RAW_21 = 28 * KIB
-RAW_20 = 36 * KIB
+RAW_10 = 0
+RAW_21 = 4 * KIB
+RAW_20 = 12 * KIB
 SPANS = [(0, 256), (256, 512), (512, 1024)]
 
 
@@ -55,7 +54,7 @@ def tile_list_embg_mix_resP_kernel(
         w4 = new_tile("w4", [P, 2 * N], U8)
         w_scales = new_tile("w_scales", [P, 2 * N], U8)
         ident = new_tile("ident", [P, P], F32)
-        windows = {b: new_tile(f"window{b}", [P, T], F32) for b in range(2)}
+        windows = [new_tile(f"window{b}", [P, T], F32) for b in range(4)]
 
         raw = {}
         resid = {}
@@ -118,13 +117,9 @@ def tile_list_embg_mix_resP_kernel(
         load_gain(2)
         load_res(2, 2)
 
-        for b in range(2):
-            nc.vector.memset(windows[b][:].bitcast(U32), 0)
+        for window in windows:
+            nc.vector.memset(window[:].bitcast(U32), 0)
         make_identity(nc, ident[:])
-
-        def clear_window(b, offset):
-            windows[b] = new_tile(f"window{b}", [P, T], F32, offset)
-            nc.gpsimd.memset(windows[b][:].bitcast(U32), 0)
 
         dy_codes = [new_tile(f"dy_codes{c}", [P, 2 * (hi - lo)], U32) for c, (lo, hi) in enumerate(SPANS)]
         dy_scales = [new_tile(f"dy_scales{c}", [P, 2 * (hi - lo)], U8) for c, (lo, hi) in enumerate(SPANS)]
@@ -276,12 +271,10 @@ def tile_list_embg_mix_resP_kernel(
         quantise_dy(0, CHUNK, 2 * CHUNK, head1[:])
         for b in range(2):
             mx_pass(b, 0, 1, half(b, 0))
-        head0 = new_tile("head0", [P, CHUNK, 4], BF16, HEAD_ROUNDED)
+        head0 = new_tile("head0", [P, CHUNK, 4], BF16)
         round_dy(on_vector, head0[:, 0:VECTOR_COLUMNS, :], raw[0, 0][:, :, 0:VECTOR_COLUMNS])
         round_dy(on_scalar, head0[:, VECTOR_COLUMNS:CHUNK, :], raw[0, 0][:, :, VECTOR_COLUMNS:CHUNK])
         quantise_dy(0, 0, CHUNK, head0[:])
-        clear_window(2, 0)
-        clear_window(3, 8 * KIB)
         for b in range(2):
             mx_pass(b, 0, 0, half(b, 0))
         products([(2, 0), (3, 0)], 2)

@@ -23,14 +23,15 @@ P = 128
 BANK = 512
 CHUNK = 256
 QUAD = 32
-VECTOR_COLUMNS = 128
+VECTOR_COLUMNS = 160
 
 
-PLANE_BANKS = [(7, 2, 5, 6), (0, 1, 3, 4)]
+PLANE_BANKS = [(7, 2, 6, 5), (0, 1, 3, 4)]
 KIB = 1024
 RAW_10 = 0
-RAW_21 = 4 * KIB
-RAW_20 = 12 * KIB
+RAW_20 = 16 * KIB
+LATE_WINDOWS = 24 * KIB
+HEAD_ROUNDED = 31 * KIB
 SPANS = [(0, 256), (256, 512), (512, 1024)]
 
 
@@ -54,17 +55,19 @@ def tile_list_embg_mix_resP_kernel(
         w4 = new_tile("w4", [P, 2 * N], U8)
         w_scales = new_tile("w_scales", [P, 2 * N], U8)
         ident = new_tile("ident", [P, P], F32)
-        windows = [new_tile(f"window{b}", [P, T], F32) for b in range(4)]
+        windows = [new_tile(f"window{b}", [P, T], F32) for b in range(2)]
 
         raw = {}
         resid = {}
         gain = {}
 
-        def load_dy(c, a, offset=None):
+        def load_dy(c, a, offset=None, piece=None):
             lo, hi = SPANS[c]
-            raw[c, a] = new_tile(f"raw{c}{a}", [P, 4, hi - lo], F32, offset)
+            if piece is not None:
+                lo, hi = lo + piece * CHUNK, lo + (piece + 1) * CHUNK
+            raw[c, a, piece] = new_tile(f"raw{c}{a}{lo}", [P, 4, hi - lo], F32, offset)
             nc.sync.dma_start(
-                out=raw[c, a][:],
+                out=raw[c, a, piece][:],
                 in_=dy[512 * a : 512 * (a + 1), lo:hi].rearrange("(p i) j -> p i j", i=4),
             )
 
@@ -107,15 +110,16 @@ def tile_list_embg_mix_resP_kernel(
         load_dy(1, 1)
         load_dy(1, 0, RAW_10)
         load_res(2, 0)
-        load_dy(2, 1, RAW_21)
+        for a in (1, 0):
+            load_dy(2, a, None, 0)
+            load_dy(2, a, RAW_20 if a == 0 else None, 1)
         load_res(0, 1)
         load_gain(1)
-        load_dy(2, 0, RAW_20)
-        nc.sync.dma_start(out=gain_rows[0 : J // P, :], in_=wgo[0].rearrange("(h q) -> h q", q=P))
         load_res(2, 1)
+        nc.sync.dma_start(out=gain_rows[0 : J // P, :], in_=wgo[0].rearrange("(h q) -> h q", q=P))
         load_res(0, 2)
-        load_gain(2)
         load_res(2, 2)
+        load_gain(2)
 
         for window in windows:
             nc.vector.memset(window[:].bitcast(U32), 0)
@@ -140,7 +144,7 @@ def tile_list_embg_mix_resP_kernel(
         def round_chunk(c, offset=None):
             grouped = new_tile(f"grouped{c}", [P, 2 * CHUNK, 4], BF16, offset)
             for a in (1, 0):
-                round_dy(nc.scalar.copy, grouped[:, a * CHUNK : (a + 1) * CHUNK, :], raw[c, a][:])
+                round_dy(nc.scalar.copy, grouped[:, a * CHUNK : (a + 1) * CHUNK, :], raw[c, a, None][:])
             return grouped
 
         def mx_pass(b, c, a, target, first=1):
@@ -267,14 +271,17 @@ def tile_list_embg_mix_resP_kernel(
         on_scalar, on_vector = nc.scalar.copy, nc.vector.tensor_copy
 
         head1 = new_tile("head1", [P, CHUNK, 4], BF16)
-        round_dy(on_scalar, head1[:], raw[0, 1][:])
+        round_dy(on_scalar, head1[:], raw[0, 1, None][:])
         quantise_dy(0, CHUNK, 2 * CHUNK, head1[:])
         for b in range(2):
             mx_pass(b, 0, 1, half(b, 0))
-        head0 = new_tile("head0", [P, CHUNK, 4], BF16)
-        round_dy(on_vector, head0[:, 0:VECTOR_COLUMNS, :], raw[0, 0][:, :, 0:VECTOR_COLUMNS])
-        round_dy(on_scalar, head0[:, VECTOR_COLUMNS:CHUNK, :], raw[0, 0][:, :, VECTOR_COLUMNS:CHUNK])
+        head0 = new_tile("head0", [P, CHUNK, 4], BF16, HEAD_ROUNDED)
+        round_dy(on_vector, head0[:, 0:VECTOR_COLUMNS, :], raw[0, 0, None][:, :, 0:VECTOR_COLUMNS])
+        round_dy(on_scalar, head0[:, VECTOR_COLUMNS:CHUNK, :], raw[0, 0, None][:, :, VECTOR_COLUMNS:CHUNK])
         quantise_dy(0, 0, CHUNK, head0[:])
+        for b in (2, 3):
+            windows.append(new_tile(f"window{b}", [P, T], F32, LATE_WINDOWS + 4 * T * (b - 2)))
+            nc.gpsimd.memset(windows[b][:].bitcast(U32), 0)
         for b in range(2):
             mx_pass(b, 0, 0, half(b, 0))
         products([(2, 0), (3, 0)], 2)
@@ -285,57 +292,62 @@ def tile_list_embg_mix_resP_kernel(
             scatter_times_gain(b, 0, first_sums[:, b, :])
 
         grouped = round_chunk(1)
-        sum_20 = new_tile("sum_20", [P, CHUNK], F32, RAW_10)
-        add_res(2, 0, half(2, 0), sum_20[:])
+        second_sums = new_tile("second_sums", [P, 2, CHUNK], F32, RAW_10)
+        add_res(2, 0, half(2, 0), second_sums[:, 0, :])
         quantise_dy(1, 0, 2 * CHUNK, grouped[:])
-        sum_30 = new_tile("sum_30", [P, CHUNK], F32, RAW_10 + KIB)
-        add_res(3, 0, half(2, 1), sum_30[:])
+        add_res(3, 0, half(2, 1), second_sums[:, 1, :])
         products([(0, 1), (1, 1)], 4)
         sum_c = [(2, 1), (3, 1)]
         products(sum_c, 3)
-        scatter_times_gain(2, 0, sum_20[:])
-        scatter_times_gain(3, 0, sum_30[:])
+        for u in range(2):
+            scatter_times_gain(2 + u, 0, second_sums[:, u, :])
 
-        rear_banks = (0, 1, 2, 6)
-        rear1 = new_tile("rear1", [P, BANK, 4], BF16)
-        round_dy(on_scalar, rear1[:], raw[2, 1][:])
-        sum_01 = new_tile("sum_01", [P, CHUNK], F32, RAW_21)
-        add_res(0, 1, half(4, 0), sum_01[:])
-        quantise_dy(2, BANK, 2 * BANK, rear1[:])
-        for b in range(4):
-            mx_pass(b, 2, 1, banks[rear_banks[b]][:])
-        scatter_times_gain(0, 1, sum_01[:])
-        turn_res(sum_c, 5)
-        turn_product(sum_c, 3, 5, new_tile("product_c", [P, BANK], F32, RAW_21 + 2 * KIB))
-
-        rear0 = new_tile("rear0", [P, BANK, 4], BF16)
-        round_dy(on_scalar, rear0[:], raw[2, 0][:])
-        sum_11 = new_tile("sum_11", [P, CHUNK], F32, RAW_20)
-        add_res(1, 1, half(4, 1), sum_11[:])
-        quantise_dy(2, 0, BANK, rear0[:])
-        for b in range(4):
-            mx_pass(b, 2, 0, banks[rear_banks[b]][:])
-        scatter_times_gain(1, 1, sum_11[:])
-        rear_sums = new_tile("rear_sums", [P, 2, BANK], F32)
+        rear = {}
+        for a in (1, 0):
+            rear[a] = new_tile(f"rear{a}", [P, BANK, 4], BF16)
+            for piece in range(2):
+                round_dy(on_scalar, rear[a][:, piece * CHUNK : (piece + 1) * CHUNK, :], raw[2, a, piece][:])
+        third_sums = new_tile("third_sums", [P, 2, CHUNK], F32, RAW_20 - KIB)
+        for a in (1, 0):
+            quantise_dy(2, a * BANK, (a + 1) * BANK, rear[a][:])
+            for b in range(3):
+                mx_pass(b, 2, a, banks[b][:])
+            add_res(1 - a, 1, half(4, 1 - a), third_sums[:, 1 - a, :])
         for b in range(2):
-            add_res(b, 2, banks[b][:], rear_sums[:, b, :])
-        for b in range(2):
-            scatter_times_gain(b, 2, rear_sums[:, b, :])
+            scatter_times_gain(b, 1, third_sums[:, b, :])
+        rear_sum = new_tile("rear_sum", [P, BANK], F32)
+        for lo in (0, CHUNK):
+            cols = slice(lo, lo + CHUNK)
+            nc.vector.tensor_tensor(rear_sum[:, cols], banks[0][:, cols], resid[0, 2][:, cols], ADD)
+        for lo in (0, CHUNK):
+            cols = slice(lo, lo + CHUNK)
+            nc.vector.tensor_tensor(places(0, BANK + lo, BANK + lo + CHUNK), rear_sum[:, cols], gain[2][:, cols], MULT)
 
-        gain_cols = new_tile("gain_cols", [P, J // P], F32, RAW_20 + KIB)
+        gain_cols = new_tile("gain_cols", [P, J // P], F32)
         nc.tensor.transpose(banks[7][:, 0:P], gain_rows[:], ident[:])
         nc.scalar.copy(out=gain_cols[:], in_=banks[7][:, 0 : J // P])
         late = {b: new_tile(f"late{b}", [P, 3 * CHUNK], F32) for b in (2, 3)}
+        late[1] = new_tile("late1", [P, BANK], F32)
+        product = new_tile("product", [P, BANK], F32)
+        turn_res([(1, 2)], 4)
+        turn_product([(1, 2)], 1, 4, product)
+        turn_back([(1, 2)], 1, 4)
+        fetch(1, [late[1][:]])
+        turn_res(sum_c, 5)
+        turn_product(sum_c, 3, 5, new_tile("product_c", [P, BANK], F32, RAW_20 + 2 * KIB))
         turn_back(sum_c, 3, 5)
         fetch(3, [late[b][:, 0:CHUNK] for b in (2, 3)])
-        product = new_tile("product", [P, BANK], F32)
-        for b, sum_bank in ((2, 7), (3, 5)):
+        for b, product_bank, sum_bank in ((2, 2, 7), (3, 5, 6)):
+            if b == 3:
+                for a in (1, 0):
+                    mx_pass(b, 2, a, banks[product_bank][:])
             turn_res([(b, 2)], sum_bank)
-            turn_product([(b, 2)], rear_banks[b], sum_bank, product)
-            turn_back([(b, 2)], rear_banks[b], sum_bank)
-            fetch(rear_banks[b], [late[b][:, CHUNK : 3 * CHUNK]])
+            turn_product([(b, 2)], product_bank, sum_bank, product)
+            turn_back([(b, 2)], product_bank, sum_bank)
+            fetch(product_bank, [late[b][:, CHUNK : 3 * CHUNK]])
 
         regrouped = []
+        nc.vector.tensor_copy(places(1, BANK, J), late[1][:])
         nc.vector.tensor_copy(places(2, CHUNK, J), late[2][:])
         for b in range(3):
             regrouped.append(store_and_regroup(b, [on_scalar] * 4, [on_scalar] * 4))

@@ -29,6 +29,7 @@ VECTOR_COLUMNS = 160
 PLANE_BANKS = [(7, 2, 6, 5), (0, 1, 3, 4)]
 KIB = 1024
 RAW_10 = 0
+RAW_21 = 8 * KIB
 RAW_20 = 16 * KIB
 LATE_WINDOWS = 24 * KIB
 HEAD_ROUNDED = 31 * KIB
@@ -112,7 +113,7 @@ def tile_list_embg_mix_resP_kernel(
         load_res(2, 0)
         for a in (1, 0):
             load_dy(2, a, None, 0)
-            load_dy(2, a, RAW_20 if a == 0 else None, 1)
+            load_dy(2, a, RAW_20 if a == 0 else RAW_21, 1)
         load_res(0, 1)
         load_gain(1)
         load_res(2, 1)
@@ -292,27 +293,31 @@ def tile_list_embg_mix_resP_kernel(
             scatter_times_gain(b, 0, first_sums[:, b, :])
 
         grouped = round_chunk(1)
-        second_sums = new_tile("second_sums", [P, 2, CHUNK], F32, RAW_10)
-        add_res(2, 0, half(2, 0), second_sums[:, 0, :])
+        sum_20 = new_tile("sum_20", [P, CHUNK], F32, RAW_10)
+        add_res(2, 0, half(2, 0), sum_20[:])
         quantise_dy(1, 0, 2 * CHUNK, grouped[:])
-        add_res(3, 0, half(2, 1), second_sums[:, 1, :])
         products([(0, 1), (1, 1)], 4)
         sum_c = [(2, 1), (3, 1)]
         products(sum_c, 3)
-        for u in range(2):
-            scatter_times_gain(2 + u, 0, second_sums[:, u, :])
+        scatter_times_gain(2, 0, sum_20[:])
 
         rear = {}
         for a in (1, 0):
             rear[a] = new_tile(f"rear{a}", [P, BANK, 4], BF16)
             for piece in range(2):
                 round_dy(on_scalar, rear[a][:, piece * CHUNK : (piece + 1) * CHUNK, :], raw[2, a, piece][:])
+        sum_30 = new_tile("sum_30", [P, CHUNK], F32, RAW_21)
+        add_res(3, 0, half(2, 1), sum_30[:])
+        quantise_dy(2, BANK, 2 * BANK, rear[1][:])
+        for b in range(3):
+            mx_pass(b, 2, 1, banks[b][:])
+        scatter_times_gain(3, 0, sum_30[:])
         third_sums = new_tile("third_sums", [P, 2, CHUNK], F32, RAW_20 - KIB)
-        for a in (1, 0):
-            quantise_dy(2, a * BANK, (a + 1) * BANK, rear[a][:])
-            for b in range(3):
-                mx_pass(b, 2, a, banks[b][:])
-            add_res(1 - a, 1, half(4, 1 - a), third_sums[:, 1 - a, :])
+        add_res(0, 1, half(4, 0), third_sums[:, 0, :])
+        quantise_dy(2, 0, BANK, rear[0][:])
+        for b in range(3):
+            mx_pass(b, 2, 0, banks[b][:])
+        add_res(1, 1, half(4, 1), third_sums[:, 1, :])
         for b in range(2):
             scatter_times_gain(b, 1, third_sums[:, b, :])
         rear_sum = new_tile("rear_sum", [P, BANK], F32)

from contextlib import ExitStack

import concourse.mybir as mybir
from concourse.masks import make_identity

K, N, T, J = 1024, 512, 2048, 1024
FLOPS = 2 * K * N * J

F32 = mybir.dt.float32
BF16 = mybir.dt.bfloat16
I32 = mybir.dt.int32
U32 = mybir.dt.uint32
U16 = mybir.dt.uint16
U8 = mybir.dt.uint8
E4M3 = mybir.dt.float8_e4m3fn_x4
E5M2 = mybir.dt.float8_e5m2_x4
E2M1 = mybir.dt.float4_e2m1fn_x4
ADD = mybir.AluOpType.add
MULT = mybir.AluOpType.mult
COPY = mybir.ActivationFunctionType.Copy

P = 128
BANK = 512
CHUNK = 256
QUAD = 32
VECTOR_COLUMNS = 160


PLANE_BANKS = [(7, 2, 6, 5), (0, 1, 3, 4)]
KIB = 1024
RAW_10 = 0
RAW_21 = 8 * KIB
RAW_20 = 16 * KIB
LATE_WINDOWS = 24 * KIB
HEAD_ROUNDED = 31 * KIB
SPANS = [(0, 256), (256, 512), (512, 1024)]


def tile_list_embg_mix_resP_kernel(
    tc, dy, w8_words, w8_scales, w4_words, w4_scales, res, wgo, offs, out_0, out_1, out_2
):
    nc = tc.nc
    with ExitStack() as ctx:
        keep = ctx.enter_context(tc.tile_pool(name="keep", bufs=1))
        shared = ctx.enter_context(tc.tile_pool(name="shared", bufs=1))
        psum = ctx.enter_context(tc.psum_pool(name="psum", bufs=1))
        banks = [psum.tile([P, BANK], F32, name=f"bank{i}") for i in range(8)]

        def new_tile(name, shape, dtype, offset=None):
            if offset is None:
                return keep.tile(shape, dtype, name=name, align_bytes=64)
            return shared.tile(shape, dtype, name=name, align_bytes=64, offset=offset)

        offsets = keep.tile([P, J // 16], U16, name="offsets")
        w8 = new_tile("w8", [P, N], U32)
        w4 = new_tile("w4", [P, 2 * N], U8)
        w_scales = new_tile("w_scales", [P, 2 * N], U8)
        ident = new_tile("ident", [P, P], F32)
        windows = [new_tile(f"window{b}", [P, T], F32) for b in range(2)]

        raw = {}
        resid = {}
        gain = {}

        def load_dy(c, a, offset=None, piece=None):
            lo, hi = SPANS[c]
            if piece is not None:
                lo, hi = lo + piece * CHUNK, lo + (piece + 1) * CHUNK
            raw[c, a, piece] = new_tile(f"raw{c}{a}{lo}", [P, 4, hi - lo], F32, offset)
            nc.sync.dma_start(
                out=raw[c, a, piece][:],
                in_=dy[512 * a : 512 * (a + 1), lo:hi].rearrange("(p i) j -> p i j", i=4),
            )

        def load_res(b0, c):
            lo, hi = SPANS[c]
            rows = new_tile(f"res{b0}{c}", [P, 2, hi - lo], F32)
            nc.sync.dma_start(out=rows[:], in_=res[P * b0 : P * (b0 + 2), lo:hi].rearrange("(d p) j -> p d j", p=P))
            for d in range(2):
                resid[b0 + d, c] = rows[:, d, :]

        def load_gain(c):
            lo, hi = SPANS[c]
            gain[c] = new_tile(f"gain{c}", [P, hi - lo], F32)
            nc.sync.dma_start(out=gain[c][:], in_=wgo[:, lo:hi])

        def load_scales(a, source):
            for q in range(4):
                nc.sync.dma_start(
                    out=w_scales[QUAD * q : QUAD * q + 4, a * N : (a + 1) * N].bitcast(I32),
                    in_=source[0][4 * q : 4 * q + 4, :].bitcast(I32),
                )

        nc.gpsimd.memset(w_scales[:].bitcast(U32), 0)
        gain_rows = new_tile("gain_rows", [P, P], F32)
        nc.gpsimd.memset(gain_rows[:], 0.0)
        warm_in = keep.tile([P, 8], F32, name="warm_in")
        warm_out = keep.tile([P, 8], BF16, name="warm_out")
        nc.vector.memset(warm_in[:], 0.0)
        nc.scalar.copy(out=warm_out[:], in_=warm_in[:])

        nc.sync.dma_start(offsets[:], offs)
        load_dy(0, 1)
        load_scales(1, w4_scales)
        load_dy(0, 0)
        nc.sync.dma_start(out=w4[:].bitcast(I32), in_=w4_words[0].bitcast(I32))
        nc.sync.dma_start(out=w8[:].bitcast(I32), in_=w8_words[0].rearrange("p n i -> p (n i)").bitcast(I32))
        load_scales(0, w8_scales)
        load_res(0, 0)
        load_gain(0)
        load_dy(1, 1)
        load_dy(1, 0, RAW_10)
        load_res(2, 0)
        for a in (1, 0):
            load_dy(2, a, None, 0)
            load_dy(2, a, RAW_20 if a == 0 else RAW_21, 1)
        load_res(0, 1)
        load_gain(1)
        load_res(2, 1)
        nc.sync.dma_start(out=gain_rows[0 : J // P, :], in_=wgo[0].rearrange("(h q) -> h q", q=P))
        load_res(0, 2)
        load_res(2, 2)
        load_gain(2)

        for window in windows:
            nc.vector.memset(window[:].bitcast(U32), 0)
        make_identity(nc, ident[:])

        dy_codes = [new_tile(f"dy_codes{c}", [P, 2 * (hi - lo)], U32) for c, (lo, hi) in enumerate(SPANS)]
        dy_scales = [new_tile(f"dy_scales{c}", [P, 2 * (hi - lo)], U8) for c, (lo, hi) in enumerate(SPANS)]

        def round_dy(copy, columns, rows):
            copy(
                out=columns.rearrange("p (g e) i -> p g i e", e=4),
                in_=rows.rearrange("p i (g e) -> p g i e", e=4),
            )

        def quantise_dy(c, lo, hi, grouped):
            nc.vector.quantize_mx(
                out=dy_codes[c][:, lo:hi].bitcast(E5M2),
                scales=dy_scales[c][:, lo:hi],
                in_=grouped.rearrange("p j i -> p (j i)"),
            )

        def round_chunk(c, offset=None):
            grouped = new_tile(f"grouped{c}", [P, 2 * CHUNK, 4], BF16, offset)
            for a in (1, 0):
                round_dy(nc.scalar.copy, grouped[:, a * CHUNK : (a + 1) * CHUNK, :], raw[c, a, None][:])
            return grouped

        def mx_pass(b, c, a, target, first=1):
            if a == 0:
                words = w8[:, P * b : P * (b + 1)].bitcast(E4M3)
            else:
                words = w4[:, 2 * P * b : 2 * P * (b + 1)].bitcast(E2M1)
            width = SPANS[c][1] - SPANS[c][0]
            cols = slice(a * width, (a + 1) * width)
            nc.tensor.matmul_mx(
                out=target,
                lhsT=words,
                lhsT_scale=w_scales[:, a * N + P * b : a * N + P * (b + 1)],
                rhs=dy_codes[c][:, cols].bitcast(E5M2),
                rhs_scale=dy_scales[c][:, cols],
                start=(a == first),
                stop=(a != first),
            )

        def half(bank, u):
            return banks[bank][:, u * CHUNK : (u + 1) * CHUNK]

        def products(units, bank, first_half=0):
            for u, (b, c) in enumerate(units, first_half):
                for a in (0, 1):
                    mx_pass(b, c, a, half(bank, u), first=0)

        def places(b, lo, hi):
            return windows[b][:].indirect(offsets[:, lo // 16 : hi // 16])

        def add_res(b, c, product, target):
            nc.vector.tensor_tensor(target, product, resid[b, c], ADD)

        def scatter_times_gain(b, c, values):
            nc.vector.tensor_tensor(places(b, *SPANS[c]), values, gain[c][:], MULT)

        def blocks_of(units):
            blocks, j0 = [], 0
            for b, c in units:
                lo, hi = SPANS[c]
                for j in range(lo, hi, P):
                    blocks.append((j // P, j0, resid[b, c][:, j - lo : j - lo + P]))
                    j0 = j0 + P
            return sorted(blocks, key=lambda block: block[:2])

        def turn_res(units, sum_bank):
            for s, (col, j0, rows) in enumerate(blocks_of(units)):
                nc.tensor.matmul(
                    banks[sum_bank][:, P * s : P * (s + 1)], rows, ident[:], start=(s == 0), stop=False, is_transpose=True
                )

        def turn_product(units, product_bank, sum_bank, product):
            nc.scalar.copy(out=product[:], in_=banks[product_bank][:])
            for s, (col, j0, rows) in enumerate(blocks_of(units)):
                nc.tensor.matmul(
                    banks[sum_bank][:, P * s : P * (s + 1)], product[:, j0 : j0 + P], ident[:],
                    start=False, stop=(s == 3), is_transpose=True,
                )

        def turn_back(units, product_bank, sum_bank, offset=None):
            blocks = blocks_of(units)
            turned = new_tile(f"turned{product_bank}", [P, BANK], F32, offset)
            for col in sorted(set(block[0] for block in blocks)):
                mine = [s for s, block in enumerate(blocks) if block[0] == col]
                cols = slice(P * mine[0], P * (mine[-1] + 1))
                nc.scalar.activation(turned[:, cols], banks[sum_bank][:, cols], COPY, scale=gain_cols[:, col : col + 1])
            for s, (col, j0, rows) in enumerate(blocks):
                nc.tensor.transpose(banks[product_bank][:, j0 : j0 + P], turned[:, P * s : P * (s + 1)], ident[:])

        def fetch(product_bank, targets):
            width = BANK // len(targets)
            for u, target in enumerate(targets):
                nc.scalar.copy(out=target, in_=banks[product_bank][:, u * width : (u + 1) * width])

        words_out = out_1[0].rearrange("p t i -> p (t i)").bitcast(I32)
        scales_out = out_2[0].bitcast(I32)
        pair_tiles = [new_tile(f"pairs{g}", [P, 2 * P], F32) for g in range(4)]
        y_codes = new_tile("y_codes", [P, 4 * BANK], U32)
        y_scales = new_tile("y_scales", [P, BANK], U8)

        def store_and_regroup(b, first_copies, second_copies):
            window = windows[b]
            first_banks, second_banks = PLANE_BANKS[b % 2], PLANE_BANKS[1 - b % 2]
            nc.sync.dma_start(out=out_0[P * b : P * (b + 1), :], in_=window[:])
            rounded = new_tile(f"rounded{b}", [P, 4, P, 2], F32)
            for g in range(4):
                turned = banks[first_banks[g]][:].rearrange("s (q r) -> s q r", q=4)
                for tq in range(4):
                    t0 = BANK * tq + P * g
                    nc.tensor.transpose(turned[:, tq, :], window[:, t0 : t0 + P], ident[:])
                first_copies[g](
                    out=pair_tiles[g][:].bitcast(BF16).rearrange("s (u m e) -> s u m e", u=2, e=2),
                    in_=turned.rearrange("s q (p u e) -> s u (q p) e", u=2, e=2),
                )
            for g in range(4):
                for u in range(2):
                    cols = slice(P * u, P * (u + 1))
                    nc.tensor.transpose(banks[second_banks[g]][:, cols], pair_tiles[g][:, cols], ident[:])
            for g in range(4):
                words = banks[second_banks[g]][:, 0 : 2 * P].rearrange("m (g u s) -> m g s u", g=1, u=2)
                second_copies[g](out=rounded[:, g : g + 1, :, :], in_=words)
            return rounded

        def quantise_out(b, rounded, lo, hi):
            flat = rounded[:].rearrange("m g s u -> m (g s u)").bitcast(BF16)
            nc.vector.quantize_mx(
                out=y_codes[:, BANK * b + lo : BANK * b + hi].bitcast(E4M3),
                scales=y_scales[4 * b : P, lo:hi],
                in_=flat[:, 4 * lo : 4 * hi],
            )

        def queue_of(tq):
            return nc.sync if tq < 2 else nc.scalar

        def store_codes(b0, b1):
            rows = words_out[QUAD * b0 : QUAD * b1, :].rearrange("(d p) t -> p d t", p=QUAD)
            for tq in (0, 2, 1, 3):
                quarter = y_codes[QUAD * tq : QUAD * (tq + 1), BANK * b0 : BANK * b1].bitcast(I32)
                queue_of(tq).dma_start(
                    out=rows[:, :, BANK * tq : BANK * (tq + 1)],
                    in_=quarter.rearrange("p (d s) -> p d s", s=BANK),
                )

        on_scalar, on_vector = nc.scalar.copy, nc.vector.tensor_copy

        head1 = new_tile("head1", [P, CHUNK, 4], BF16)
        round_dy(on_scalar, head1[:], raw[0, 1, None][:])
        quantise_dy(0, CHUNK, 2 * CHUNK, head1[:])
        for b in range(2):
            mx_pass(b, 0, 1, half(b, 0))
        head0 = new_tile("head0", [P, CHUNK, 4], BF16, HEAD_ROUNDED)
        round_dy(on_vector, head0[:, 0:VECTOR_COLUMNS, :], raw[0, 0, None][:, :, 0:VECTOR_COLUMNS])
        round_dy(on_scalar, head0[:, VECTOR_COLUMNS:CHUNK, :], raw[0, 0, None][:, :, VECTOR_COLUMNS:CHUNK])
        quantise_dy(0, 0, CHUNK, head0[:])
        for b in (2, 3):
            windows.append(new_tile(f"window{b}", [P, T], F32, LATE_WINDOWS + 4 * T * (b - 2)))
            nc.gpsimd.memset(windows[b][:].bitcast(U32), 0)
        for b in range(2):
            mx_pass(b, 0, 0, half(b, 0))
        products([(2, 0), (3, 0)], 2)
        first_sums = new_tile("first_sums", [P, 2, CHUNK], F32)
        for b in range(2):
            add_res(b, 0, half(b, 0), first_sums[:, b, :])
        for b in range(2):
            scatter_times_gain(b, 0, first_sums[:, b, :])

        grouped = round_chunk(1)
        sum_20 = new_tile("sum_20", [P, CHUNK], F32, RAW_10)
        add_res(2, 0, half(2, 0), sum_20[:])
        quantise_dy(1, 0, 2 * CHUNK, grouped[:])
        products([(0, 1), (1, 1)], 4)
        sum_c = [(2, 1), (3, 1)]
        products(sum_c, 3)
        scatter_times_gain(2, 0, sum_20[:])

        rear = {}
        for a in (1, 0):
            rear[a] = new_tile(f"rear{a}", [P, BANK, 4], BF16)
            for piece in range(2):
                round_dy(on_scalar, rear[a][:, piece * CHUNK : (piece + 1) * CHUNK, :], raw[2, a, piece][:])
        sum_30 = new_tile("sum_30", [P, CHUNK], F32, RAW_21)
        add_res(3, 0, half(2, 1), sum_30[:])
        quantise_dy(2, BANK, 2 * BANK, rear[1][:])
        for b in range(3):
            mx_pass(b, 2, 1, banks[b][:])
        scatter_times_gain(3, 0, sum_30[:])
        third_sums = new_tile("third_sums", [P, 2, CHUNK], F32, RAW_20 - KIB)
        add_res(0, 1, half(4, 0), third_sums[:, 0, :])
        quantise_dy(2, 0, BANK, rear[0][:])
        for b in range(3):
            mx_pass(b, 2, 0, banks[b][:])
        add_res(1, 1, half(4, 1), third_sums[:, 1, :])
        for b in range(2):
            scatter_times_gain(b, 1, third_sums[:, b, :])
        rear_sum = new_tile("rear_sum", [P, BANK], F32)
        for lo in (0, CHUNK):
            cols = slice(lo, lo + CHUNK)
            nc.vector.tensor_tensor(rear_sum[:, cols], banks[0][:, cols], resid[0, 2][:, cols], ADD)
        for lo in (0, CHUNK):
            cols = slice(lo, lo + CHUNK)
            nc.vector.tensor_tensor(places(0, BANK + lo, BANK + lo + CHUNK), rear_sum[:, cols], gain[2][:, cols], MULT)

        gain_cols = new_tile("gain_cols", [P, J // P], F32)
        nc.tensor.transpose(banks[7][:, 0:P], gain_rows[:], ident[:])
        nc.scalar.copy(out=gain_cols[:], in_=banks[7][:, 0 : J // P])
        late = {b: new_tile(f"late{b}", [P, 3 * CHUNK], F32) for b in (2, 3)}
        late[1] = new_tile("late1", [P, BANK], F32)
        product = new_tile("product", [P, BANK], F32)
        turn_res([(1, 2)], 4)
        turn_product([(1, 2)], 1, 4, product)
        turn_back([(1, 2)], 1, 4)
        fetch(1, [late[1][:]])
        turn_res(sum_c, 5)
        turn_product(sum_c, 3, 5, new_tile("product_c", [P, BANK], F32, RAW_20 + 2 * KIB))
        turn_back(sum_c, 3, 5)
        fetch(3, [late[b][:, 0:CHUNK] for b in (2, 3)])
        for b, product_bank, sum_bank in ((2, 2, 7), (3, 5, 6)):
            if b == 3:
                for a in (1, 0):
                    mx_pass(b, 2, a, banks[product_bank][:])
            turn_res([(b, 2)], sum_bank)
            turn_product([(b, 2)], product_bank, sum_bank, product)
            turn_back([(b, 2)], product_bank, sum_bank)
            fetch(product_bank, [late[b][:, CHUNK : 3 * CHUNK]])

        regrouped = []
        nc.vector.tensor_copy(places(1, BANK, J), late[1][:])
        nc.vector.tensor_copy(places(2, CHUNK, J), late[2][:])
        for b in range(3):
            regrouped.append(store_and_regroup(b, [on_scalar] * 4, [on_scalar] * 4))
        nc.vector.tensor_copy(places(3, CHUNK, J), late[3][:])
        for b in range(3):
            quantise_out(b, regrouped[b], 0, BANK)
        store_codes(0, 3)
        last = store_and_regroup(3, [on_scalar] * 3 + [on_vector], [on_vector, on_scalar] * 2)
        for lo in (0, CHUNK):
            quantise_out(3, last, lo, lo + CHUNK)
        store_codes(3, 4)
        for tq in range(4):
            queue_of(tq).dma_start(
                out=scales_out[:, P * tq : P * (tq + 1)],
                in_=y_scales[QUAD * tq : QUAD * tq + 16, :].bitcast(I32),
            )
